import numpy as np, ml_dtypes
CORES = [113,118,241,246]
N = 4
BF = ml_dtypes.bfloat16
P, L, B, T = 2048, 192, 1, 5
def skew(rng, n, hot):
    u = rng.random((N, 8, n))
    return np.take_along_axis(hot, np.minimum((P * u * u).astype(np.int64), P - 1), 2)
def parts(rng):
    x = rng.integers(0, 256, (N, 8, 16, P)); h = rng.integers(0, 256, (N, 8, 16, L))
    hot = np.argsort(rng.random((N, 8, P)), axis=2)
    pl = skew(rng, 16 * P, np.roll(hot, -1, axis=0)).reshape(N, 8, 16, P); kt = skew(rng, 16 * L, hot).reshape(N, 8, 16, L)
    nx = np.argsort(rng.random((N, 8, P)), axis=2); nx[:, 1::2] = skew(rng, P, hot)[:, 1::2]
    bm = rng.integers(0, P, (N, 8, L))
    th = np.stack([rng.integers(750, 1001, (N, 8)), rng.integers(900, 1251, (N, 8))], axis=2)
    return x, pl, nx, kt, h, bm, th
def pack(x, pl, nx, kt, h, bm, th):
    return {"xp": np.ascontiguousarray(x.reshape(N, 128, P)).astype(np.float32).astype(BF), "pl": np.ascontiguousarray(pl.reshape(N, 128, P)).astype(np.int32), "nx": np.ascontiguousarray(nx).astype(np.int32),
            "kt": np.ascontiguousarray(kt.reshape(N, 128, L)).astype(np.int32), "hm": np.ascontiguousarray(h.reshape(N, 128, L)).astype(np.float32).astype(BF), "bm": np.ascontiguousarray(bm).astype(np.int32), "th": np.ascontiguousarray(th).astype(np.int32)}
def setup_inputs(rng):
    return pack(*parts(rng))
def setup_inputs_spread(rng):
    x, pl, nx, kt, h, bm, th = parts(rng)
    x = np.minimum((rng.random(x.shape) * np.exp2(8.1 * rng.random((N, 8, 1, P)))).astype(np.int64), 255)
    h = np.minimum((rng.random(h.shape) * np.exp2(8.1 * rng.random((N, 8, 1, L)))).astype(np.int64), 255)
    th = np.minimum(np.exp2(12.0 * rng.random((N, 8, 2))).astype(np.int64), 4095); th[:, 2, 0] = rng.integers(300, 1200, N)
    hot = np.argsort(rng.random((N, 8, P)), axis=2); u = rng.random((N, 8, 16 * P)) ** 4
    pl = np.take_along_axis(np.roll(hot, -1, axis=0), np.minimum((P * u).astype(np.int64), P - 1), 2).reshape(N, 8, 16, P)
    nx[:, ::3] = skew(rng, P, hot)[:, ::3]
    return pack(x, pl, nx, kt, h, bm, th)
def edge(rng, n):
    return np.where(rng.random((N, 8, n)) < 0.7, (P - 1) * rng.integers(0, 2, (N, 8, n)), rng.integers(0, P, (N, 8, n)))
def setup_inputs_ends(rng):
    k = rng.integers(0, 5, (N, 8, 1, P)); x = np.where(k == 0, 0, np.where(k == 1, 255, 255 * rng.integers(0, 2, (N, 8, 16, P))))
    k = rng.integers(0, 8, (N, 8, 1, L)); h = np.where(k == 0, 0, np.where(k == 1, 255, np.where(k == 2, 127, 255 * rng.integers(0, 2, (N, 8, 16, L)))))
    x[..., 0] = 0; x[..., P - 1] = 255
    pl = edge(rng, 16 * P).reshape(N, 8, 16, P); kt = edge(rng, 16 * L).reshape(N, 8, 16, L); nx = edge(rng, P); bm = edge(rng, L)
    th = 4095 * np.ones((N, 8, 2), np.int64); th[:, :, 1] = 4095 * rng.integers(0, 2, (N, 8))
    for q in range(N):
        o = rng.permutation(7); th[q, o[:2], 0] = 0; th[q, o[2], 1] = 0; th[q, 7, 1] = 4095
        for g in range(8):
            if (q + g) % 4 == 0: nx[q, g, 0] = P - 1; nx[q, g, P - 1] = 0
            else: nx[q, g, 0] = rng.integers(7, P - 1); nx[q, g, P - 1] = rng.integers(7, P - 1)
        for g in (int(o[3]), 7):
            a = x[q, g]; a[:, [P - 1, 1, 2, 3]] = 255; a[:, [0, 4, 5, 6]] = 0
            kt[q, g, :, L - 1] = np.tile(np.array([P - 1, 1, 2, 3]), 4); h[q, g, :, L - 1] = 0
            kt[q, g, :, L - 2] = np.tile(np.array([5, 0, 4, 6]), 4); h[q, g, :, L - 2] = 255
    return pack(x, pl, nx, kt, h, bm, th)
def setup_inputs_corners(rng):
    x, pl, nx, kt, h, bm, th = parts(rng); pp = np.arange(P); kk = np.arange(16)[:, None]; li = np.arange(L)[None, :]
    for q in range(N):
        for g in range(8):
            b = (q - 1) % N; w = (g + q) % 8
            if w == 0: nx[q, g] = pp; th[q, g] = (4095, 4095)
            elif w == 1: nx[q, g] = pp ^ 1; th[q, g] = (1200, 0)
            elif w == 2:
                nx[q, g] = (pp + 1) % P; kt[q, g] = (P - 40 + li + kk) % P; pl[b, g] = (pp[None, :] + kk) % P; th[q, g] = (4095, 4095)
            elif w == 3:
                nx[q, g] = P - 1; bm[q, g] = np.where(li[0] % 3 == 0, 0, np.where(li[0] % 3 == 1, P - 1, li[0])); th[q, g] = (2000, 4095)
            elif w == 4:
                z = (0, P - 1, P // 2)[q % 3]; kt[q, g] = z; pl[b, g] = z; th[q, g] = (4095, 1100)
            elif w == 5:
                x[q, g] = x[q, g][:, pp - (pp & 7)]; th[q, g] = (2000, 1000)
                kt[q, g] = 8 * rng.integers(0, P // 8, (1, L)) + rng.integers(0, 8, (16, L)); pl[b, g] = 8 * rng.integers(0, P // 8, (1, P)) + rng.integers(0, 8, (16, P))
            elif w == 6:
                th[q, g] = (0, 4095); bm[q, g, 0] = 0; bm[q, g, L - 1] = P - 1; nx[q, g, 0] = 0
            else:
                kt[q, g] = (li + kk) & 15; pl[b, g] = rng.integers(0, 16, (16, P)); nx[q, g, :16] = (np.arange(16) + 1) & 15; th[q, g] = (4095, 4095)
    x[:, 7] = 255; h[:, 7] = 255; nx[:, 7] = pp; th[:, 7] = 4095
    kt[:, 7] = np.where(li < 31, 16 + li, (li + kk) & 15); pl[:, 7] = kk; pl[:, 7, :, 16:47] = 64 + np.arange(31)
    for q in range(N):
        b = (q - 1) % N; assert np.sum(np.any(~np.isin(pl[b, 7][:, kt[b, 7, 0]], kt[q, 7, 0]), axis=0)) == 31
    return pack(x, pl, nx, kt, h, bm, th)
def setup_inputs_ties(rng):
    x, pl, nx, kt, h, bm, th = parts(rng); t = rng.integers(40, 101, (N, 8, 1))
    far = t + np.where(rng.random((N, 8, P)) < 0.5, rng.integers(-1, 2, (N, 8, P)), rng.integers(0, 34, (N, 8, P)))
    x = 100 + np.where(np.arange(16)[:, None] == rng.integers(0, 16, (N, 8, 1, P)), far[:, :, None, :], 0)
    h = 100 + np.zeros((N, 8, 16, L), np.int64); h[:, :, 0] += (rng.random((N, 8, L)) < 0.125).astype(np.int64)
    order = np.argsort(far + rng.random(far.shape), axis=2); q = np.array([0.0, 0.2, 0.35, 0.55, 0.7, 0.9])
    def near(n, o):
        a = (P * rng.choice(q, (N, 8, 1, n))).astype(np.int64); i = np.minimum(a + ((P - a) * rng.random((N, 8, 16, n))).astype(np.int64), P - 1)
        return np.take_along_axis(o, i.reshape(N, 8, 16 * n), 2).reshape(N, 8, 16, n)
    kt = near(L, order); pl = near(P, np.roll(order, -1, axis=0))
    th = np.concatenate([t, ((t - 1) >> 1) + t + rng.integers(-1, 2, (N, 8, 1))], axis=2)
    return pack(x, pl, nx, kt, h, bm, th)
def sums(d):
    return (d[None, :] + ((np.arange(16)[:, None] + np.arange(d.shape[0])[None, :]) & 15)) >> 4
def setup_inputs_counts(rng):
    x, pl, nx, kt, h, bm, th = parts(rng); li = np.arange(L); kk = np.arange(16)[:, None]; gs = [int(g) for g in rng.permutation(8)]
    o = np.argsort(rng.random((N, 8, P)), axis=2)[:, :, :5 * L].reshape(N, 8, 5, L)
    h[:, gs[:6]] = 0
    for w in range(5):
        g = gs[w]; r = rng.permutation(L)
        for q in range(N):
            a, b, c, e, f = o[q, g]; a2, b2, c2, e2, f2 = o[(q + 1) % N, g]; pq = pl[q, g]; nq = nx[q, g]; kq = kt[q, g]
            if w < 2: t = 16 * int(rng.integers(128, 250)) + int(rng.choice(np.array([3, 4, 5, 11, 12, 13])))
            else: t = int(rng.integers(64, 4001))
            d = t + 40 + rng.integers(0, 41, P)
            if w == 0:
                d = t - 17 + rng.integers(0, 35, P); d[a] = t - 17 + li % 35; kq[:] = a; th[q, g, 0] = t
            elif w == 1:
                d = rng.integers(0, 4081, P); d[a] = 0; d[b] = t - 17 + li % 35; nq[a] = b; kq[:] = a; th[q, g] = (int(rng.integers(64, 4001)), t)
            elif w == 2:
                d[a] = 0; d[b] = t - 2 + li % 36; nq[a] = f; pq[:, a] = b2; kq[:] = a; th[q, g] = (t, 0)
            elif w == 3:
                m = r[:40]; v = r[40:53]
                d[a] = 0; d[b] = 0; d[c[m]] = t - 2 + np.arange(40) % 36
                nq[a] = f; nq[b] = f; nq[a[v]] = a[v]
                pq[:, a] = f2; pq[:, a[m]] = b2[m]; pq[:, a[v]] = a2[v][(np.arange(13) + kk) % 13]; pq[:, b[m]] = c2[m]
                kq[:] = a; th[q, g] = (t, 0)
            else:
                m = r[:52]; z = r[52:]
                d[a[m]] = 0; d[e[z]] = t - 2 + np.arange(L - 52) % 36
                nq[a[m[:-1]]] = a[m[1:]]; nq[a[m[-1]]] = f[0]; nq[b] = c; bm[q, g] = b
                pq[:, a] = f2; pq[:, b] = f2; pq[:, f] = f2; pq[:, c] = e2
                kq[:] = f; kq[:, m] = a[m]; th[q, g] = (t, 0)
            x[q, g] = sums(d)
    g = gs[5]; x[:, g] = 0; nx[:, g] = np.arange(P); th[:, g] = 4095
    kt[:, g] = np.where(li[None, :] < 31, 16 + li[None, :], (li[None, :] + kk) & 15); pl[:, g] = kk; pl[:, g, :, 16:47] = 64 + np.arange(31)
    return pack(x, pl, nx, kt, h, bm, th)
def check_inputs(d):
    bad = []
    for k, hi in (("xp", 255), ("pl", P - 1), ("nx", P - 1), ("kt", P - 1), ("hm", 255), ("bm", P - 1), ("th", 4095)):
        v = np.asarray(d[k]).astype(np.float64)
        if not (np.min(v) >= 0 and np.max(v) <= hi): bad.append("range of " + k)
        if k in ("xp", "hm") and np.any(v != np.floor(v)): bad.append("whole numbers of " + k)
    return bad
def pick(a, ix):
    return np.take_along_axis(a, ix[:, :, None, :], 3)
def mark(flags, y, go):
    a, g, i = np.nonzero(go); flags[a, g, y[a, g, i]] = True
def reference(xp, pl, nx, kt, hm, bm, th):
    x = xp.astype(np.float32).astype(np.int64).reshape(N, 8, 16, P); par = pl.astype(np.int64).reshape(N, 8, 16, P); nxt = nx.astype(np.int64)
    k = kt.astype(np.int64).reshape(N, 8, 16, L); h = hm.astype(np.float32).astype(np.int64).reshape(N, 8, 16, L)
    b = bm.astype(np.int64); t1 = th.astype(np.int64)[:, :, 0:1]; t2 = th.astype(np.int64)[:, :, 1:2]
    j = np.tile(np.arange(P, dtype=np.int64), (N, 8, 1)); eaten = np.zeros((N, 8, P), bool); a = np.zeros((N, 8, 1), np.int64)
    for t in range(T):
        c = np.take_along_axis(j, k.reshape(N, 8, 16 * L), 2).reshape(N, 8, 16, L)
        void = np.take_along_axis(eaten, c.reshape(N, 8, 16 * L), 2).reshape(N, 8, 16, L)
        d = np.stack([np.add.reduce(np.abs(pick(x, c[:, :, i]) - h), axis=2) for i in range(16)], axis=2)
        d = np.where(void, 2 ** 20, d)
        w = np.argmin(d, axis=2)[:, :, None, :]
        hit = np.take_along_axis(d, w, 2)[:, :, 0] < t1 + (a & 31)
        y = np.where(hit, np.take_along_axis(c, w, 2)[:, :, 0], np.take_along_axis(j, b, 2))
        new = np.zeros((N, 8, P), bool); go = hit
        h = np.where(go[:, :, None, :], (h + pick(x, y)) >> 1, h); mark(new, y, go)
        for s in range(B):
            n = np.take_along_axis(j, np.take_along_axis(nxt, y, 2), 2); xn = pick(x, n)
            go = go & ~np.take_along_axis(eaten, n, 2) & (np.add.reduce(np.abs(xn - h), axis=2) <= t2)
            y = np.where(go, n, y); h = np.where(go[:, :, None, :], (h + xn) >> 1, h); mark(new, y, go)
        b = np.take_along_axis(nxt, y, 2); a = np.add.reduce(hit.astype(np.int64), axis=2, keepdims=True)
        j = np.where(new, nxt, j); eaten = eaten | new
        j = np.take_along_axis(j, j, 2)
        if t < T - 1:
            k = np.roll(pick(par, y), 1, axis=0); h = np.roll(h, 1, axis=0)
    return {"yj": j.astype(np.float32), "yh": h.reshape(N, 128, L).astype(np.float32).astype(BF), "yb": b.astype(np.float32)}

@@ -1,0 +1,618 @@
+from concourse.mybir import AluOpType as Op, ActivationFunctionType as Act
+
+BIG = 1.0e9
+VOID = 640.0
+L, P, NV = 192, 2048, 5
+HS = P
+VO = P + L
+TW = VO + 16
+NX = 128
+CB = L - NX
+CHUNKS = (0, 64, 128)
+QW = 130
+PRE = 5
+NQ = 5
+LAST1 = 60
+SPLIT = (50, 60, 60)
+GK = 9
+
+B16, F32, I32, U16 = "bfloat16", "float32", "int32", "uint16"
+SCRATCH = {
+    "TX": ("sbuf", [128, TW], B16), "XV": ("sbuf", [128, P], B16), "TF": ("sbuf", [128, TW], B16),
+    "BB": ("sbuf", [128, P], B16), "B1": ("sbuf", [128, P], B16), "PL": ("sbuf", [128, P], I32),
+    "HX": ("sbuf", [128, NX * 16], B16), "DX": ("sbuf", [128, NX * 16], B16), "AX": ("sbuf", [128, NX * 16], B16),
+    "GB": ("sbuf", [128, CB * 16], B16), "AB": ("sbuf", [128, CB * 16], B16),
+    "KI": ("sbuf", [128, L], I32), "KA": ("sbuf", [128, 2 * L], I32), "KAB": ("sbuf", [128, 2 * L], F32),
+    "VT": ("sbuf", [128, 2 * L], F32), "MS": ("sbuf", [128, 2 * L], F32), "RST": ("sbuf", [128, 2 * L], F32), "RS0": ("sbuf", [128, 2 * L], F32),
+    "MI": ("sbuf", [128, 24], I32), "ML": ("sbuf", [128, 24], I32), "LB": ("sbuf", [128, 24], B16), "MV": ("sbuf", [128, 12], B16),
+    "L1": ("sbuf", [128, 12], U16), "MISS": ("sbuf", [128, 12], F32), "CV": ("sbuf", [128, 24], F32), "SEL": ("sbuf", [128, 24], F32),
+    "IV": ("sbuf", [128, 12], I32), "IX": ("sbuf", [128, 24], I32),
+    "SI": ("sbuf", [128, L], I32), "Q1": ("sbuf", [128, L], I32), "FF": ("sbuf", [128, 3 * L], B16),
+    "M1": ("sbuf", [128, 12], U16), "E2": ("sbuf", [128, L], B16), "AE": ("sbuf", [128, L], B16), "F2": ("sbuf", [128, L], I32),
+    "BR": ("sbuf", [128, L], B16), "QR": ("sbuf", [128, 48], F32), "BRL": ("sbuf", [128, 12], F32),
+    "BN": ("sbuf", [128, 12], F32), "YM": ("sbuf", [128, 24], F32),
+    "YF": ("sbuf", [128, 12], F32), "YU": ("sbuf", [128, 12], U16), "BF": ("sbuf", [128, 12], F32), "BU": ("sbuf", [128, 12], U16),
+    "JB": ("sbuf", [128, 24], F32), "FB": ("sbuf", [128, L], B16),
+    "OR": ("sbuf", [128, 24 * 128], B16), "OQ": ("sbuf", [128, 24 * QW], B16), "CS": ("sbuf", [128, 128], F32),
+    "MK": ("sbuf", [128, 128], B16), "JL": ("sbuf", [128, 128], F32), "NL": ("sbuf", [128, 128], F32),
+    "ZF": ("sbuf", [128, 128], F32), "ZU": ("sbuf", [128, 128], U16), "JU": ("sbuf", [128, 128], U16),
+    "AI": ("sbuf", [128, 2], I32), "AJ": ("sbuf", [128, 2], I32), "AK": ("sbuf", [128, 2], F32), "THR": ("sbuf", [128, 2], F32),
+    "T1K": ("sbuf", [128, 2], F32), "T2": ("sbuf", [128, 2], F32),
+    "ROW": ("sbuf", [128, P], F32), "RB": ("sbuf", [128, 4 * L], F32),
+    "BD": ("sbuf", [128, 128], B16), "ONE": ("sbuf", [128, 128], B16), "ZER": ("sbuf", [128, 128], B16), "ON2": ("sbuf", [128, L], B16),
+    "ID": ("sbuf", [128, 128], B16), "NI": ("sbuf", [128, 128], B16), "SP": ("sbuf", [128, 128], B16), "SM": ("sbuf", [128, 128], B16),
+    "N32": ("sbuf", [128, 128], B16), "KBM": ("sbuf", [128, 128], B16), "BO": ("sbuf", [128, 128], B16),
+    "WYR": ("sbuf", [128, 128], B16), "WNR": ("sbuf", [128, 128], B16), "IQ": ("sbuf", [128, 129], B16),
+    "SU": ("sbuf", [128, 2048], B16), "SY": ("sbuf", [128, 2048], B16), "SN": ("sbuf", [128, 2048], B16), "SQ": ("sbuf", [128, 2048], B16),
+    "SR": ("sbuf", [128, 2048], B16), "MT": ("sbuf", [128, 2048], B16), "PP": ("sbuf", [128, 8 * 128], B16),
+    "CO": ("sbuf", [128, 16], F32), "CT": ("sbuf", [128, 16], F32), "RC": ("sbuf", [128, 16], F32), "R16": ("sbuf", [128, 16], F32),
+    "IP": ("sbuf", [128, 2], I32), "IW": ("sbuf", [128, 2], I32), "IL": ("sbuf", [128, 128], I32), "I12": ("sbuf", [128, 12], I32), "IC": ("sbuf", [128, 128], I32),
+    "CF": ("sbuf", [128, 4 * 128], B16), "CW": ("sbuf", [128, 4 * 128], I32), "NXC": ("sbuf", [128, 128], I32), "ICm": ("sbuf", [128, 128], I32),
+    "BMC": ("sbuf", [128, 12], I32), "BMw": ("sbuf", [128, 24], I32), "BMf": ("sbuf", [128, 24], B16), "BMR": ("sbuf", [128, L], B16),
+    "TH": ("sbuf", [128, 2], I32), "THw": ("sbuf", [128, 4], I32), "THf": ("sbuf", [128, 4], B16),
+    "TSR": ("sbuf", [128, 128], B16), "TSx": ("sbuf", [128, 128], B16), "TS0": ("sbuf", [128, 128], B16), "TS1": ("sbuf", [128, 128], B16),
+    "TMP": ("sbuf", [128, 512], B16),
+    "HH": ("sbuf", [128, 2 * NV * L], B16), "KK": ("sbuf", [128, 2 * NV * L], U16),
+}
+ALIAS = {}
+for _t in range(NV):
+    ALIAS["H%d" % _t] = ("HH", L * _t, L)
+    ALIAS["HS%d" % _t] = ("HH", L * (NV + _t), L)
+    ALIAS["K%d" % _t] = ("KK", L * _t, L)
+    ALIAS["KS%d" % _t] = ("KK", L * (NV + _t), L)
+for _k, _n in enumerate(("BD0", "BD1", "N3a", "N3b")):
+    ALIAS[_n] = ("TMP", 128 * _k, 128)
+for _k, _n in enumerate(("FY", "FN", "GF")):
+    ALIAS[_n] = ("FF", L * _k, L)
+for _t in range(8):
+    SCRATCH["p%d" % _t] = ("psum", [128, 512], F32)
+NDMA = 32
+SEMAPHORES = ["sV", "sA", "sT", "sG", "loc"] + ["d%d" % k for k in range(NDMA)] + ["ha%d" % t for t in range(1, NV)] + ["ka%d" % t for t in range(1, NV)]
+
+
+def make_emitter(g, T):
+    queues = {"V": g.vector, "A": g.scalar, "T": g.tensor, "G": g, "S": g.sync, "C": g.scalar}
+    hist, know, snap, count, nd = {}, {}, {}, {}, [0]
+
+    def ap(r):
+        name, c0, c1, st, p = r
+        return T[name][p, c0:c1:st] if st != 1 else T[name][p, c0:c1]
+
+    def clash(a, b):
+        if a[1] >= b[2] or b[1] >= a[2]:
+            return False
+        if a[3] == b[3] and a[3] > 1 and (a[1] - b[1]) % a[3]:
+            return False
+        if a[4] != b[4] and a[4].step is not None and a[4].step == b[4].step and a[4].start != b[4].start:
+            return False
+        return True
+
+    def await_(q, sem, val):
+        k = know.setdefault(q, {})
+        if k.get(sem, 0) >= val:
+            return
+        queues[q].wait_ge(T.sem[sem], val)
+        for s, v in snap.get((sem, val), {}).items():
+            if v > k.get(s, 0):
+                k[s] = v
+        k[sem] = val
+
+    def deps(q, reads, writes):
+        need = {}
+        for w, rs in ((False, reads), (True, writes)):
+            for r in rs:
+                psum = SCRATCH.get(r[0], ("",))[0] == "psum"
+                for (h, hw, hq, sem, val) in hist.get(r[0], []):
+                    if psum and hq != q:
+                        hit = True
+                    else:
+                        hit = (w or hw) and clash(r, h)
+                        if hit and psum and q == "T":
+                            hit = False
+                    if hit and val > need.get(sem, 0):
+                        need[sem] = val
+        for sem in sorted(need):
+            await_(q, sem, need[sem])
+
+    def note(q, reads, writes, sem, val):
+        for w, rs in ((False, reads), (True, writes)):
+            for r in rs:
+                h = hist.setdefault(r[0], [])
+                if w and r[0][0] != "p":
+                    h[:] = [e for e in h if not (r[1] <= e[0][1] and r[2] >= e[0][2] and r[3] == 1 and r[4] == slice(None) and (e[2] != q or e[1]))]
+                h[:] = [e for e in h if not (e[2] == q and e[1] == w and e[0] == r)]
+                h.append((r, w, q, sem, val))
+
+    def op(q, fn, reads, writes):
+        deps(q, reads, writes)
+        sem = "s" + q
+        count[q] = count.get(q, 0) + 1
+        fn(queues[q]).then_inc(T.sem[sem], 1)
+        k = dict(know.setdefault(q, {}))
+        k[sem] = count[q]
+        snap[(sem, count[q])] = k
+        note(q, reads, writes, sem, count[q])
+
+    def dma(q, out, in_, reads, writes):
+        kq = "A" if q == "C" else q
+        deps(kq, reads, writes)
+        sem = "d%d" % nd[0]
+        nd[0] += 1
+        queues[q].dma_start(out, in_).then_inc(T.sem[sem], 16)
+        snap[(sem, 16)] = dict(know.setdefault(kq, {}))
+        note("D" + sem, reads, writes, sem, 16)
+
+    def arrive(name, sem, val):
+        note("R" + sem, [], [R(name)], sem, val)
+
+    def finish():
+        for q in ("V", "A", "T", "G"):
+            if count.get(q):
+                await_("G", "s" + q, count[q])
+        for k in range(nd[0]):
+            await_("G", "d%d" % k, 16)
+
+    return ap, op, dma, arrive, deps, finish
+
+
+def R(name, c0=0, c1=None, st=1, p=slice(None)):
+    if name in ALIAS:
+        base, off, w = ALIAS[name]
+        return (base, off + c0, off + (w if c1 is None else c1), st, p)
+    return (name, c0, SCRATCH[name][1][1] if c1 is None else c1, st, p)
+
+
+def col(name, j):
+    return R(name, j, j + 1)
+
+
+def rank_program(g, core, T, topo):
+    rank = T.rank_of(core)
+    if rank is None:
+        return
+    n = len(T.cores)
+    nxt, prv = T.cores[(rank + 1) % n], T.cores[(rank - 1) % n]
+    rid, pid = topo.addr(nxt, core)
+    mask = topo.mask(core, nxt)
+    ap, op, dma, arrive, deps, finish = make_emitter(g, T)
+
+    def tt(out, a, b, o):
+        op("V", lambda e: e.tensor_tensor(ap(out), ap(a), ap(b), o), [a, b], [out])
+
+    def ts(out, a, s1, o0, s2=None, o1=None):
+        rd = [a] + [s for s in (s1, s2) if isinstance(s, tuple)]
+        v1 = ap(s1) if isinstance(s1, tuple) else s1
+        v2 = ap(s2) if isinstance(s2, tuple) else s2
+        if o1 is None:
+            op("V", lambda e: e.tensor_scalar(ap(out), ap(a), v1, None, o0), rd, [out])
+        else:
+            op("V", lambda e: e.tensor_scalar(ap(out), ap(a), v1, v2, o0, o1), rd, [out])
+
+    def cp(out, a):
+        op("V", lambda e: e.tensor_copy(ap(out), ap(a)), [a], [out])
+
+    def fill(out, c):
+        op("V", lambda e: e.memset(ap(out), c), [], [out])
+
+    def act(out, a, f=Act.Copy):
+        op("A", lambda e: e.activation(ap(out), ap(a), f), [a], [out])
+
+    def act_bias(out, a, f, b):
+        op("A", lambda e: e.activation(ap(out), ap(a), f, bias=ap(b)), [a, b], [out])
+
+    def act_lin(out, a, sc, bs):
+        op("A", lambda e: e.activation(ap(out), ap(a), Act.Copy, bias=bs, scale=sc), [a], [out])
+
+    def act_scale(out, a, c):
+        op("A", lambda e: e.activation(ap(out), ap(a), Act.Copy, scale=ap(c)), [a, c], [out])
+
+    def vgather(out, win, off):
+        op("V", lambda e: e.tensor_copy(ap(out), ap(win).indirect(ap(off))), [win, off], [out])
+
+    def agather(out, win, off):
+        op("A", lambda e: e.activation(ap(out), ap(win).indirect(ap(off)), Act.Copy), [win, off], [out])
+
+    def ttgather(out, win, off, b, o):
+        op("V", lambda e: e.tensor_tensor(ap(out), ap(win).indirect(ap(off)), ap(b), o), [win, off, b], [out])
+
+    def mm(out, lhs, rhs, start=True, stop=True):
+        op("T", lambda e: e.matmul(ap(out), ap(lhs), ap(rhs), start, stop), [lhs, rhs], [out])
+
+    def iota(out, pat, base, cm):
+        small = SCRATCH[out[0]][2] != I32
+        op("G", lambda e: e.iota(ap(out), pat, base, cm, allow_small_or_imprecise_dtypes=True) if small else e.iota(ap(out), pat, base, cm), [], [out])
+
+    def asel(out, a, pat, o, fv, base, cm):
+        op("G", lambda e: e.affine_select(ap(out), ap(a), pat, o, fv, base, cm), [a], [out])
+
+    def lists(out, S, src, width):
+        for r in range(16):
+            mm(R(out[0], out[1], out[1] + width), R(S, 128 * r, 128 * r + 128), R(src, r, 16 * width, 16), r == 0, r == 15)
+
+    def lists2(bank, c, S, width):
+        for r in range(16):
+            mm(R(bank, c, c + width), R(S, 128 * r, 128 * r + 128), R("FF", r, 16 * width, 16), r == 0, r == 15)
+
+    DJ = R("p2", 384, 512)
+
+    dma("S", T["KI"][:, :], T["kt"][:, :], [], [R("KI")])
+    dma("C", T["NXC"][:, :], T["nx"][:, :], [], [R("NXC")])
+    dma("S", ap(R("H0")), T["hm"][:, :], [], [R("H0")])
+    dma("S", T["TX"][:, 0:P], T["xp"][:, :], [], [R("TX", 0, P)])
+    dma("C", T["TH"][0:8, :], T["th"][:, :], [], [R("TH")])
+    dma("C", T["BMC"][:, :], T["bm"][:, :], [], [R("BMC")])
+    dma("S", T["XV"][:, :], T["xp"][:, :], [], [R("XV")])
+    dma("S", T["PL"][:, :], T["pl"][:, :], [], [R("PL")])
+
+    fill(R("ONE"), 1.0)
+    fill(R("ON2"), 1.0)
+    fill(R("ZER"), 0.0)
+    iota(R("IP"), [[0, 2]], 0, 1)
+    iota(R("BD0"), [[0, 8], [1, 16]], 0, 0)
+    asel(R("BD1"), R("BD0"), [[-16, 8], [0, 16]], Op.is_ge, -1.0, 0, 1)
+    asel(R("BD"), R("BD1"), [[16, 8], [0, 16]], Op.is_ge, -1.0, 15, -1)
+    asel(R("ID"), R("ONE"), [[-1, 128]], Op.is_equal, 0.0, 0, 1)
+    iota(R("IC"), [[1, 128]], 0, 128)
+    iota(R("I12"), [[32, 6], [0, 2]], 0, 0)
+    asel(R("SP"), R("ONE"), [[-1, 128]], Op.is_equal, 0.0, 16, 1)
+    asel(R("SM"), R("ONE"), [[-1, 128]], Op.is_equal, 0.0, -16, 1)
+    e8 = slice(0, 8)
+    asel(R("TSx", p=e8), R("ONE", p=e8), [[1, 128]], Op.is_ge, 0.0, 0, -16)
+    asel(R("TSR", p=e8), R("TSx", p=e8), [[-1, 128]], Op.is_ge, 0.0, 15, 16)
+    asel(R("TS0", p=e8), R("ONE", p=e8), [[-2, 4], [0, 32]], Op.is_equal, 0.0, 0, 1)
+    asel(R("TS1", p=e8), R("ONE", p=e8), [[-2, 4], [0, 32]], Op.is_equal, 0.0, -1, 1)
+    iota(R("IQ"), [[1, 129]], -129, 0)
+    iota(R("R16"), [[1, 16]], 0, 0)
+    iota(R("IL"), [[16, 128]], 0, 0)
+    asel(R("N3a"), R("ONE"), [[-32, 4], [0, 32]], Op.is_ge, 0.0, 0, 1)
+    asel(R("N3b"), R("N3a"), [[32, 4], [0, 32]], Op.is_ge, 0.0, 31, -1)
+
+    PM, RM1, RM0 = col("CO", 0), col("CO", 1), col("CO", 2)
+    WY, WN, WQ, K64, W140, P32 = (col("CO", j) for j in range(3, 9))
+    ts(R("IW", 0, 1), R("IP", 0, 1), 15, Op.bitwise_and)
+    ts(R("IW", 1, 2), R("IP", 1, 2), 31, Op.bitwise_and)
+    cp(PM, R("IW", 0, 1))
+    for j, (f, w) in enumerate(((0, 16.0), (1, 1.0), (2, 16.0), (3, 1.0), (0, 1.0), (4, -128.0), (1, 1.0))):
+        ts(col("CT", j), PM, float(f), Op.is_equal, w, Op.mult)
+    tt(WY, col("CT", 0), col("CT", 1), Op.add)
+    tt(WN, col("CT", 2), col("CT", 3), Op.add)
+    tt(WQ, col("CT", 4), col("CT", 5), Op.add)
+    for j, w in enumerate((WN, col("CT", 6), WQ)):
+        ts(col("CT", 8 + j), w, 1.0 / 1024, Op.mult)
+    ts(K64, PM, 64.0, Op.mult)
+    for r in range(16):
+        ts(R("SU", 128 * r, 128 * r + 128), R("BD"), float(r), Op.is_equal, 1024.0, Op.mult)
+    act_scale(R("SN"), R("SU"), col("CT", 8))
+    act_scale(R("SR"), R("SU"), col("CT", 9))
+    ts(R("CW", 256, 384), R("NXC"), 4, Op.logical_shift_right)
+    ts(R("CW", 384, 512), R("NXC"), 15, Op.bitwise_and)
+    ts(R("ICm"), R("IC"), P - 1, Op.bitwise_and)
+    ts(R("CW", 0, 128), R("ICm"), 4, Op.logical_shift_right)
+    ts(R("CW", 128, 256), R("ICm"), 15, Op.bitwise_and)
+    cp(R("CF"), R("CW"))
+    for f in range(16):
+        src = R("CF", 128 * f, 128 * f + 128) if f < 4 else R("ONE" if f == 4 else "ZER")
+        dst = R("TF", 0, P, 1, slice(f, 128, 16))
+        dma("S", ap(dst), ap(src), [src], [dst])
+    cp(R("K0"), R("KI"))
+    for k in range(16):
+        cp(R("HX", k, NX * 16, 16), R("H0", 0, NX))
+    ts(R("THw", 0, 2, 1, e8), R("TH", 0, 2, 1, e8), 4032, Op.bitwise_and)
+    ts(R("THw", 2, 4, 1, e8), R("TH", 0, 2, 1, e8), 63, Op.bitwise_and)
+    cp(R("THf", 0, 4, 1, e8), R("THw", 0, 4, 1, e8))
+    for j in range(2):
+        mm(R("p7", 200, 202), R("TSR", p=e8), R("THf", 2 * j, 2 * j + 2, 1, e8), j == 0, j == 1)
+    for s in range(2):
+        for j in range(2):
+            mm(R("p7", 202 + s, 203 + s), R("TS%d" % s, p=e8), R("THf", 2 * j, 2 * j + 1, 1, e8), j == 0, j == 1)
+    ts(R("KBM"), R("ID"), K64, Op.mult)
+    ts(R("NI"), R("ID"), -1.0, Op.mult)
+
+    def more_constants():
+        ts(R("BO"), R("BD"), 0.0, Op.is_ge)
+        cp(P32, R("IW", 1, 2))
+        ts(R("RC"), R("R16"), PM, Op.is_equal, VOID, Op.mult)
+        ts(R("WYR"), R("BO"), WY, Op.mult)
+        ts(R("IV"), R("I12"), P32, Op.add)
+        act_scale(R("SQ"), R("SU"), col("CT", 10))
+        for r in range(16):
+            act_scale(R("MT", 128 * r, 128 * r + 128), R("BO"), col("RC", r))
+        lists(R("p2", 0), "SN", "TF", 128)
+        act(R("NL"), R("p2", 0, 128))
+        fill(R("TF", VO, TW), 0.0)
+        iota(R("RS0"), [[0, 2 * L]], 2 ** 24 - 1, 0)
+        asel(R("RST"), R("RS0"), [[0, 24], [1, 16]], Op.is_equal, -BIG, 0, 0)
+        fill(R("TX", VO, TW), 1024.0)
+        fill(R("BMR"), 0.0)
+        ts(R("BMw", 0, 12), R("BMC"), 4, Op.logical_shift_right)
+        ts(R("BMw", 12, 24), R("BMC"), 15, Op.bitwise_and)
+        ts(R("IX", 0, 12), R("IV"), 63, Op.bitwise_and)
+        ts(R("IX", 12, 24), R("IV"), 6, Op.logical_shift_right)
+        ts(W140, PM, 2.0, Op.is_equal, float(VO // 16), Op.mult)
+        cp(R("BMf"), R("BMw"))
+        for f in range(2):
+            src, dst = R("BMf", 12 * f, 12 * f + 12), R("BMR", 0, L, 1, slice(f, 128, 16))
+            dma("S", ap(dst), ap(src), [src], [dst])
+        ts(RM1, R("IW", 1, 2), 16.0, Op.is_ge)
+        ts(RM0, R("IW", 1, 2), 16.0, Op.is_lt)
+        ts(R("TF", HS, VO), R("ON2"), W140, Op.mult)
+        ts(R("CV", 0, 12), R("IX", 0, 12), 64.0, Op.add)
+        ts(R("CV", 12, 24), R("IX", 12, 24), float(HS // 64 - 1), Op.add)
+        for w, wt in enumerate((1.0, 64.0)):
+            for u in range(2):
+                for s in range(2):
+                    m = "ID" if u == s else ("SP" if s else "SM")
+                    j = 4 * w + 2 * u + s
+                    ts(R("PP", 128 * j, 128 * j + 128), R(m), RM1 if u else RM0, Op.mult, wt, Op.mult)
+        cp(R("T2"), R("p7", 200, 202))
+        ts(R("T1K"), R("p7", 202, 204), 1024.0, Op.mult)
+        ts(R("THR"), R("p7", 202, 204), 1024.0, Op.mult)
+        for r in range(16):
+            asel(R("SY", 128 * r, 128 * r + 128), R("WYR"), [[0, 8], [1, 16]], Op.is_equal, 0.0, -r, 0)
+        dma("S", ap(R("BB")), ap(R("TF", 0, P)), [R("TF", 0, P)], [R("BB")])
+
+    def late_constants():
+        ts(R("JL", 0, 64), R("IL", 0, 64), PM, Op.add)
+        ts(R("JL", 64, 128), R("IL", 64, 128), PM, Op.add)
+        ts(R("N32"), R("N3b"), -1.0, Op.mult)
+        ts(R("WNR"), R("BO"), WN, Op.mult)
+
+    def bookmarks():
+        agather(R("FB"), R("TF", 0, P), R("BU"))
+        bookmark_fields()
+
+    def bookmark_fields():
+        lists(R("p6", 100), "SY", "FB", 12)
+        lists(R("p6", 112), "SN", "FB", 12)
+
+    def bookmark_lists():
+        act(R("JB", 0, 12), R("p6", 100, 112))
+        act_lin(R("JB", 12, 24), R("p6", 112, 124), 1.0, -float(VO))
+
+    for t in range(NV):
+        last = t == NV - 1
+        H, K = "H%d" % t, "K%d" % t
+        if t:
+            cp(R("KI"), R(K))
+        agather(R("GB"), R("TX", 0, P), R(K, NX, L))
+        nc = len(CHUNKS) - 1
+        for c in range(nc):
+            a, b = CHUNKS[c], CHUNKS[c + 1]
+            ttgather(R("DX", 16 * a, 16 * b), R("TX", 0, P), R(K, a, b), R("HX", 16 * a, 16 * b), Op.subtract)
+
+        def sums(i0, i1, *srcs):
+            o = R("p0", i0, i1)
+            mm(o, R("KBM"), R("ON2", 0, i1 - i0), True, False)
+            for src in srcs:
+                for k in range(16):
+                    mm(o, R("SU", 128 * k, 128 * k + 128), src(k), False, k == 15 and src is srcs[-1])
+
+        def sums_c(c):
+            a, b = CHUNKS[c], CHUNKS[c + 1]
+            if c == nc - 1:
+                if t:
+                    cp(R("AI"), R("p6", 200, 202))
+                ts(R("AX", 16 * a, 16 * b), R("DX", 16 * a, 16 * b), -2.0, Op.mult, 0.0, Op.max)
+                sums(a, b, lambda k: R("DX", 16 * a + k, 16 * b, 16), lambda k: R("AX", 16 * a + k, 16 * b, 16))
+            else:
+                act(R("AX", 16 * a, 16 * b), R("DX", 16 * a, 16 * b), Act.Abs)
+                sums(a, b, lambda k: R("AX", 16 * a + k, 16 * b, 16))
+
+        for k in range(16):
+            o = R("p%d" % (1 + k // 8), (k % 8) * CB, (k % 8) * CB + CB)
+            mm(o, R("ID"), R("GB", k, 16 * CB, 16), True, False)
+            mm(o, R("NI"), R(H, NX, L), False, True)
+        sums_c(0)
+        for j in range(2):
+            act(R("AB", 8 * CB * j, 8 * CB * j + 8 * CB), R("p%d" % (1 + j), 0, 8 * CB), Act.Abs)
+        for c in range(nc - 1, 0, -1):
+            sums_c(c)
+        sums(NX, L, lambda k: R("AB", CB * k, CB * k + CB))
+        act(R("TX", HS, VO), R(H))
+        ts(R("KA", 0, L), R("KI"), 63, Op.bitwise_and)
+        if t:
+            ts(R("AJ"), R("AI"), 31, Op.bitwise_and)
+        ts(R("KA", L, 2 * L), R("KI"), 6, Op.logical_shift_right)
+        if t:
+            ts(R("AK"), R("AJ"), 1024.0, Op.mult)
+            tt(R("THR"), R("AK"), R("T1K"), Op.add)
+            bookmarks()
+            act(R("JL", SPLIT[2], 128), R("p7", SPLIT[2], 128))
+            act(R("JL", 0, SPLIT[2]), R("p5", 0, SPLIT[2]))
+            bookmark_lists()
+        else:
+            more_constants()
+        def half(name, w):
+            return R(name, L * w, L * w + L)
+
+        def twelve(name, w):
+            return R(name, 12 * w, 12 * w + 12)
+
+        for w in range(2):
+            tt(half("KAB", w), R("p0", 0, L), half("KA", w), Op.add)
+        for w in range(2):
+            op("V", lambda e: e.transpose(ap(half("VT", w)), ap(half("KAB", w))), [half("KAB", w)], [half("VT", w)])
+        for w in range(2):
+            op("V", lambda e: e.tensor_tensor_scan(ap(half("MS", w)), ap(half("RST", w)), ap(half("VT", w)), BIG, Op.max, Op.min), [half("RST", w), half("VT", w)], [half("MS", w)])
+        cp(twelve("MI", 0), R("MS", 15, L, 16))
+        for s in range(2):
+            ts(R("MV", s, 12, 2), R("MS", 15 + 16 * s, L, 32), col("THR", s), Op.is_ge)
+        cp(twelve("MI", 1), R("MS", L + 15, 2 * L, 16))
+        ts(twelve("ML", 0), twelve("MI", 0), 63, Op.bitwise_and)
+        for w in range(2):
+            tt(twelve("SEL", w), R("MV"), twelve("CV", w), Op.mult)
+        ts(twelve("ML", 1), twelve("MI", 1), 63, Op.bitwise_and)
+        for w in range(2):
+            tt(twelve("LB", w), twelve("ML", w), twelve("SEL", w), Op.max)
+        for u in range(2):
+            for w in range(2):
+                for s in range(2):
+                    j = 4 * w + 2 * u + s
+                    mm(R("p3", u, 12, 2), R("PP", 128 * j, 128 * j + 128), R("LB", 12 * w + s, 12 * w + 12, 2), w == 0 and s == 0, w == 1 and s == 1)
+        cp(R("L1"), R("p3", 0, 12))
+
+        def missed():
+            tt(R("YM", 0, 12), R("JB", 0, 12), R("MISS"), Op.mult)
+            tt(R("YM", 12, 24), R("JB", 12, 24), R("MISS"), Op.mult)
+
+        ttgather(R("SI"), R("TX", 0, VO), R("L1"), R(H), Op.add)
+        agather(R("FY"), R("TF", 0, VO), R("L1"))
+        ts(R("MISS"), R("p3", 0, 12), float(HS), Op.is_ge)
+        ts(R("Q1"), R("SI"), 1, Op.arith_shift_right)
+        if t and not last:
+            missed()
+        lists(R("p3", 16), "SN", "FY", 12)
+        if t == 0:
+            late_constants()
+        tt(DJ, R("NL"), R("JL"), Op.subtract)
+        cp(R("M1"), R("p3", 16, 28))
+        ttgather(R("E2"), R("TX"), R("M1"), R("Q1"), Op.subtract)
+        agather(R("FN"), R("TF"), R("M1"))
+        act(R("AE"), R("E2"), Act.Abs)
+        def one_hot(j):
+            if j < 12:
+                ts(R("OR", 128 * j, 128 * j + 128), R("BD"), col("QR", 24 + j), Op.is_equal)
+            else:
+                ts(R("OR", 128 * j, 128 * j + 128), R("BD"), col("QR", 24 + j), Op.is_equal, col("BRL", j - 12), Op.mult)
+
+        def steps(j):
+            if j < 24 - NQ:
+                act_bias(R("OQ", QW * j, QW * j + 129), R("IQ"), Act.Sign, col("QR", j))
+            else:
+                ts(R("OQ", QW * j, QW * j + 129), R("IQ"), col("QR", j), Op.add, 0.0, Op.is_gt)
+
+        def products(j0, j1):
+            for j in range(j0, j1):
+                mm(R("p0", 0, 129), R("OR", 128 * j, 128 * j + 128), R("OQ", QW * j, QW * j + 129), j == 0, j == 23)
+
+        lists(R("p6", 140), "SR", "FY", 12)
+        lists(R("p4", 0), "SQ", "FY", 12)
+        mm(R("p5", 0, L), R("BO"), R("AE"))
+        cp(R("QR", 24, 36), R("p6", 140, 152))
+        ts(R("F2"), R("E2"), 0.5, Op.mult, -0.25, Op.add)
+        act_lin(R("QR", 0, 12), R("p4", 0, 12), -1.0, 0.5)
+        for j in range(12):
+            steps(j)
+        for j in range(PRE):
+            one_hot(j)
+        ts(R("BR"), R("p5", 0, L), col("T2", 1), Op.is_le)
+        for j in range(PRE, 12):
+            one_hot(j)
+        lists(R("p4", 12), "SQ", "FN", 12)
+        lists(R("p3", 52), "SR", "FN", 12)
+        lists(R("p7", 0), "SU", "BR", 12)
+        if t == 0:
+            lists(R("p6", 0), "SY", "BMR", 12)
+        products(0, 12)
+        mm(R("p1", 0, L), R("ID"), R("FN"), True, False)
+        mm(R("p1", 0, L), R("NI"), R("FY"), False, True)
+        act_lin(R("QR", 12, 24), R("p4", 12, 24), -1.0, 0.5)
+        tt(R("p2", 0, L), R("F2"), R("BR"), Op.mult)
+        cp(R("QR", 36, 48), R("p3", 52, 64))
+        tt(R("HS%d" % t), R("p2", 0, L), R("Q1"), Op.add)
+        cp(R("BRL"), R("p7", 0, 12))
+        if not last:
+            deps("G", [R("HS%d" % t)], [])
+            g.remote_dma(ap(R("H%d" % (t + 1))), ap(R("HS%d" % t)), T.sem["ha%d" % (t + 1)], T.sem["loc"], pid, rid, mask)
+        else:
+            dma("S", T["yh"][:, :], ap(R("HS%d" % t)), [R("HS%d" % t)], [])
+        if t == 0:
+            cp(R("BU"), R("p6", 0, 12))
+            agather(R("FB"), R("TF", 0, P), R("BU"))
+        for j in range(24 - NQ, 24):
+            steps(j)
+        for j in range(12, 24):
+            if j < 24 - NQ:
+                steps(j)
+            one_hot(j)
+        products(12, 24)
+        tt(R("GF"), R("p1", 0, L), R("BR"), Op.mult)
+        if not last:
+            for k, src in enumerate(("FY", "GF")):
+                for r in range(16):
+                    mm(R("p5", 256, 268), R("SY", 128 * r, 128 * r + 128), R(src, r, L, 16), k == 0 and r == 0, k == 1 and r == 15)
+            if t == 0:
+                bookmark_fields()
+                bookmark_lists()
+            lists(R("p4", 100), "SN", "GF", 12)
+        hs = ((64, 128), (0, 64))
+        for a, b in hs:
+            cp(R("CS", a, b), R("p0", a, b))
+        for a, b in hs:
+            tt(R("MK", a, b), R("p0", a + 1, b + 1), R("CS", a, b), Op.is_gt)
+        for a, b in hs:
+            tt(R("p2", a, b), R("MK", a, b), R("p2", 384 + a, 384 + b), Op.mult)
+        for a, b in hs:
+            tt(R("ZF", a, b), R("p2", a, b), R("JL", a, b), Op.add)
+        for a, b in hs:
+            cp(R("ZU", a, b), R("ZF", a, b))
+        s1, s2, s3 = SPLIT
+        if last:
+            s1 = LAST1
+        agather(R("B1", 16 * s1, P), R("BB"), R("ZU", s1, 128))
+        if not last:
+            if t == 0:
+                vgather(R("B1", 0, 16 * s1), R("BB"), R("ZU", 0, s1))
+                missed()
+            tt(R("YF"), R("p5", 256, 268), R("YM", 0, 12), Op.add)
+            tt(R("BN"), R("p3", 16, 28), R("YM", 12, 24), Op.add)
+            cp(R("YU"), R("YF"))
+            vgather(R("KS%d" % t), R("PL"), R("YU"))
+            deps("G", [R("KS%d" % t)], [])
+            g.remote_dma(ap(R("K%d" % (t + 1))), ap(R("KS%d" % t)), T.sem["ka%d" % (t + 1)], T.sem["loc"], pid, rid, mask)
+            tt(R("BF"), R("p4", 100, 112), R("BN"), Op.add)
+        if t:
+            vgather(R("B1", 0, 16 * s1), R("BB"), R("ZU", 0, s1))
+        if last:
+            mm(R("p5", 0, L), R("WNR"), R("FY"), True, False)
+            mm(R("p5", 0, L), R("WNR"), R("GF"), False, True)
+            mm(R("p6", 0, L), R("WNR"), R("FB"))
+            cp(R("RB", 0, L), R("p5", 0, L))
+            tt(R("RB", L, 2 * L), R("p6", 0, L), R("RB", 0, L), Op.subtract)
+            ts(R("RB", 2 * L, 3 * L), R("RB", 0, L), float(P), Op.is_ge)
+        vgather(R("TF", 0, 16 * s2), R("B1"), R("ZU", 0, s2))
+        agather(R("TF", 16 * s2, P), R("B1"), R("ZU", s2, 128))
+        if last:
+            tt(R("RB", 3 * L, 4 * L), R("RB", L, 2 * L), R("RB", 2 * L, 3 * L), Op.mult)
+            tt(R("RB", L, 2 * L), R("RB", 3 * L, 4 * L), R("RB", 0, L), Op.add)
+            src = R("RB", L, 2 * L, 1, slice(0, 128, 16))
+            dma("S", T["yb"][:, :], ap(src), [src], [])
+            for j in range(4):
+                mm(R("p%d" % (1 + j), 0, 512), R("WYR"), R("TF", 512 * j, 512 * j + 512))
+                if j % 2:
+                    act(R("ROW", 512 * j, 512 * j + 512), R("p%d" % (1 + j)))
+                else:
+                    cp(R("ROW", 512 * j, 512 * j + 512), R("p%d" % (1 + j)))
+            src = R("ROW", 0, P, 1, slice(0, 128, 16))
+            dma("S", T["yj"][:, :], ap(src), [src], [])
+            break
+        for j in range(4):
+            b = "p%d" % (1 + j)
+            if j >= 2:
+                mm(R(b), R("ID"), R("XV", 512 * j, 512 * j + 512), True, False)
+            for r in range(16):
+                mm(R(b, r, 512, 16), R("MT", 128 * r, 128 * r + 128), R("MK", 32 * j, 32 * j + 32), j < 2, j < 2 or r == 15)
+        for b, q0, q1 in (("p5", 0, s3), ("p7", s3, 128)):
+            for r in range(16):
+                mm(R(b, q0, q1), R("SY", 128 * r, 128 * r + 128), R("TF", 16 * q0 + r, 16 * q1, 16), r == 0, r == 15)
+        for j in (2, 3):
+            act(R("XV", 512 * j, 512 * j + 512), R("p%d" % (1 + j)))
+        tt(R("XV", 0, 512), R("XV", 0, 512), R("p1"), Op.add)
+        tt(R("XV", 512, 1024), R("XV", 512, 1024), R("p2"), Op.add)
+        h1 = "H%d" % (t + 1)
+        cnt = len(topo.engines(prv, core))
+        arrive(h1, "ha%d" % (t + 1), cnt)
+        arrive("K%d" % (t + 1), "ka%d" % (t + 1), cnt)
+        for k in range(GK):
+            asel(R("HX", k, NX * 16, 16), R(h1, 0, NX), [[0, NX]], Op.is_ge, 0.0, 1, 0)
+        for k in range(GK, 16):
+            cp(R("HX", k, NX * 16, 16), R(h1, 0, NX))
+        cp(R("JU", 0, s3), R("p5", 0, s3))
+        cp(R("BU"), R("BF"))
+        cp(R("JU", s3, 128), R("p7", s3, 128))
+        vgather(R("TX", 0, 16 * s3), R("XV"), R("JU", 0, s3))
+        agather(R("TX", 16 * s3, P), R("XV"), R("JU", s3, 128))
+        for b in range(6):
+            mm(R("p6", 200, 202), R("N32"), R("MV", 2 * b, 2 * b + 2), b == 0, b == 5)
+    finish()
+    g.wait_ge(T.sem["loc"], 2 * (NV - 1) * len(topo.engines(core, nxt)))

@@ -1,69 +1,64 @@
 from concourse.mybir import AluOpType as Op, ActivationFunctionType as Act
 
 BIG = 1.0e9
-VOID = 640.0
+VOID = 8192.0
+GATE = 8192.0
 L, P, NV = 192, 2048, 5
 HS = P
 VO = P + L
-TW = VO + 16
 NX = 128
 CB = L - NX
-CHUNKS = (0, 64, 128)
-QW = 130
-PRE = 5
-NQ = 5
-LAST1 = 60
-SPLIT = (50, 60, 60)
-GK = 9
+SPLIT = (56, 62, 62)
+LAST = (60, 64)
+GK = 5
+HI, LO, NH, NL, ONE, L2, C1, C2, C3 = range(9)
 
 B16, F32, I32, U16 = "bfloat16", "float32", "int32", "uint16"
 SCRATCH = {
-    "TX": ("sbuf", [128, TW], B16), "XV": ("sbuf", [128, P], B16), "TF": ("sbuf", [128, TW], B16),
+    "TX": ("sbuf", [128, VO], B16), "XV": ("sbuf", [128, P], B16), "TF": ("sbuf", [128, VO], B16),
     "BB": ("sbuf", [128, P], B16), "B1": ("sbuf", [128, P], B16), "PL": ("sbuf", [128, P], I32),
+    "IOT": ("sbuf", [128, P], F32), "BF1": ("sbuf", [128, P], F32), "ROW": ("sbuf", [128, P], F32), "RB": ("sbuf", [128, L], F32),
     "HX": ("sbuf", [128, NX * 16], B16), "DX": ("sbuf", [128, NX * 16], B16), "AX": ("sbuf", [128, NX * 16], B16),
     "GB": ("sbuf", [128, CB * 16], B16), "AB": ("sbuf", [128, CB * 16], B16),
     "KI": ("sbuf", [128, L], I32), "KA": ("sbuf", [128, 2 * L], I32), "KAB": ("sbuf", [128, 2 * L], F32),
-    "VT": ("sbuf", [128, 2 * L], F32), "MS": ("sbuf", [128, 2 * L], F32), "RST": ("sbuf", [128, 2 * L], F32), "RS0": ("sbuf", [128, 2 * L], F32),
+    "VT": ("sbuf", [128, 2 * L], F32), "MS": ("sbuf", [128, 2 * L], F32), "RST": ("sbuf", [128, L], F32), "RS0": ("sbuf", [128, L], F32),
     "MI": ("sbuf", [128, 24], I32), "ML": ("sbuf", [128, 24], I32), "LB": ("sbuf", [128, 24], B16), "MV": ("sbuf", [128, 12], B16),
-    "L1": ("sbuf", [128, 12], U16), "MISS": ("sbuf", [128, 12], F32), "CV": ("sbuf", [128, 24], F32), "SEL": ("sbuf", [128, 24], F32),
+    "L1": ("sbuf", [128, 12], U16), "CV": ("sbuf", [128, 24], F32), "SEL": ("sbuf", [128, 24], F32),
     "IV": ("sbuf", [128, 12], I32), "IX": ("sbuf", [128, 24], I32),
-    "SI": ("sbuf", [128, L], I32), "Q1": ("sbuf", [128, L], I32), "FF": ("sbuf", [128, 3 * L], B16),
+    "SI": ("sbuf", [128, L], I32), "Q1": ("sbuf", [128, L], I32), "FF": ("sbuf", [128, 2 * L], B16), "GF": ("sbuf", [128, L], B16),
     "M1": ("sbuf", [128, 12], U16), "E2": ("sbuf", [128, L], B16), "AE": ("sbuf", [128, L], B16), "F2": ("sbuf", [128, L], I32),
-    "BR": ("sbuf", [128, L], B16), "QR": ("sbuf", [128, 48], F32), "BRL": ("sbuf", [128, 12], F32),
-    "BN": ("sbuf", [128, 12], F32), "YM": ("sbuf", [128, 24], F32),
-    "YF": ("sbuf", [128, 12], F32), "YU": ("sbuf", [128, 12], U16), "BF": ("sbuf", [128, 12], F32), "BU": ("sbuf", [128, 12], U16),
-    "JB": ("sbuf", [128, 24], F32), "FB": ("sbuf", [128, L], B16),
-    "OR": ("sbuf", [128, 24 * 128], B16), "OQ": ("sbuf", [128, 24 * QW], B16), "CS": ("sbuf", [128, 128], F32),
-    "MK": ("sbuf", [128, 128], B16), "JL": ("sbuf", [128, 128], F32), "NL": ("sbuf", [128, 128], F32),
-    "ZF": ("sbuf", [128, 128], F32), "ZU": ("sbuf", [128, 128], U16), "JU": ("sbuf", [128, 128], U16),
+    "BS": ("sbuf", [128, L], B16), "BR": ("sbuf", [128, L], B16), "YU": ("sbuf", [128, 12], U16), "BU": ("sbuf", [128, 12], U16),
+    "MM": ("sbuf", [128, 3 * 128], B16), "NN": ("sbuf", [128, 24 * 128], B16),
+    "MK": ("sbuf", [128, 128], B16), "UH": ("sbuf", [128, 128], B16), "UL": ("sbuf", [128, 128], B16), "VL": ("sbuf", [128, 128], B16),
+    "DI": ("sbuf", [128, 128], I32), "DH": ("sbuf", [128, 128], I32), "DL": ("sbuf", [128, 128], I32),
+    "ZU": ("sbuf", [128, 128], U16), "JU": ("sbuf", [128, 128], U16),
     "AI": ("sbuf", [128, 2], I32), "AJ": ("sbuf", [128, 2], I32), "AK": ("sbuf", [128, 2], F32), "THR": ("sbuf", [128, 2], F32),
-    "T1K": ("sbuf", [128, 2], F32), "T2": ("sbuf", [128, 2], F32),
-    "ROW": ("sbuf", [128, P], F32), "RB": ("sbuf", [128, 4 * L], F32),
-    "BD": ("sbuf", [128, 128], B16), "ONE": ("sbuf", [128, 128], B16), "ZER": ("sbuf", [128, 128], B16), "ON2": ("sbuf", [128, L], B16),
+    "T1K": ("sbuf", [128, 2], F32),
+    "BD": ("sbuf", [128, 128], B16), "ONES": ("sbuf", [128, 128], B16), "ON2": ("sbuf", [128, L], B16),
     "ID": ("sbuf", [128, 128], B16), "NI": ("sbuf", [128, 128], B16), "SP": ("sbuf", [128, 128], B16), "SM": ("sbuf", [128, 128], B16),
-    "N32": ("sbuf", [128, 128], B16), "KBM": ("sbuf", [128, 128], B16), "BO": ("sbuf", [128, 128], B16),
-    "WYR": ("sbuf", [128, 128], B16), "WNR": ("sbuf", [128, 128], B16), "IQ": ("sbuf", [128, 129], B16),
-    "SU": ("sbuf", [128, 2048], B16), "SY": ("sbuf", [128, 2048], B16), "SN": ("sbuf", [128, 2048], B16), "SQ": ("sbuf", [128, 2048], B16),
-    "SR": ("sbuf", [128, 2048], B16), "MT": ("sbuf", [128, 2048], B16), "PP": ("sbuf", [128, 8 * 128], B16),
-    "CO": ("sbuf", [128, 16], F32), "CT": ("sbuf", [128, 16], F32), "RC": ("sbuf", [128, 16], F32), "R16": ("sbuf", [128, 16], F32),
-    "IP": ("sbuf", [128, 2], I32), "IW": ("sbuf", [128, 2], I32), "IL": ("sbuf", [128, 128], I32), "I12": ("sbuf", [128, 12], I32), "IC": ("sbuf", [128, 128], I32),
-    "CF": ("sbuf", [128, 4 * 128], B16), "CW": ("sbuf", [128, 4 * 128], I32), "NXC": ("sbuf", [128, 128], I32), "ICm": ("sbuf", [128, 128], I32),
+    "N32": ("sbuf", [128, 128], B16), "KBM": ("sbuf", [128, 128], B16), "BO": ("sbuf", [128, 128], B16), "NBO": ("sbuf", [128, 128], B16),
+    "IDW": ("sbuf", [128, 3 * 128], B16), "WNR": ("sbuf", [128, 128], B16), "IQ": ("sbuf", [128, 128], B16),
+    "WM": ("sbuf", [128, 128], B16), "WG": ("sbuf", [128, 128], B16), "WD": ("sbuf", [128, 8], B16), "WT": ("sbuf", [128, 4 * 128], B16),
+    "SU": ("sbuf", [128, 2048], B16), "SY": ("sbuf", [128, 2048], B16), "SN": ("sbuf", [128, 2048], B16), "SF": ("sbuf", [128, 2048], B16),
+    "PP": ("sbuf", [128, 8 * 128], B16), "CO": ("sbuf", [128, 32], F32), "EQ": ("sbuf", [128, 16], F32), "R16": ("sbuf", [128, 16], F32),
+    "IP": ("sbuf", [128, 2], I32), "IW": ("sbuf", [128, 2], I32), "I12": ("sbuf", [128, 12], I32),
+    "CF": ("sbuf", [128, 4 * 128], B16), "CW": ("sbuf", [128, 2 * 128], I32), "NXC": ("sbuf", [128, 128], I32),
     "BMC": ("sbuf", [128, 12], I32), "BMw": ("sbuf", [128, 24], I32), "BMf": ("sbuf", [128, 24], B16), "BMR": ("sbuf", [128, L], B16),
     "TH": ("sbuf", [128, 2], I32), "THw": ("sbuf", [128, 4], I32), "THf": ("sbuf", [128, 4], B16),
     "TSR": ("sbuf", [128, 128], B16), "TSx": ("sbuf", [128, 128], B16), "TS0": ("sbuf", [128, 128], B16), "TS1": ("sbuf", [128, 128], B16),
-    "TMP": ("sbuf", [128, 512], B16),
+    "TMP": ("sbuf", [128, 5 * 128], B16),
     "HH": ("sbuf", [128, 2 * NV * L], B16), "KK": ("sbuf", [128, 2 * NV * L], U16),
 }
-ALIAS = {}
+ALIAS = {"FY": ("FF", 0, L), "FN": ("FF", L, L)}
 for _t in range(NV):
     ALIAS["H%d" % _t] = ("HH", L * _t, L)
     ALIAS["HS%d" % _t] = ("HH", L * (NV + _t), L)
     ALIAS["K%d" % _t] = ("KK", L * _t, L)
     ALIAS["KS%d" % _t] = ("KK", L * (NV + _t), L)
-for _k, _n in enumerate(("BD0", "BD1", "N3a", "N3b")):
+for _k, _n in enumerate(("BD0", "BD1", "N3a", "N3b", "IH")):
     ALIAS[_n] = ("TMP", 128 * _k, 128)
-for _k, _n in enumerate(("FY", "FN", "GF")):
-    ALIAS[_n] = ("FF", L * _k, L)
+for _k, _n in enumerate(("I16", "IM", "IVD")):
+    ALIAS[_n] = ("IDW", 128 * _k, 128)
 for _t in range(8):
     SCRATCH["p%d" % _t] = ("psum", [128, 512], F32)
 NDMA = 32
@@ -166,6 +161,14 @@ def col(name, j):
     return R(name, j, j + 1)
 
 
+def row(name, f, c0, c1):
+    return R(name, c0, c1, 1, slice(f, 128, 16))
+
+
+def blk(name, j, w=128):
+    return R(name, w * j, w * j + w)
+
+
 def rank_program(g, core, T, topo):
     rank = T.rank_of(core)
     if rank is None:
@@ -194,14 +197,8 @@ def rank_program(g, core, T, topo):
     def fill(out, c):
         op("V", lambda e: e.memset(ap(out), c), [], [out])
 
-    def act(out, a, f=Act.Copy):
-        op("A", lambda e: e.activation(ap(out), ap(a), f), [a], [out])
-
-    def act_bias(out, a, f, b):
-        op("A", lambda e: e.activation(ap(out), ap(a), f, bias=ap(b)), [a, b], [out])
-
-    def act_lin(out, a, sc, bs):
-        op("A", lambda e: e.activation(ap(out), ap(a), Act.Copy, bias=bs, scale=sc), [a], [out])
+    def act(out, a, f=Act.Copy, bias=0.0, scale=1.0):
+        op("A", lambda e: e.activation(ap(out), ap(a), f, bias=bias, scale=scale), [a], [out])
 
     def act_scale(out, a, c):
         op("A", lambda e: e.activation(ap(out), ap(a), Act.Copy, scale=ap(c)), [a, c], [out])
@@ -209,8 +206,11 @@ def rank_program(g, core, T, topo):
     def vgather(out, win, off):
         op("V", lambda e: e.tensor_copy(ap(out), ap(win).indirect(ap(off))), [win, off], [out])
 
-    def agather(out, win, off):
-        op("A", lambda e: e.activation(ap(out), ap(win).indirect(ap(off)), Act.Copy), [win, off], [out])
+    def agather(out, win, off, c=None):
+        if c is None:
+            op("A", lambda e: e.activation(ap(out), ap(win).indirect(ap(off)), Act.Copy), [win, off], [out])
+        else:
+            op("A", lambda e: e.activation(ap(out), ap(win).indirect(ap(off)), Act.Copy, scale=ap(c)), [win, off, c], [out])
 
     def ttgather(out, win, off, b, o):
         op("V", lambda e: e.tensor_tensor(ap(out), ap(win).indirect(ap(off)), ap(b), o), [win, off, b], [out])
@@ -225,190 +225,190 @@ def rank_program(g, core, T, topo):
     def asel(out, a, pat, o, fv, base, cm):
         op("G", lambda e: e.affine_select(ap(out), ap(a), pat, o, fv, base, cm), [a], [out])
 
-    def lists(out, S, src, width):
+    def gcopy(out, a, width):
+        asel(out, a, [[0, width]], Op.is_ge, 0.0, 1, 0)
+
+    def local(q, dst, src):
+        dma(q, ap(dst), ap(src), [src], [dst])
+
+    def lists(bank, c, S, src, q0, q1, start=True, stop=True):
         for r in range(16):
-            mm(R(out[0], out[1], out[1] + width), R(S, 128 * r, 128 * r + 128), R(src, r, 16 * width, 16), r == 0, r == 15)
+            mm(R(bank, c, c + q1 - q0), blk(S, r), R(src, 16 * q0 + r, 16 * q1, 16), start and r == 0, stop and r == 15)
 
-    def lists2(bank, c, S, width):
-        for r in range(16):
-            mm(R(bank, c, c + width), R(S, 128 * r, 128 * r + 128), R("FF", r, 16 * width, 16), r == 0, r == 15)
+    def send(t, name, sem):
+        deps("G", [R("%sS%d" % (name, t))], [])
+        g.remote_dma(ap(R("%s%d" % (name, t + 1))), ap(R("%sS%d" % (name, t))), T.sem["%s%d" % (sem, t + 1)], T.sem["loc"], pid, rid, mask)
+        arrive("%s%d" % (name, t + 1), "%s%d" % (sem, t + 1), len(topo.engines(prv, core)))
 
-    DJ = R("p2", 384, 512)
-
-    dma("S", T["KI"][:, :], T["kt"][:, :], [], [R("KI")])
-    dma("C", T["NXC"][:, :], T["nx"][:, :], [], [R("NXC")])
-    dma("S", ap(R("H0")), T["hm"][:, :], [], [R("H0")])
+    e8 = slice(0, 8)
     dma("S", T["TX"][:, 0:P], T["xp"][:, :], [], [R("TX", 0, P)])
-    dma("C", T["TH"][0:8, :], T["th"][:, :], [], [R("TH")])
-    dma("C", T["BMC"][:, :], T["bm"][:, :], [], [R("BMC")])
-    dma("S", T["XV"][:, :], T["xp"][:, :], [], [R("XV")])
-    dma("S", T["PL"][:, :], T["pl"][:, :], [], [R("PL")])
+    dma("C", T["KI"][:, :], T["kt"][:, :], [], [R("KI")])
+    dma("C", ap(R("H0")), T["hm"][:, :], [], [R("H0")])
+    dma("S", T["NXC"][:, :], T["nx"][:, :], [], [R("NXC")])
+    dma("S", T["BMC"][:, :], T["bm"][:, :], [], [R("BMC")])
+    dma("C", T["TH"][e8, :], T["th"][:, :], [], [R("TH")])
+    dma("C", T["PL"][:, :], T["pl"][:, :], [], [R("PL")])
 
-    fill(R("ONE"), 1.0)
-    fill(R("ON2"), 1.0)
-    fill(R("ZER"), 0.0)
+    PM, RM1, RM0, WY, WN, K64, P32, WF, PM8, NOT1 = (col("CO", j) for j in range(10))
+    CY, CN, CF_, CMa, CMb, CMc, CG, CD, CX, CZ, CV1, CV2 = (col("CO", j) for j in range(10, 22))
+
+    def weights(out, tmp, *pairs):
+        ts(out, col("EQ", pairs[0][0]), pairs[0][1], Op.mult)
+        for f, w in pairs[1:]:
+            ts(out, col("EQ", f), w, Op.mult, out, Op.add)
+
     iota(R("IP"), [[0, 2]], 0, 1)
+    iota(R("R16"), [[1, 16]], 0, 0)
     iota(R("BD0"), [[0, 8], [1, 16]], 0, 0)
+    fill(R("ONES"), 1.0)
+    fill(R("TF"), 1.0)
     asel(R("BD1"), R("BD0"), [[-16, 8], [0, 16]], Op.is_ge, -1.0, 0, 1)
     asel(R("BD"), R("BD1"), [[16, 8], [0, 16]], Op.is_ge, -1.0, 15, -1)
-    asel(R("ID"), R("ONE"), [[-1, 128]], Op.is_equal, 0.0, 0, 1)
-    iota(R("IC"), [[1, 128]], 0, 128)
-    iota(R("I12"), [[32, 6], [0, 2]], 0, 0)
-    asel(R("SP"), R("ONE"), [[-1, 128]], Op.is_equal, 0.0, 16, 1)
-    asel(R("SM"), R("ONE"), [[-1, 128]], Op.is_equal, 0.0, -16, 1)
-    e8 = slice(0, 8)
-    asel(R("TSx", p=e8), R("ONE", p=e8), [[1, 128]], Op.is_ge, 0.0, 0, -16)
-    asel(R("TSR", p=e8), R("TSx", p=e8), [[-1, 128]], Op.is_ge, 0.0, 15, 16)
-    asel(R("TS0", p=e8), R("ONE", p=e8), [[-2, 4], [0, 32]], Op.is_equal, 0.0, 0, 1)
-    asel(R("TS1", p=e8), R("ONE", p=e8), [[-2, 4], [0, 32]], Op.is_equal, 0.0, -1, 1)
-    iota(R("IQ"), [[1, 129]], -129, 0)
-    iota(R("R16"), [[1, 16]], 0, 0)
-    iota(R("IL"), [[16, 128]], 0, 0)
-    asel(R("N3a"), R("ONE"), [[-32, 4], [0, 32]], Op.is_ge, 0.0, 0, 1)
-    asel(R("N3b"), R("N3a"), [[32, 4], [0, 32]], Op.is_ge, 0.0, 31, -1)
-
-    PM, RM1, RM0 = col("CO", 0), col("CO", 1), col("CO", 2)
-    WY, WN, WQ, K64, W140, P32 = (col("CO", j) for j in range(3, 9))
+    iota(R("IH"), [[1, 8], [0, 16]], 0, 0)
+    asel(R("ID"), R("ONES"), [[-1, 128]], Op.is_equal, 0.0, 0, 1)
     ts(R("IW", 0, 1), R("IP", 0, 1), 15, Op.bitwise_and)
     ts(R("IW", 1, 2), R("IP", 1, 2), 31, Op.bitwise_and)
+    fill(R("ON2"), 1.0)
+    fill(R("BMR"), 0.0)
     cp(PM, R("IW", 0, 1))
-    for j, (f, w) in enumerate(((0, 16.0), (1, 1.0), (2, 16.0), (3, 1.0), (0, 1.0), (4, -128.0), (1, 1.0))):
-        ts(col("CT", j), PM, float(f), Op.is_equal, w, Op.mult)
-    tt(WY, col("CT", 0), col("CT", 1), Op.add)
-    tt(WN, col("CT", 2), col("CT", 3), Op.add)
-    tt(WQ, col("CT", 4), col("CT", 5), Op.add)
-    for j, w in enumerate((WN, col("CT", 6), WQ)):
-        ts(col("CT", 8 + j), w, 1.0 / 1024, Op.mult)
+    cp(P32, R("IW", 1, 2))
+    tt(blk("CF", 1), R("BD0"), R("BD0"), Op.mult)
+    ts(R("EQ"), R("R16"), PM, Op.is_equal)
+    ts(PM8, PM, 8.0, Op.mult)
     ts(K64, PM, 64.0, Op.mult)
+    local("S", row("TF", LO, 0, P), R("BD0"))
+    local("S", row("TF", L2, 0, P), blk("CF", 1))
     for r in range(16):
-        ts(R("SU", 128 * r, 128 * r + 128), R("BD"), float(r), Op.is_equal, 1024.0, Op.mult)
-    act_scale(R("SN"), R("SU"), col("CT", 8))
-    act_scale(R("SR"), R("SU"), col("CT", 9))
-    ts(R("CW", 256, 384), R("NXC"), 4, Op.logical_shift_right)
-    ts(R("CW", 384, 512), R("NXC"), 15, Op.bitwise_and)
-    ts(R("ICm"), R("IC"), P - 1, Op.bitwise_and)
-    ts(R("CW", 0, 128), R("ICm"), 4, Op.logical_shift_right)
-    ts(R("CW", 128, 256), R("ICm"), 15, Op.bitwise_and)
-    cp(R("CF"), R("CW"))
-    for f in range(16):
-        src = R("CF", 128 * f, 128 * f + 128) if f < 4 else R("ONE" if f == 4 else "ZER")
-        dst = R("TF", 0, P, 1, slice(f, 128, 16))
-        dma("S", ap(dst), ap(src), [src], [dst])
+        ts(blk("SU", r), R("BD"), float(r), Op.is_equal, 1024.0, Op.mult)
+    ts(blk("CF", 0), R("IH"), PM8, Op.add)
+    local("S", row("TF", HI, 0, P), blk("CF", 0))
+    weights(WY, CX, (HI, 16.0), (LO, 1.0))
+    weights(WN, CX, (NH, 16.0), (NL, 1.0))
     cp(R("K0"), R("KI"))
+    ts(CY, WY, 1.0 / 1024, Op.mult)
+    ts(CN, WN, 1.0 / 1024, Op.mult)
+    ts(R("CW", 0, 128), R("NXC"), 4, Op.logical_shift_right)
+    ts(R("CW", 128, 256), R("NXC"), 15, Op.bitwise_and)
+    ts(R("BMw", 0, 12), R("BMC"), 4, Op.logical_shift_right)
+    ts(R("BMw", 12, 24), R("BMC"), 15, Op.bitwise_and)
+    cp(R("CF", 256, 512), R("CW"))
+    cp(R("BMf"), R("BMw"))
+    local("S", row("TF", NH, 0, P), blk("CF", 2))
+    local("S", row("TF", NL, 0, P), blk("CF", 3))
+    for f in (HI, LO):
+        local("S", row("BMR", f, 0, L), blk("BMf", f, 12))
     for k in range(16):
         cp(R("HX", k, NX * 16, 16), R("H0", 0, NX))
-    ts(R("THw", 0, 2, 1, e8), R("TH", 0, 2, 1, e8), 4032, Op.bitwise_and)
-    ts(R("THw", 2, 4, 1, e8), R("TH", 0, 2, 1, e8), 63, Op.bitwise_and)
-    cp(R("THf", 0, 4, 1, e8), R("THw", 0, 4, 1, e8))
-    for j in range(2):
-        mm(R("p7", 200, 202), R("TSR", p=e8), R("THf", 2 * j, 2 * j + 2, 1, e8), j == 0, j == 1)
-    for s in range(2):
-        for j in range(2):
-            mm(R("p7", 202 + s, 203 + s), R("TS%d" % s, p=e8), R("THf", 2 * j, 2 * j + 1, 1, e8), j == 0, j == 1)
     ts(R("KBM"), R("ID"), K64, Op.mult)
     ts(R("NI"), R("ID"), -1.0, Op.mult)
+    iota(R("I12"), [[32, 6], [0, 2]], 0, 0)
+    asel(R("TSx", p=e8), R("ONES", p=e8), [[1, 128]], Op.is_ge, 0.0, 0, -16)
+    asel(R("TSR", p=e8), R("TSx", p=e8), [[-1, 128]], Op.is_ge, 0.0, 15, 16)
+    asel(R("TS0", p=e8), R("ONES", p=e8), [[-2, 4], [0, 32]], Op.is_equal, 0.0, 0, 1)
+    asel(R("TS1", p=e8), R("ONES", p=e8), [[-2, 4], [0, 32]], Op.is_equal, 0.0, -1, 1)
+    asel(R("SP"), R("ONES"), [[-1, 128]], Op.is_equal, 0.0, 16, 1)
+    asel(R("SM"), R("ONES"), [[-1, 128]], Op.is_equal, 0.0, -16, 1)
+    iota(R("RS0"), [[0, L]], 2 ** 24 - 1, 0)
+    asel(R("RST"), R("RS0"), [[0, 12], [1, 16]], Op.is_equal, -BIG, 0, 0)
+    iota(R("IQ"), [[1, 128]], 0, 0)
+    asel(R("N3a"), R("ONES"), [[-32, 4], [0, 32]], Op.is_ge, 0.0, 0, 1)
+    asel(R("N3b"), R("N3a"), [[32, 4], [0, 32]], Op.is_ge, 0.0, 31, -1)
+    for r in range(16):
+        gcopy(blk("XV", r), R("TX", r, P, 16), 128)
+    local("S", R("BB"), R("TF", 0, P))
+    local("S", R("VL"), row("XV", 0, 0, P))
 
-    def more_constants():
-        ts(R("BO"), R("BD"), 0.0, Op.is_ge)
-        cp(P32, R("IW", 1, 2))
-        ts(R("RC"), R("R16"), PM, Op.is_equal, VOID, Op.mult)
-        ts(R("WYR"), R("BO"), WY, Op.mult)
+    def constants_for_keys():
+        ts(R("SY"), R("SU"), CY, Op.mult)
+        ts(R("THw", 0, 2, 1, e8), R("TH", 0, 2, 1, e8), 4032, Op.bitwise_and)
+        ts(R("THw", 2, 4, 1, e8), R("TH", 0, 2, 1, e8), 63, Op.bitwise_and)
         ts(R("IV"), R("I12"), P32, Op.add)
-        act_scale(R("SQ"), R("SU"), col("CT", 10))
-        for r in range(16):
-            act_scale(R("MT", 128 * r, 128 * r + 128), R("BO"), col("RC", r))
-        lists(R("p2", 0), "SN", "TF", 128)
-        act(R("NL"), R("p2", 0, 128))
-        fill(R("TF", VO, TW), 0.0)
-        iota(R("RS0"), [[0, 2 * L]], 2 ** 24 - 1, 0)
-        asel(R("RST"), R("RS0"), [[0, 24], [1, 16]], Op.is_equal, -BIG, 0, 0)
-        fill(R("TX", VO, TW), 1024.0)
-        fill(R("BMR"), 0.0)
-        ts(R("BMw", 0, 12), R("BMC"), 4, Op.logical_shift_right)
-        ts(R("BMw", 12, 24), R("BMC"), 15, Op.bitwise_and)
-        ts(R("IX", 0, 12), R("IV"), 63, Op.bitwise_and)
-        ts(R("IX", 12, 24), R("IV"), 6, Op.logical_shift_right)
-        ts(W140, PM, 2.0, Op.is_equal, float(VO // 16), Op.mult)
-        cp(R("BMf"), R("BMw"))
-        for f in range(2):
-            src, dst = R("BMf", 12 * f, 12 * f + 12), R("BMR", 0, L, 1, slice(f, 128, 16))
-            dma("S", ap(dst), ap(src), [src], [dst])
         ts(RM1, R("IW", 1, 2), 16.0, Op.is_ge)
         ts(RM0, R("IW", 1, 2), 16.0, Op.is_lt)
-        ts(R("TF", HS, VO), R("ON2"), W140, Op.mult)
+        cp(R("THf", 0, 4, 1, e8), R("THw", 0, 4, 1, e8))
+        lists("p6", 0, "SY", "BMR", 0, 12)
+        ts(R("IX", 0, 12), R("IV"), 63, Op.bitwise_and)
+        ts(R("IX", 12, 24), R("IV"), 6, Op.logical_shift_right)
+        ts(NOT1, col("EQ", ONE), -1.0, Op.mult, 1.0, Op.add)
+        ts(R("BO"), R("BD"), 0.0, Op.is_ge)
+        mm(R("p5", 0, 4), R("TSR", p=e8), R("THf", 0, 4, 1, e8))
+        for s in range(2):
+            for j in range(2):
+                mm(R("p5", 4 + s, 5 + s), R("TS%d" % s, p=e8), R("THf", 2 * j, 2 * j + 1, 1, e8), j == 0, j == 1)
         ts(R("CV", 0, 12), R("IX", 0, 12), 64.0, Op.add)
         ts(R("CV", 12, 24), R("IX", 12, 24), float(HS // 64 - 1), Op.add)
+        cp(R("BU"), R("p6", 0, 12))
         for w, wt in enumerate((1.0, 64.0)):
             for u in range(2):
                 for s in range(2):
                     m = "ID" if u == s else ("SP" if s else "SM")
-                    j = 4 * w + 2 * u + s
-                    ts(R("PP", 128 * j, 128 * j + 128), R(m), RM1 if u else RM0, Op.mult, wt, Op.mult)
-        cp(R("T2"), R("p7", 200, 202))
-        ts(R("T1K"), R("p7", 202, 204), 1024.0, Op.mult)
-        ts(R("THR"), R("p7", 202, 204), 1024.0, Op.mult)
-        for r in range(16):
-            asel(R("SY", 128 * r, 128 * r + 128), R("WYR"), [[0, 8], [1, 16]], Op.is_equal, 0.0, -r, 0)
-        dma("S", ap(R("BB")), ap(R("TF", 0, P)), [R("TF", 0, P)], [R("BB")])
+                    ts(blk("PP", 4 * w + 2 * u + s), R(m), RM1 if u else RM0, Op.mult, wt, Op.mult)
+        ts(R("T1K"), R("p5", 4, 6), 1024.0, Op.mult)
+        ts(R("THR"), R("p5", 4, 6), 1024.0, Op.mult)
+        ts(CV1, col("EQ", C2), R("p5", 1, 2), Op.mult)
+        ts(CV2, col("EQ", C3), R("p5", 3, 4), Op.mult)
+        act_scale(R("SN"), R("SU"), CN)
+        agather(R("TF", HS, VO), R("TF", 0, P), R("BU"), NOT1)
+        lists("p7", 0, "SY", "TF", 0, 128, True, False)
 
-    def late_constants():
-        ts(R("JL", 0, 64), R("IL", 0, 64), PM, Op.add)
-        ts(R("JL", 64, 128), R("IL", 64, 128), PM, Op.add)
+    def constants_for_marks():
+        weights(CG, CX, (ONE, GATE), (C1, -GATE))
+        weights(CMc, CX, (ONE, GATE), (C1, -GATE), (L2, -GATE), (C2, 0.5))
+        weights(CD, CX, (NH, 16.0), (NL, 1.0), (HI, -16.0), (LO, -1.0), (C1, float(P)))
+        ts(CG, CG, CV1, Op.add, CV2, Op.add)
+        ts(CMa, col("EQ", LO), 2 * GATE, Op.mult)
+        ts(CMb, col("EQ", C1), -GATE, Op.mult)
+        ts(R("WD"), R("BO", 0, 128, 16), CD, Op.mult)
+        ts(R("WG"), R("BO"), CG, Op.mult)
+        ts(blk("WT", 0), R("BD"), 0.0, Op.max, CMa, Op.mult)
+        ts(blk("WT", 1), blk("CF", 1), CMb, Op.mult, CMc, Op.add)
+        ts(R("NBO"), R("BO"), -1.0, Op.mult)
+        for r in range(16):
+            mm(R("p4", 128 + r, 256, 16), R("TF", r, P, 16), R("WD"))
+        tt(blk("WT", 2), blk("WT", 1), R("BO"), Op.mult)
+        for nm, w in (("I16", 16.0), ("IM", -float(P)), ("IVD", VOID)):
+            ts(R(nm), R("ID"), w, Op.mult)
+        tt(R("WM"), blk("WT", 0), blk("WT", 2), Op.add)
+        cp(R("DI"), R("p4", 128, 256))
+        weights(WF, CX, (HI, 1.0 / 1024), (LO, 128.0 / 1024))
+        ts(R("DH"), R("DI"), 4, Op.logical_shift_right)
+        ts(R("DL"), R("DI"), 15, Op.bitwise_and)
         ts(R("N32"), R("N3b"), -1.0, Op.mult)
         ts(R("WNR"), R("BO"), WN, Op.mult)
 
-    def bookmarks():
-        agather(R("FB"), R("TF", 0, P), R("BU"))
-        bookmark_fields()
+    def preload(t):
+        mm(R("p0", 0, L), R("KBM"), R("ON2"), True, False)
+        for k in range(16):
+            mm(R("p%d" % (1 + k // 8), (k % 8) * CB, (k % 8) * CB + CB), R("NI"), R("H%d" % t, NX, L), k % 8 == 0, False)
 
-    def bookmark_fields():
-        lists(R("p6", 100), "SY", "FB", 12)
-        lists(R("p6", 112), "SN", "FB", 12)
-
-    def bookmark_lists():
-        act(R("JB", 0, 12), R("p6", 100, 112))
-        act_lin(R("JB", 12, 24), R("p6", 112, 124), 1.0, -float(VO))
-
+    preload(0)
     for t in range(NV):
         last = t == NV - 1
         H, K = "H%d" % t, "K%d" % t
-        if t:
-            cp(R("KI"), R(K))
         agather(R("GB"), R("TX", 0, P), R(K, NX, L))
-        nc = len(CHUNKS) - 1
-        for c in range(nc):
-            a, b = CHUNKS[c], CHUNKS[c + 1]
+        for a, b in ((0, 64), (64, 128)):
             ttgather(R("DX", 16 * a, 16 * b), R("TX", 0, P), R(K, a, b), R("HX", 16 * a, 16 * b), Op.subtract)
 
-        def sums(i0, i1, *srcs):
-            o = R("p0", i0, i1)
-            mm(o, R("KBM"), R("ON2", 0, i1 - i0), True, False)
-            for src in srcs:
-                for k in range(16):
-                    mm(o, R("SU", 128 * k, 128 * k + 128), src(k), False, k == 15 and src is srcs[-1])
-
-        def sums_c(c):
-            a, b = CHUNKS[c], CHUNKS[c + 1]
-            if c == nc - 1:
-                if t:
-                    cp(R("AI"), R("p6", 200, 202))
-                ts(R("AX", 16 * a, 16 * b), R("DX", 16 * a, 16 * b), -2.0, Op.mult, 0.0, Op.max)
-                sums(a, b, lambda k: R("DX", 16 * a + k, 16 * b, 16), lambda k: R("AX", 16 * a + k, 16 * b, 16))
-            else:
-                act(R("AX", 16 * a, 16 * b), R("DX", 16 * a, 16 * b), Act.Abs)
-                sums(a, b, lambda k: R("AX", 16 * a + k, 16 * b, 16))
+        def sums(i0, i1, src, ks, stop=False):
+            for k in ks:
+                mm(R("p0", i0, i1), blk("SU", k), src(k), False, stop and k == ks[-1])
 
         for k in range(16):
-            o = R("p%d" % (1 + k // 8), (k % 8) * CB, (k % 8) * CB + CB)
-            mm(o, R("ID"), R("GB", k, 16 * CB, 16), True, False)
-            mm(o, R("NI"), R(H, NX, L), False, True)
-        sums_c(0)
+            mm(R("p%d" % (1 + k // 8), (k % 8) * CB, (k % 8) * CB + CB), R("ID"), R("GB", k, 16 * CB, 16), False, k % 8 == 7)
+        act(R("AX", 0, 1024), R("DX", 0, 1024), Act.Abs)
         for j in range(2):
-            act(R("AB", 8 * CB * j, 8 * CB * j + 8 * CB), R("p%d" % (1 + j), 0, 8 * CB), Act.Abs)
-        for c in range(nc - 1, 0, -1):
-            sums_c(c)
-        sums(NX, L, lambda k: R("AB", CB * k, CB * k + CB))
+            act(blk("AB", j, 8 * CB), R("p%d" % (1 + j), 0, 8 * CB), Act.Abs)
+        if t:
+            cp(R("KI"), R(K))
+        ts(R("AX", 1024, 2048), R("DX", 1024, 2048), -2.0, Op.mult, 0.0, Op.max)
+        sums(0, 64, lambda k: R("AX", k, 1024, 16), range(16))
+        sums(64, 128, lambda k: R("DX", 1024 + k, 2048, 16), range(16))
+        sums(NX, L, lambda k: blk("AB", k, CB), range(8))
+        sums(64, 128, lambda k: R("AX", 1024 + k, 2048, 16), range(16))
+        sums(NX, L, lambda k: blk("AB", k, CB), range(8, 16), True)
         act(R("TX", HS, VO), R(H))
+        if t:
+            cp(R("AI"), R("p6", 200, 202))
         ts(R("KA", 0, L), R("KI"), 63, Op.bitwise_and)
         if t:
             ts(R("AJ"), R("AI"), 31, Op.bitwise_and)
@@ -416,203 +416,141 @@ def rank_program(g, core, T, topo):
         if t:
             ts(R("AK"), R("AJ"), 1024.0, Op.mult)
             tt(R("THR"), R("AK"), R("T1K"), Op.add)
-            bookmarks()
-            act(R("JL", SPLIT[2], 128), R("p7", SPLIT[2], 128))
-            act(R("JL", 0, SPLIT[2]), R("p5", 0, SPLIT[2]))
-            bookmark_lists()
+            lists("p7", 0, "SY", "TF", 0, 128, True, False)
         else:
-            more_constants()
-        def half(name, w):
-            return R(name, L * w, L * w + L)
-
-        def twelve(name, w):
-            return R(name, 12 * w, 12 * w + 12)
-
+            constants_for_keys()
         for w in range(2):
-            tt(half("KAB", w), R("p0", 0, L), half("KA", w), Op.add)
+            tt(blk("KAB", w, L), R("p0", 0, L), blk("KA", w, L), Op.add)
         for w in range(2):
-            op("V", lambda e: e.transpose(ap(half("VT", w)), ap(half("KAB", w))), [half("KAB", w)], [half("VT", w)])
+            op("V", lambda e: e.transpose(ap(blk("VT", w, L)), ap(blk("KAB", w, L))), [blk("KAB", w, L)], [blk("VT", w, L)])
         for w in range(2):
-            op("V", lambda e: e.tensor_tensor_scan(ap(half("MS", w)), ap(half("RST", w)), ap(half("VT", w)), BIG, Op.max, Op.min), [half("RST", w), half("VT", w)], [half("MS", w)])
-        cp(twelve("MI", 0), R("MS", 15, L, 16))
+            op("V", lambda e: e.tensor_tensor_scan(ap(blk("MS", w, L)), ap(R("RST")), ap(blk("VT", w, L)), BIG, Op.max, Op.min), [R("RST"), blk("VT", w, L)], [blk("MS", w, L)])
+        cp(blk("MI", 0, 12), R("MS", 15, L, 16))
         for s in range(2):
             ts(R("MV", s, 12, 2), R("MS", 15 + 16 * s, L, 32), col("THR", s), Op.is_ge)
-        cp(twelve("MI", 1), R("MS", L + 15, 2 * L, 16))
-        ts(twelve("ML", 0), twelve("MI", 0), 63, Op.bitwise_and)
+        cp(blk("MI", 1, 12), R("MS", L + 15, 2 * L, 16))
+        ts(blk("ML", 0, 12), blk("MI", 0, 12), 63, Op.bitwise_and)
         for w in range(2):
-            tt(twelve("SEL", w), R("MV"), twelve("CV", w), Op.mult)
-        ts(twelve("ML", 1), twelve("MI", 1), 63, Op.bitwise_and)
+            tt(blk("SEL", w, 12), R("MV"), blk("CV", w, 12), Op.mult)
+        ts(blk("ML", 1, 12), blk("MI", 1, 12), 63, Op.bitwise_and)
         for w in range(2):
-            tt(twelve("LB", w), twelve("ML", w), twelve("SEL", w), Op.max)
+            tt(blk("LB", w, 12), blk("ML", w, 12), blk("SEL", w, 12), Op.max)
         for u in range(2):
             for w in range(2):
                 for s in range(2):
-                    j = 4 * w + 2 * u + s
-                    mm(R("p3", u, 12, 2), R("PP", 128 * j, 128 * j + 128), R("LB", 12 * w + s, 12 * w + 12, 2), w == 0 and s == 0, w == 1 and s == 1)
+                    mm(R("p3", u, 12, 2), blk("PP", 4 * w + 2 * u + s), R("LB", 12 * w + s, 12 * w + 12, 2), w == 0 and s == 0, w == 1 and s == 1)
+        if t == 0:
+            constants_for_marks()
         cp(R("L1"), R("p3", 0, 12))
 
-        def missed():
-            tt(R("YM", 0, 12), R("JB", 0, 12), R("MISS"), Op.mult)
-            tt(R("YM", 12, 24), R("JB", 12, 24), R("MISS"), Op.mult)
-
-        ttgather(R("SI"), R("TX", 0, VO), R("L1"), R(H), Op.add)
-        agather(R("FY"), R("TF", 0, VO), R("L1"))
-        ts(R("MISS"), R("p3", 0, 12), float(HS), Op.is_ge)
+        ttgather(R("SI"), R("TX"), R("L1"), R(H), Op.add)
+        agather(R("FY"), R("TF"), R("L1"))
         ts(R("Q1"), R("SI"), 1, Op.arith_shift_right)
-        if t and not last:
-            missed()
-        lists(R("p3", 16), "SN", "FY", 12)
-        if t == 0:
-            late_constants()
-        tt(DJ, R("NL"), R("JL"), Op.subtract)
+        lists("p3", 16, "SN", "FY", 0, 12)
+        up = slice(64, 128)
+        WQ = R("ID", HI, 128, 16)
+        mm(R("p4", 0, 8), blk("FF", 0), WQ)
+        mm(R("p1", 0, 128), blk("FF", 0), R("WM"))
+        mm(R("p2", 128, 256), R("FY", 64, L), R("WG"), True, False)
+        mm(R("p2", 0, 128, 1, up), R("FY", 0, 64), R("WG"), False, False)
+        mm(R("p2", 0, 128, 1, slice(0, 64)), R("FY", 128, L), R("WG"), False, False)
+        mm(R("p6", 0, L), R("WG"), R("FY"), True, False)
         cp(R("M1"), R("p3", 16, 28))
-        ttgather(R("E2"), R("TX"), R("M1"), R("Q1"), Op.subtract)
-        agather(R("FN"), R("TF"), R("M1"))
-        act(R("AE"), R("E2"), Act.Abs)
-        def one_hot(j):
-            if j < 12:
-                ts(R("OR", 128 * j, 128 * j + 128), R("BD"), col("QR", 24 + j), Op.is_equal)
-            else:
-                ts(R("OR", 128 * j, 128 * j + 128), R("BD"), col("QR", 24 + j), Op.is_equal, col("BRL", j - 12), Op.mult)
+        act(blk("MM", 0), R("p1", 0, 128), Act.Relu, scale=1024.0)
+        ttgather(R("E2"), R("TX", 0, P), R("M1"), R("Q1"), Op.subtract)
+        agather(R("FN"), R("TF", 0, P), R("M1"))
 
-        def steps(j):
-            if j < 24 - NQ:
-                act_bias(R("OQ", QW * j, QW * j + 129), R("IQ"), Act.Sign, col("QR", j))
-            else:
-                ts(R("OQ", QW * j, QW * j + 129), R("IQ"), col("QR", j), Op.add, 0.0, Op.is_gt)
+        def one_hot(c, gs):
+            for gg in gs:
+                ts(blk("NN", 8 * c + gg), R("IQ"), col("p4" if c == 0 else "p5", 8 * c + gg), Op.is_equal)
 
-        def products(j0, j1):
-            for j in range(j0, j1):
-                mm(R("p0", 0, 129), R("OR", 128 * j, 128 * j + 128), R("OQ", QW * j, QW * j + 129), j == 0, j == 23)
+        def products(c):
+            for gg in range(8):
+                mm(R("p0", 16 * gg, 16 * gg + 16), blk("NN", 8 * c + gg), R("MM", 128 * c + 16 * gg, 128 * c + 16 * gg + 16), c == 0 and gg == 0, c == 2 and gg == 7)
 
-        lists(R("p6", 140), "SR", "FY", 12)
-        lists(R("p4", 0), "SQ", "FY", 12)
-        mm(R("p5", 0, L), R("BO"), R("AE"))
-        cp(R("QR", 24, 36), R("p6", 140, 152))
+        one_hot(0, range(3))
+        ts(R("AE"), R("E2"), -2.0, Op.mult, 0.0, Op.max)
+        for c in (1, 2):
+            mm(R("p5", 8 * c, 8 * c + 8), blk("FF", c), WQ)
+        for c in (1, 2):
+            mm(blk("p2", c - 1), blk("FF", c), R("WM"), False, False)
+        for src in ("E2", "AE"):
+            mm(R("p2", 0, 128, 1, up), R(src, 0, 64), R("NBO"), False, False)
+            mm(R("p2", 128, 256), R(src, 64, L), R("NBO"), False, src == "AE")
+        one_hot(0, range(3, 8))
+        act(R("MM", 128, 384), R("p2", 0, 256), Act.Relu, scale=1024.0)
+        for src in ("E2", "AE"):
+            mm(R("p6", 0, L), R("NBO"), R(src), False, src == "AE")
+        products(0)
+        act(R("BS"), R("p6", 0, L), Act.Sign, bias=0.5)
+        act(R("BR"), R("BS"), Act.Relu)
+        mm(R("p4", 256, 256 + L), R("ID"), R("FN"), True, False)
+        mm(R("p4", 256, 256 + L), R("NI"), R("FY"), False, True)
+        one_hot(1, range(8))
+        one_hot(2, range(8))
+        products(1)
+        products(2)
+        if not last:
+            lists("p3", 32, "SY", "FY", 0, 12, True, False)
         ts(R("F2"), R("E2"), 0.5, Op.mult, -0.25, Op.add)
-        act_lin(R("QR", 0, 12), R("p4", 0, 12), -1.0, 0.5)
-        for j in range(12):
-            steps(j)
-        for j in range(PRE):
-            one_hot(j)
-        ts(R("BR"), R("p5", 0, L), col("T2", 1), Op.is_le)
-        for j in range(PRE, 12):
-            one_hot(j)
-        lists(R("p4", 12), "SQ", "FN", 12)
-        lists(R("p3", 52), "SR", "FN", 12)
-        lists(R("p7", 0), "SU", "BR", 12)
-        if t == 0:
-            lists(R("p6", 0), "SY", "BMR", 12)
-        products(0, 12)
-        mm(R("p1", 0, L), R("ID"), R("FN"), True, False)
-        mm(R("p1", 0, L), R("NI"), R("FY"), False, True)
-        act_lin(R("QR", 12, 24), R("p4", 12, 24), -1.0, 0.5)
-        tt(R("p2", 0, L), R("F2"), R("BR"), Op.mult)
-        cp(R("QR", 36, 48), R("p3", 52, 64))
-        tt(R("HS%d" % t), R("p2", 0, L), R("Q1"), Op.add)
-        cp(R("BRL"), R("p7", 0, 12))
+        tt(R("GF"), R("p4", 256, 256 + L), R("BR"), Op.mult)
+        tt(R("UH"), R("p0", 0, 128), R("DH"), Op.min)
+        ts(R("MK"), R("p0", 0, 128), 0.0, Op.is_gt)
+        tt(R("UL"), R("p0", 0, 128), R("DL"), Op.min)
+        for src, w in (("UH", "I16"), ("MK", "IM"), ("UL", "ID")):
+            mm(R("p7", 0, 128), R(src), R(w), False, src == "UL")
+        tt(R("p5", 256, 256 + L), R("F2"), R("BR"), Op.mult)
         if not last:
-            deps("G", [R("HS%d" % t)], [])
-            g.remote_dma(ap(R("H%d" % (t + 1))), ap(R("HS%d" % t)), T.sem["ha%d" % (t + 1)], T.sem["loc"], pid, rid, mask)
-        else:
+            lists("p3", 32, "SY", "GF", 0, 12, False, True)
+            mm(R("p1", 0, 128), R("MK"), R("IVD"), True, False)
+            mm(R("p1", 0, 128), R("ID"), R("VL"), False, True)
+        cp(R("ZU"), R("p7", 0, 128))
+        tt(R("HS%d" % t), R("p5", 256, 256 + L), R("Q1"), Op.add)
+        if last:
             dma("S", T["yh"][:, :], ap(R("HS%d" % t)), [R("HS%d" % t)], [])
-        if t == 0:
-            cp(R("BU"), R("p6", 0, 12))
-            agather(R("FB"), R("TF", 0, P), R("BU"))
-        for j in range(24 - NQ, 24):
-            steps(j)
-        for j in range(12, 24):
-            if j < 24 - NQ:
-                steps(j)
-            one_hot(j)
-        products(12, 24)
-        tt(R("GF"), R("p1", 0, L), R("BR"), Op.mult)
-        if not last:
-            for k, src in enumerate(("FY", "GF")):
-                for r in range(16):
-                    mm(R("p5", 256, 268), R("SY", 128 * r, 128 * r + 128), R(src, r, L, 16), k == 0 and r == 0, k == 1 and r == 15)
-            if t == 0:
-                bookmark_fields()
-                bookmark_lists()
-            lists(R("p4", 100), "SN", "GF", 12)
-        hs = ((64, 128), (0, 64))
-        for a, b in hs:
-            cp(R("CS", a, b), R("p0", a, b))
-        for a, b in hs:
-            tt(R("MK", a, b), R("p0", a + 1, b + 1), R("CS", a, b), Op.is_gt)
-        for a, b in hs:
-            tt(R("p2", a, b), R("MK", a, b), R("p2", 384 + a, 384 + b), Op.mult)
-        for a, b in hs:
-            tt(R("ZF", a, b), R("p2", a, b), R("JL", a, b), Op.add)
-        for a, b in hs:
-            cp(R("ZU", a, b), R("ZF", a, b))
-        s1, s2, s3 = SPLIT
-        if last:
-            s1 = LAST1
-        agather(R("B1", 16 * s1, P), R("BB"), R("ZU", s1, 128))
-        if not last:
-            if t == 0:
-                vgather(R("B1", 0, 16 * s1), R("BB"), R("ZU", 0, s1))
-                missed()
-            tt(R("YF"), R("p5", 256, 268), R("YM", 0, 12), Op.add)
-            tt(R("BN"), R("p3", 16, 28), R("YM", 12, 24), Op.add)
-            cp(R("YU"), R("YF"))
-            vgather(R("KS%d" % t), R("PL"), R("YU"))
-            deps("G", [R("KS%d" % t)], [])
-            g.remote_dma(ap(R("K%d" % (t + 1))), ap(R("KS%d" % t)), T.sem["ka%d" % (t + 1)], T.sem["loc"], pid, rid, mask)
-            tt(R("BF"), R("p4", 100, 112), R("BN"), Op.add)
-        if t:
-            vgather(R("B1", 0, 16 * s1), R("BB"), R("ZU", 0, s1))
-        if last:
-            mm(R("p5", 0, L), R("WNR"), R("FY"), True, False)
-            mm(R("p5", 0, L), R("WNR"), R("GF"), False, True)
-            mm(R("p6", 0, L), R("WNR"), R("FB"))
-            cp(R("RB", 0, L), R("p5", 0, L))
-            tt(R("RB", L, 2 * L), R("p6", 0, L), R("RB", 0, L), Op.subtract)
-            ts(R("RB", 2 * L, 3 * L), R("RB", 0, L), float(P), Op.is_ge)
-        vgather(R("TF", 0, 16 * s2), R("B1"), R("ZU", 0, s2))
-        agather(R("TF", 16 * s2, P), R("B1"), R("ZU", s2, 128))
-        if last:
-            tt(R("RB", 3 * L, 4 * L), R("RB", L, 2 * L), R("RB", 2 * L, 3 * L), Op.mult)
-            tt(R("RB", L, 2 * L), R("RB", 3 * L, 4 * L), R("RB", 0, L), Op.add)
-            src = R("RB", L, 2 * L, 1, slice(0, 128, 16))
-            dma("S", T["yb"][:, :], ap(src), [src], [])
-            for j in range(4):
-                mm(R("p%d" % (1 + j), 0, 512), R("WYR"), R("TF", 512 * j, 512 * j + 512))
-                if j % 2:
-                    act(R("ROW", 512 * j, 512 * j + 512), R("p%d" % (1 + j)))
-                else:
-                    cp(R("ROW", 512 * j, 512 * j + 512), R("p%d" % (1 + j)))
-            src = R("ROW", 0, P, 1, slice(0, 128, 16))
-            dma("S", T["yj"][:, :], ap(src), [src], [])
+            mm(R("p6", 0, L), R("WNR"), R("FY"), True, False)
+            mm(R("p6", 0, L), R("WNR"), R("GF"), False, True)
+            s1, s2 = LAST
+            agather(R("BF1", 16 * s1, P), R("IOT"), R("ZU", s1, 128))
+            vgather(R("BF1", 0, 16 * s1), R("IOT"), R("ZU", 0, s1))
+            cp(R("RB"), R("p6", 0, L))
+            dma("S", T["yb"][:, :], ap(row("RB", 0, 0, L)), [R("RB")], [])
+            agather(R("ROW", 16 * s2, P), R("BF1"), R("ZU", s2, 128))
+            vgather(R("ROW", 0, 16 * s2), R("BF1"), R("ZU", 0, s2))
+            dma("S", T["yj"][:, :], ap(row("ROW", 0, 0, P)), [R("ROW")], [])
             break
-        for j in range(4):
-            b = "p%d" % (1 + j)
-            if j >= 2:
-                mm(R(b), R("ID"), R("XV", 512 * j, 512 * j + 512), True, False)
-            for r in range(16):
-                mm(R(b, r, 512, 16), R("MT", 128 * r, 128 * r + 128), R("MK", 32 * j, 32 * j + 32), j < 2, j < 2 or r == 15)
-        for b, q0, q1 in (("p5", 0, s3), ("p7", s3, 128)):
-            for r in range(16):
-                mm(R(b, q0, q1), R("SY", 128 * r, 128 * r + 128), R("TF", 16 * q0 + r, 16 * q1, 16), r == 0, r == 15)
-        for j in (2, 3):
-            act(R("XV", 512 * j, 512 * j + 512), R("p%d" % (1 + j)))
-        tt(R("XV", 0, 512), R("XV", 0, 512), R("p1"), Op.add)
-        tt(R("XV", 512, 1024), R("XV", 512, 1024), R("p2"), Op.add)
-        h1 = "H%d" % (t + 1)
-        cnt = len(topo.engines(prv, core))
-        arrive(h1, "ha%d" % (t + 1), cnt)
-        arrive("K%d" % (t + 1), "ka%d" % (t + 1), cnt)
-        for k in range(GK):
-            asel(R("HX", k, NX * 16, 16), R(h1, 0, NX), [[0, NX]], Op.is_ge, 0.0, 1, 0)
-        for k in range(GK, 16):
-            cp(R("HX", k, NX * 16, 16), R(h1, 0, NX))
-        cp(R("JU", 0, s3), R("p5", 0, s3))
-        cp(R("BU"), R("BF"))
-        cp(R("JU", s3, 128), R("p7", s3, 128))
-        vgather(R("TX", 0, 16 * s3), R("XV"), R("JU", 0, s3))
-        agather(R("TX", 16 * s3, P), R("XV"), R("JU", s3, 128))
+        send(t, "H", "ha")
+        act(R("VL"), R("p1", 0, 128))
+        local("S", row("XV", 0, 0, P), R("VL"))
+        s1, s2, s3 = SPLIT
+        agather(R("B1", 16 * s1, P), R("BB"), R("ZU", s1, 128))
+        cp(R("YU"), R("p3", 32, 44))
+        lists("p4", 0, "SN", "FY", 0, 12, True, False)
+        lists("p4", 0, "SN", "GF", 0, 12, False, True)
         for b in range(6):
             mm(R("p6", 200, 202), R("N32"), R("MV", 2 * b, 2 * b + 2), b == 0, b == 5)
+        if t == 0:
+            ts(R("SF"), R("SU"), WF, Op.mult)
+        vgather(R("KS%d" % t), R("PL"), R("YU"))
+        send(t, "K", "ka")
+        vgather(R("B1", 0, 16 * s1), R("BB"), R("ZU", 0, s1))
+        cp(R("BU"), R("p4", 0, 12))
+        vgather(R("TF", 0, 16 * s2), R("B1"), R("ZU", 0, s2))
+        agather(R("TF", 16 * s2, P), R("B1"), R("ZU", s2, 128))
+        lists("p5", 0, "SF", "TF", 0, s3)
+        lists("p3", 0, "SF", "TF", s3, 128)
+        h1 = "H%d" % (t + 1)
+        for k in range(GK):
+            gcopy(R("HX", k, NX * 16, 16), R(h1, 0, NX), NX)
+        for k in range(GK, 16):
+            cp(R("HX", k, NX * 16, 16), R(h1, 0, NX))
+        agather(R("TF", HS, VO), R("TF", 0, P), R("BU"), NOT1)
+        cp(R("JU", 0, s3), R("p5", 0, s3))
+        cp(R("JU", s3, 128), R("p3", 0, 128 - s3))
+        preload(t + 1)
+        vgather(R("TX", 0, 16 * s3), R("XV"), R("JU", 0, s3))
+        agather(R("TX", 16 * s3, P), R("XV"), R("JU", s3, 128))
+        if t == 1:
+            iota(R("IOT"), [[1, P]], 0, 0)
     finish()
     g.wait_ge(T.sem["loc"], 2 * (NV - 1) * len(topo.engines(core, nxt)))

@@ -1,16 +1,17 @@
 from concourse.mybir import AluOpType as Op, ActivationFunctionType as Act
 
 BIG = 1.0e9
-VOID = 8192.0
+VOID = 128.0
 GATE = 8192.0
 L, P, NV = 192, 2048, 5
 HS = P
 VO = P + L
 NX = 128
 CB = L - NX
-SPLIT = (56, 62, 62)
+SPLIT = (56, 64, 64)
 LAST = (60, 64)
 GK = 5
+AK0 = 8
 HI, LO, NH, NL, ONE, L2, C1, C2, C3 = range(9)
 
 B16, F32, I32, U16 = "bfloat16", "float32", "int32", "uint16"
@@ -27,20 +28,21 @@ SCRATCH = {
     "IV": ("sbuf", [128, 12], I32), "IX": ("sbuf", [128, 24], I32),
     "SI": ("sbuf", [128, L], I32), "Q1": ("sbuf", [128, L], I32), "FF": ("sbuf", [128, 2 * L], B16), "GF": ("sbuf", [128, L], B16),
     "M1": ("sbuf", [128, 12], U16), "E2": ("sbuf", [128, L], B16), "AE": ("sbuf", [128, L], B16), "F2": ("sbuf", [128, L], I32),
-    "BS": ("sbuf", [128, L], B16), "BR": ("sbuf", [128, L], B16), "YU": ("sbuf", [128, 12], U16), "BU": ("sbuf", [128, 12], U16),
+    "BR": ("sbuf", [128, L], B16), "YU": ("sbuf", [128, 12], U16), "BU": ("sbuf", [128, 12], U16),
     "MM": ("sbuf", [128, 3 * 128], B16), "NN": ("sbuf", [128, 24 * 128], B16),
     "MK": ("sbuf", [128, 128], B16), "UH": ("sbuf", [128, 128], B16), "UL": ("sbuf", [128, 128], B16), "VL": ("sbuf", [128, 128], B16),
     "DI": ("sbuf", [128, 128], I32), "DH": ("sbuf", [128, 128], I32), "DL": ("sbuf", [128, 128], I32),
+    "DN": ("sbuf", [128, 128], I32), "DJ": ("sbuf", [128, 128], F32), "BS": ("sbuf", [128, L], B16),
     "ZU": ("sbuf", [128, 128], U16), "JU": ("sbuf", [128, 128], U16),
     "AI": ("sbuf", [128, 2], I32), "AJ": ("sbuf", [128, 2], I32), "AK": ("sbuf", [128, 2], F32), "THR": ("sbuf", [128, 2], F32),
     "T1K": ("sbuf", [128, 2], F32),
-    "BD": ("sbuf", [128, 128], B16), "ONES": ("sbuf", [128, 128], B16), "ON2": ("sbuf", [128, L], B16),
-    "ID": ("sbuf", [128, 128], B16), "NI": ("sbuf", [128, 128], B16), "SP": ("sbuf", [128, 128], B16), "SM": ("sbuf", [128, 128], B16),
+    "BD": ("sbuf", [128, 128], B16), "ONES": ("sbuf", [128, 512], B16),
+    "IDP": ("sbuf", [128, 160], B16), "NI": ("sbuf", [128, 128], B16),
     "N32": ("sbuf", [128, 128], B16), "KBM": ("sbuf", [128, 128], B16), "BO": ("sbuf", [128, 128], B16), "NBO": ("sbuf", [128, 128], B16),
     "IDW": ("sbuf", [128, 3 * 128], B16), "WNR": ("sbuf", [128, 128], B16), "IQ": ("sbuf", [128, 128], B16),
-    "WM": ("sbuf", [128, 128], B16), "WG": ("sbuf", [128, 128], B16), "WD": ("sbuf", [128, 8], B16), "WT": ("sbuf", [128, 4 * 128], B16),
-    "SU": ("sbuf", [128, 2048], B16), "SY": ("sbuf", [128, 2048], B16), "SN": ("sbuf", [128, 2048], B16), "SF": ("sbuf", [128, 2048], B16),
-    "PP": ("sbuf", [128, 8 * 128], B16), "CO": ("sbuf", [128, 32], F32), "EQ": ("sbuf", [128, 16], F32), "R16": ("sbuf", [128, 16], F32),
+    "WM": ("sbuf", [128, 128], B16), "WG": ("sbuf", [128, 128], B16), "WD": ("sbuf", [128, 8], B16), "WT": ("sbuf", [128, 3 * 128], B16),
+    "SU": ("sbuf", [128, 144], B16), "SY": ("sbuf", [128, 144], B16), "SN": ("sbuf", [128, 144], B16), "SF": ("sbuf", [128, 144], B16),
+    "PP": ("sbuf", [128, 4 * 160], B16), "CO": ("sbuf", [128, 32], F32), "EQ": ("sbuf", [128, 16], F32),
     "IP": ("sbuf", [128, 2], I32), "IW": ("sbuf", [128, 2], I32), "I12": ("sbuf", [128, 12], I32),
     "CF": ("sbuf", [128, 4 * 128], B16), "CW": ("sbuf", [128, 2 * 128], I32), "NXC": ("sbuf", [128, 128], I32),
     "BMC": ("sbuf", [128, 12], I32), "BMw": ("sbuf", [128, 24], I32), "BMf": ("sbuf", [128, 24], B16), "BMR": ("sbuf", [128, L], B16),
@@ -49,7 +51,7 @@ SCRATCH = {
     "TMP": ("sbuf", [128, 5 * 128], B16),
     "HH": ("sbuf", [128, 2 * NV * L], B16), "KK": ("sbuf", [128, 2 * NV * L], U16),
 }
-ALIAS = {"FY": ("FF", 0, L), "FN": ("FF", L, L)}
+ALIAS = {"FY": ("FF", 0, L), "FN": ("FF", L, L), "ID": ("IDP", 16, 128), "ON2": ("ONES", 0, L)}
 for _t in range(NV):
     ALIAS["H%d" % _t] = ("HH", L * _t, L)
     ALIAS["HS%d" % _t] = ("HH", L * (NV + _t), L)
@@ -197,6 +199,12 @@ def rank_program(g, core, T, topo):
     def fill(out, c):
         op("V", lambda e: e.memset(ap(out), c), [], [out])
 
+    def turn(out, a):
+        op("V", lambda e: e.transpose(ap(out), ap(a)), [a], [out])
+
+    def scan(out, a, b, init, o0, o1):
+        op("V", lambda e: e.tensor_tensor_scan(ap(out), ap(a), ap(b), init, o0, o1), [a, b], [out])
+
     def act(out, a, f=Act.Copy, bias=0.0, scale=1.0):
         op("A", lambda e: e.activation(ap(out), ap(a), f, bias=bias, scale=scale), [a], [out])
 
@@ -233,7 +241,7 @@ def rank_program(g, core, T, topo):
 
     def lists(bank, c, S, src, q0, q1, start=True, stop=True):
         for r in range(16):
-            mm(R(bank, c, c + q1 - q0), blk(S, r), R(src, 16 * q0 + r, 16 * q1, 16), start and r == 0, stop and r == 15)
+            mm(R(bank, c, c + q1 - q0), R(S, 15 - r, 143 - r), R(src, 16 * q0 + r, 16 * q1, 16), start and r == 0, stop and r == 15)
 
     def send(t, name, sem):
         deps("G", [R("%sS%d" % (name, t))], [])
@@ -247,134 +255,132 @@ def rank_program(g, core, T, topo):
     dma("S", T["NXC"][:, :], T["nx"][:, :], [], [R("NXC")])
     dma("S", T["BMC"][:, :], T["bm"][:, :], [], [R("BMC")])
     dma("C", T["TH"][e8, :], T["th"][:, :], [], [R("TH")])
-    dma("C", T["PL"][:, :], T["pl"][:, :], [], [R("PL")])
 
-    PM, RM1, RM0, WY, WN, K64, P32, WF, PM8, NOT1 = (col("CO", j) for j in range(10))
-    CY, CN, CF_, CMa, CMb, CMc, CG, CD, CX, CZ, CV1, CV2 = (col("CO", j) for j in range(10, 22))
+    PM, RM1, RM0, K64, P32, WF, PM8, NOT1, CY, CN, CMa, CMb, CMc, CG0, CG, CD, CV1, CV2 = (col("CO", j) for j in range(18))
+    later = []
 
-    def weights(out, tmp, *pairs):
-        ts(out, col("EQ", pairs[0][0]), pairs[0][1], Op.mult)
-        for f, w in pairs[1:]:
-            ts(out, col("EQ", f), w, Op.mult, out, Op.add)
+    def gap(k):
+        for _ in range(min(k, len(later))):
+            later.pop(0)()
 
     iota(R("IP"), [[0, 2]], 0, 1)
-    iota(R("R16"), [[1, 16]], 0, 0)
     iota(R("BD0"), [[0, 8], [1, 16]], 0, 0)
     fill(R("ONES"), 1.0)
-    fill(R("TF"), 1.0)
+    for j in range(4):
+        act(blk("TF", j, 512), R("ONES"))
     asel(R("BD1"), R("BD0"), [[-16, 8], [0, 16]], Op.is_ge, -1.0, 0, 1)
-    asel(R("BD"), R("BD1"), [[16, 8], [0, 16]], Op.is_ge, -1.0, 15, -1)
     iota(R("IH"), [[1, 8], [0, 16]], 0, 0)
-    asel(R("ID"), R("ONES"), [[-1, 128]], Op.is_equal, 0.0, 0, 1)
+    asel(R("BD"), R("BD1"), [[16, 8], [0, 16]], Op.is_ge, -1.0, 15, -1)
+    asel(R("IDP"), R("ONES", 0, 160), [[-1, 160]], Op.is_equal, 0.0, 16, 1)
     ts(R("IW", 0, 1), R("IP", 0, 1), 15, Op.bitwise_and)
     ts(R("IW", 1, 2), R("IP", 1, 2), 31, Op.bitwise_and)
-    fill(R("ON2"), 1.0)
+    fill(R("SU", 128, 144), 0.0)
     fill(R("BMR"), 0.0)
+    tt(blk("CF", 1), R("BD0"), R("BD0"), Op.mult)
     cp(PM, R("IW", 0, 1))
     cp(P32, R("IW", 1, 2))
-    tt(blk("CF", 1), R("BD0"), R("BD0"), Op.mult)
-    ts(R("EQ"), R("R16"), PM, Op.is_equal)
-    ts(PM8, PM, 8.0, Op.mult)
-    ts(K64, PM, 64.0, Op.mult)
     local("S", row("TF", LO, 0, P), R("BD0"))
     local("S", row("TF", L2, 0, P), blk("CF", 1))
-    for r in range(16):
-        ts(blk("SU", r), R("BD"), float(r), Op.is_equal, 1024.0, Op.mult)
+    ts(RM1, R("IW", 1, 2), 16.0, Op.is_ge)
+    ts(RM0, R("IW", 1, 2), 16.0, Op.is_lt)
+    ts(R("EQ"), R("BD0", 0, 16), PM, Op.is_equal)
+    ts(PM8, PM, 8.0, Op.mult)
+    ts(K64, PM, 64.0, Op.mult)
+    two = ((CY, HI, 16.0 / 1024, LO, 1.0 / 1024), (CN, NH, 16.0 / 1024, NL, 1.0 / 1024), (WF, HI, 1.0 / 1024, LO, 128.0 / 1024), (CG0, ONE, GATE, C1, -GATE))
+    for c, f, w, f2, w2 in two:
+        ts(c, col("EQ", f), w, Op.mult)
     ts(blk("CF", 0), R("IH"), PM8, Op.add)
+    for c, f, w, f2, w2 in two:
+        ts(c, col("EQ", f2), w2, Op.mult, c, Op.add)
     local("S", row("TF", HI, 0, P), blk("CF", 0))
-    weights(WY, CX, (HI, 16.0), (LO, 1.0))
-    weights(WN, CX, (NH, 16.0), (NL, 1.0))
-    cp(R("K0"), R("KI"))
-    ts(CY, WY, 1.0 / 1024, Op.mult)
-    ts(CN, WN, 1.0 / 1024, Op.mult)
+    ts(NOT1, col("EQ", ONE), -1.0, Op.mult, 1.0, Op.add)
+    ts(CMa, col("EQ", LO), 2 * GATE, Op.mult)
+    ts(CMb, col("EQ", C1), -GATE, Op.mult)
+    ts(CMc, col("EQ", L2), -GATE, Op.mult, CG0, Op.add)
+    ts(CD, CN, CY, Op.subtract, 1024.0, Op.mult)
+    ts(R("SU", 0, 128), R("BD"), 15.0, Op.is_equal, 1024.0, Op.mult)
+    ts(R("BO"), R("BD"), 0.0, Op.is_ge)
     ts(R("CW", 0, 128), R("NXC"), 4, Op.logical_shift_right)
     ts(R("CW", 128, 256), R("NXC"), 15, Op.bitwise_and)
     ts(R("BMw", 0, 12), R("BMC"), 4, Op.logical_shift_right)
     ts(R("BMw", 12, 24), R("BMC"), 15, Op.bitwise_and)
     cp(R("CF", 256, 512), R("CW"))
     cp(R("BMf"), R("BMw"))
+    cp(R("K0"), R("KI"))
     local("S", row("TF", NH, 0, P), blk("CF", 2))
     local("S", row("TF", NL, 0, P), blk("CF", 3))
     for f in (HI, LO):
         local("S", row("BMR", f, 0, L), blk("BMf", f, 12))
+    for S, c in (("SY", CY), ("SN", CN), ("SF", WF)):
+        ts(R(S), R("SU"), c, Op.mult)
+    ts(R("WD"), R("BO", 0, 128, 16), CD, Op.mult)
+    ts(R("THw", 0, 2, 1, e8), R("TH", 0, 2, 1, e8), 4032, Op.bitwise_and)
+    ts(R("THw", 2, 4, 1, e8), R("TH", 0, 2, 1, e8), 63, Op.bitwise_and)
     for k in range(16):
-        cp(R("HX", k, NX * 16, 16), R("H0", 0, NX))
-    ts(R("KBM"), R("ID"), K64, Op.mult)
-    ts(R("NI"), R("ID"), -1.0, Op.mult)
+        if k < AK0:
+            act(R("HX", k, NX * 16, 16), R("H0", 0, NX))
+        else:
+            cp(R("HX", k, NX * 16, 16), R("H0", 0, NX))
+    act_scale(R("KBM"), R("ID"), K64)
+    act(R("NI"), R("ID"), scale=-1.0)
+    asel(R("TSx", p=e8), R("ONES", 0, 128, p=e8), [[1, 128]], Op.is_ge, 0.0, 0, -16)
     iota(R("I12"), [[32, 6], [0, 2]], 0, 0)
-    asel(R("TSx", p=e8), R("ONES", p=e8), [[1, 128]], Op.is_ge, 0.0, 0, -16)
+    cp(R("THf", 0, 4, 1, e8), R("THw", 0, 4, 1, e8))
+    ts(R("IV"), R("I12"), P32, Op.add)
     asel(R("TSR", p=e8), R("TSx", p=e8), [[-1, 128]], Op.is_ge, 0.0, 15, 16)
-    asel(R("TS0", p=e8), R("ONES", p=e8), [[-2, 4], [0, 32]], Op.is_equal, 0.0, 0, 1)
-    asel(R("TS1", p=e8), R("ONES", p=e8), [[-2, 4], [0, 32]], Op.is_equal, 0.0, -1, 1)
-    asel(R("SP"), R("ONES"), [[-1, 128]], Op.is_equal, 0.0, 16, 1)
-    asel(R("SM"), R("ONES"), [[-1, 128]], Op.is_equal, 0.0, -16, 1)
+    asel(R("TS0", p=e8), R("ONES", 0, 128, p=e8), [[-2, 4], [0, 32]], Op.is_equal, 0.0, 0, 1)
+    asel(R("TS1", p=e8), R("ONES", 0, 128, p=e8), [[-2, 4], [0, 32]], Op.is_equal, 0.0, -1, 1)
     iota(R("RS0"), [[0, L]], 2 ** 24 - 1, 0)
-    asel(R("RST"), R("RS0"), [[0, 12], [1, 16]], Op.is_equal, -BIG, 0, 0)
     iota(R("IQ"), [[1, 128]], 0, 0)
-    asel(R("N3a"), R("ONES"), [[-32, 4], [0, 32]], Op.is_ge, 0.0, 0, 1)
-    asel(R("N3b"), R("N3a"), [[32, 4], [0, 32]], Op.is_ge, 0.0, 31, -1)
+    asel(R("RST"), R("RS0"), [[0, 12], [1, 16]], Op.is_equal, -BIG, 0, 0)
     for r in range(16):
         gcopy(blk("XV", r), R("TX", r, P, 16), 128)
+    asel(R("N3a"), R("ONES", 0, 128), [[-32, 4], [0, 32]], Op.is_ge, 0.0, 0, 1)
+    asel(R("N3b"), R("N3a"), [[32, 4], [0, 32]], Op.is_ge, 0.0, 31, -1)
+    dma("S", T["PL"][:, :], T["pl"][:, :], [], [R("PL")])
     local("S", R("BB"), R("TF", 0, P))
     local("S", R("VL"), row("XV", 0, 0, P))
 
-    def constants_for_keys():
-        ts(R("SY"), R("SU"), CY, Op.mult)
-        ts(R("THw", 0, 2, 1, e8), R("TH", 0, 2, 1, e8), 4032, Op.bitwise_and)
-        ts(R("THw", 2, 4, 1, e8), R("TH", 0, 2, 1, e8), 63, Op.bitwise_and)
-        ts(R("IV"), R("I12"), P32, Op.add)
-        ts(RM1, R("IW", 1, 2), 16.0, Op.is_ge)
-        ts(RM0, R("IW", 1, 2), 16.0, Op.is_lt)
-        cp(R("THf", 0, 4, 1, e8), R("THw", 0, 4, 1, e8))
-        lists("p6", 0, "SY", "BMR", 0, 12)
-        ts(R("IX", 0, 12), R("IV"), 63, Op.bitwise_and)
-        ts(R("IX", 12, 24), R("IV"), 6, Op.logical_shift_right)
-        ts(NOT1, col("EQ", ONE), -1.0, Op.mult, 1.0, Op.add)
-        ts(R("BO"), R("BD"), 0.0, Op.is_ge)
+    def constant_sums():
         mm(R("p5", 0, 4), R("TSR", p=e8), R("THf", 0, 4, 1, e8))
         for s in range(2):
             for j in range(2):
                 mm(R("p5", 4 + s, 5 + s), R("TS%d" % s, p=e8), R("THf", 2 * j, 2 * j + 1, 1, e8), j == 0, j == 1)
-        ts(R("CV", 0, 12), R("IX", 0, 12), 64.0, Op.add)
-        ts(R("CV", 12, 24), R("IX", 12, 24), float(HS // 64 - 1), Op.add)
-        cp(R("BU"), R("p6", 0, 12))
-        for w, wt in enumerate((1.0, 64.0)):
-            for u in range(2):
-                for s in range(2):
-                    m = "ID" if u == s else ("SP" if s else "SM")
-                    ts(blk("PP", 4 * w + 2 * u + s), R(m), RM1 if u else RM0, Op.mult, wt, Op.mult)
-        ts(R("T1K"), R("p5", 4, 6), 1024.0, Op.mult)
-        ts(R("THR"), R("p5", 4, 6), 1024.0, Op.mult)
-        ts(CV1, col("EQ", C2), R("p5", 1, 2), Op.mult)
-        ts(CV2, col("EQ", C3), R("p5", 3, 4), Op.mult)
-        act_scale(R("SN"), R("SU"), CN)
-        agather(R("TF", HS, VO), R("TF", 0, P), R("BU"), NOT1)
-        lists("p7", 0, "SY", "TF", 0, 128, True, False)
-
-    def constants_for_marks():
-        weights(CG, CX, (ONE, GATE), (C1, -GATE))
-        weights(CMc, CX, (ONE, GATE), (C1, -GATE), (L2, -GATE), (C2, 0.5))
-        weights(CD, CX, (NH, 16.0), (NL, 1.0), (HI, -16.0), (LO, -1.0), (C1, float(P)))
-        ts(CG, CG, CV1, Op.add, CV2, Op.add)
-        ts(CMa, col("EQ", LO), 2 * GATE, Op.mult)
-        ts(CMb, col("EQ", C1), -GATE, Op.mult)
-        ts(R("WD"), R("BO", 0, 128, 16), CD, Op.mult)
-        ts(R("WG"), R("BO"), CG, Op.mult)
-        ts(blk("WT", 0), R("BD"), 0.0, Op.max, CMa, Op.mult)
-        ts(blk("WT", 1), blk("CF", 1), CMb, Op.mult, CMc, Op.add)
-        ts(R("NBO"), R("BO"), -1.0, Op.mult)
+        lists("p6", 0, "SY", "BMR", 0, 12)
         for r in range(16):
-            mm(R("p4", 128 + r, 256, 16), R("TF", r, P, 16), R("WD"))
-        tt(blk("WT", 2), blk("WT", 1), R("BO"), Op.mult)
-        for nm, w in (("I16", 16.0), ("IM", -float(P)), ("IVD", VOID)):
-            ts(R(nm), R("ID"), w, Op.mult)
-        tt(R("WM"), blk("WT", 0), blk("WT", 2), Op.add)
-        cp(R("DI"), R("p4", 128, 256))
-        weights(WF, CX, (HI, 1.0 / 1024), (LO, 128.0 / 1024))
-        ts(R("DH"), R("DI"), 4, Op.logical_shift_right)
-        ts(R("DL"), R("DI"), 15, Op.bitwise_and)
-        ts(R("N32"), R("N3b"), -1.0, Op.mult)
-        ts(R("WNR"), R("BO"), WN, Op.mult)
+            mm(R("p4", r, 128, 16), R("TF", r, P, 16), R("WD"))
+
+    def constants_for_keys():
+        for u in range(2):
+            act_scale(blk("PP", u, 160), R("IDP"), RM1 if u else RM0)
+        act(R("PP", 320, 640), R("PP", 0, 320), scale=64.0)
+        act(R("NBO"), R("BO"), scale=-1.0)
+        act(R("IM"), R("ID"), scale=-33.0)
+        act(R("IVD"), R("ID"), scale=VOID)
+        lists("p7", 0, "SY", "TF", 0, 128, True, False)
+        cp(R("BU"), R("p6", 0, 12))
+        ts(R("DI"), R("p4", 0, 128), -1.0, Op.mult, 4095.0, Op.add)
+        ts(R("IX", 0, 12), R("IV"), 63, Op.bitwise_and)
+        ts(R("IX", 12, 24), R("IV"), 6, Op.logical_shift_right)
+        ts(R("THR"), R("p5", 4, 6), 1024.0, Op.mult)
+        agather(R("TF", HS, VO), R("TF", 0, P), R("BU"), NOT1)
+        ts(R("DN"), R("DI"), 31, Op.bitwise_and)
+        ts(CV1, col("EQ", C2), R("p5", 1, 2), Op.mult, CG0, Op.add)
+        ts(CV2, col("EQ", C3), R("p5", 3, 4), Op.mult)
+        later.extend([
+            lambda: ts(R("CV", 0, 12), R("IX", 0, 12), 64.0, Op.add),
+            lambda: ts(R("CV", 12, 24), R("IX", 12, 24), float(HS // 64 - 1), Op.add),
+            lambda: ts(CG, CV1, CV2, Op.add),
+            lambda: ts(R("T1K"), R("p5", 4, 6), 1024.0, Op.mult),
+            lambda: ts(blk("WT", 0), R("BD"), 0.0, Op.max, CMa, Op.mult),
+            lambda: ts(blk("WT", 1), blk("CF", 1), CMb, Op.mult, CMc, Op.add),
+            lambda: act_scale(R("WG"), R("BO"), CG),
+            lambda: ts(R("DL"), R("DN"), 65.0, Op.add),
+            lambda: ts(R("DJ"), R("DN"), 33.0, Op.mult, 33.0 * 65, Op.add),
+            lambda: tt(blk("WT", 2), blk("WT", 1), R("BO"), Op.mult),
+            lambda: tt(R("DH"), R("p4", 0, 128), R("DJ"), Op.add),
+            lambda: tt(R("WM"), blk("WT", 0), blk("WT", 2), Op.add),
+        ])
 
     def preload(t):
         mm(R("p0", 0, L), R("KBM"), R("ON2"), True, False)
@@ -391,15 +397,17 @@ def rank_program(g, core, T, topo):
 
         def sums(i0, i1, src, ks, stop=False):
             for k in ks:
-                mm(R("p0", i0, i1), blk("SU", k), src(k), False, stop and k == ks[-1])
+                mm(R("p0", i0, i1), R("SU", 15 - k, 143 - k), src(k), False, stop and k == ks[-1])
 
         for k in range(16):
             mm(R("p%d" % (1 + k // 8), (k % 8) * CB, (k % 8) * CB + CB), R("ID"), R("GB", k, 16 * CB, 16), False, k % 8 == 7)
+        if t == 0:
+            constant_sums()
         act(R("AX", 0, 1024), R("DX", 0, 1024), Act.Abs)
         for j in range(2):
             act(blk("AB", j, 8 * CB), R("p%d" % (1 + j), 0, 8 * CB), Act.Abs)
         if t:
-            cp(R("KI"), R(K))
+            cp(R("AI"), R("p6", 200, 202))
         ts(R("AX", 1024, 2048), R("DX", 1024, 2048), -2.0, Op.mult, 0.0, Op.max)
         sums(0, 64, lambda k: R("AX", k, 1024, 16), range(16))
         sums(64, 128, lambda k: R("DX", 1024 + k, 2048, 16), range(16))
@@ -408,57 +416,53 @@ def rank_program(g, core, T, topo):
         sums(NX, L, lambda k: blk("AB", k, CB), range(8, 16), True)
         act(R("TX", HS, VO), R(H))
         if t:
-            cp(R("AI"), R("p6", 200, 202))
+            cp(R("KI"), R(K))
+            ts(R("AJ"), R("AI"), 31, Op.bitwise_and)
         ts(R("KA", 0, L), R("KI"), 63, Op.bitwise_and)
         if t:
-            ts(R("AJ"), R("AI"), 31, Op.bitwise_and)
+            ts(R("AK"), R("AJ"), 1024.0, Op.mult)
         ts(R("KA", L, 2 * L), R("KI"), 6, Op.logical_shift_right)
         if t:
-            ts(R("AK"), R("AJ"), 1024.0, Op.mult)
             tt(R("THR"), R("AK"), R("T1K"), Op.add)
             lists("p7", 0, "SY", "TF", 0, 128, True, False)
         else:
             constants_for_keys()
         for w in range(2):
             tt(blk("KAB", w, L), R("p0", 0, L), blk("KA", w, L), Op.add)
+        gap(3)
         for w in range(2):
-            op("V", lambda e: e.transpose(ap(blk("VT", w, L)), ap(blk("KAB", w, L))), [blk("KAB", w, L)], [blk("VT", w, L)])
+            turn(blk("VT", w, L), blk("KAB", w, L))
+        gap(4)
         for w in range(2):
-            op("V", lambda e: e.tensor_tensor_scan(ap(blk("MS", w, L)), ap(R("RST")), ap(blk("VT", w, L)), BIG, Op.max, Op.min), [R("RST"), blk("VT", w, L)], [blk("MS", w, L)])
+            scan(blk("MS", w, L), R("RST"), blk("VT", w, L), BIG, Op.max, Op.min)
         cp(blk("MI", 0, 12), R("MS", 15, L, 16))
         for s in range(2):
             ts(R("MV", s, 12, 2), R("MS", 15 + 16 * s, L, 32), col("THR", s), Op.is_ge)
         cp(blk("MI", 1, 12), R("MS", L + 15, 2 * L, 16))
         ts(blk("ML", 0, 12), blk("MI", 0, 12), 63, Op.bitwise_and)
+        gap(1)
         for w in range(2):
             tt(blk("SEL", w, 12), R("MV"), blk("CV", w, 12), Op.mult)
         ts(blk("ML", 1, 12), blk("MI", 1, 12), 63, Op.bitwise_and)
+        gap(1)
         for w in range(2):
             tt(blk("LB", w, 12), blk("ML", w, 12), blk("SEL", w, 12), Op.max)
-        for u in range(2):
-            for w in range(2):
+            gap(1)
+        for w in range(2):
+            for u in range(2):
                 for s in range(2):
-                    mm(R("p3", u, 12, 2), blk("PP", 4 * w + 2 * u + s), R("LB", 12 * w + s, 12 * w + 12, 2), w == 0 and s == 0, w == 1 and s == 1)
-        if t == 0:
-            constants_for_marks()
+                    c = 160 * (2 * w + u) + 16 - 16 * (s - u)
+                    mm(R("p3", u, 12, 2), R("PP", c, c + 128), R("LB", 12 * w + s, 12 * w + 12, 2), w + u + s == 0, w + u + s == 3)
+        gap(7)
         cp(R("L1"), R("p3", 0, 12))
+        gap(3)
 
         ttgather(R("SI"), R("TX"), R("L1"), R(H), Op.add)
         agather(R("FY"), R("TF"), R("L1"))
+        gap(3)
         ts(R("Q1"), R("SI"), 1, Op.arith_shift_right)
-        lists("p3", 16, "SN", "FY", 0, 12)
         up = slice(64, 128)
         WQ = R("ID", HI, 128, 16)
-        mm(R("p4", 0, 8), blk("FF", 0), WQ)
-        mm(R("p1", 0, 128), blk("FF", 0), R("WM"))
-        mm(R("p2", 128, 256), R("FY", 64, L), R("WG"), True, False)
-        mm(R("p2", 0, 128, 1, up), R("FY", 0, 64), R("WG"), False, False)
-        mm(R("p2", 0, 128, 1, slice(0, 64)), R("FY", 128, L), R("WG"), False, False)
-        mm(R("p6", 0, L), R("WG"), R("FY"), True, False)
-        cp(R("M1"), R("p3", 16, 28))
-        act(blk("MM", 0), R("p1", 0, 128), Act.Relu, scale=1024.0)
-        ttgather(R("E2"), R("TX", 0, P), R("M1"), R("Q1"), Op.subtract)
-        agather(R("FN"), R("TF", 0, P), R("M1"))
 
         def one_hot(c, gs):
             for gg in gs:
@@ -468,8 +472,23 @@ def rank_program(g, core, T, topo):
             for gg in range(8):
                 mm(R("p0", 16 * gg, 16 * gg + 16), blk("NN", 8 * c + gg), R("MM", 128 * c + 16 * gg, 128 * c + 16 * gg + 16), c == 0 and gg == 0, c == 2 and gg == 7)
 
-        one_hot(0, range(3))
+        mm(R("p4", 0, 8), blk("FF", 0), WQ)
+        lists("p3", 16, "SN", "FY", 0, 12)
+        mm(R("p1", 0, 128), blk("FF", 0), R("WM"))
+        mm(R("p2", 128, 256), R("FY", 64, L), R("WG"), True, False)
+        mm(R("p2", 0, 128, 1, up), R("FY", 0, 64), R("WG"), False, False)
+        mm(R("p2", 0, 128, 1, slice(0, 64)), R("FY", 128, L), R("WG"), False, False)
+        mm(R("p6", 0, L), R("WG"), R("FY"), True, False)
+        one_hot(0, range(N0))
+        cp(R("M1"), R("p3", 16, 28))
+        one_hot(0, range(N0, 8))
+        act(blk("MM", 0), R("p1", 0, 128), Act.Relu, 8192.0, 16384.0)
+        ttgather(R("E2"), R("TX", 0, P), R("M1"), R("Q1"), Op.subtract)
+        agather(R("FN"), R("TF", 0, P), R("M1"))
+        gap(9)
+        products(0)
         ts(R("AE"), R("E2"), -2.0, Op.mult, 0.0, Op.max)
+        ts(R("F2"), R("E2"), 0.5, Op.mult, -0.25, Op.add)
         for c in (1, 2):
             mm(R("p5", 8 * c, 8 * c + 8), blk("FF", c), WQ)
         for c in (1, 2):
@@ -477,13 +496,10 @@ def rank_program(g, core, T, topo):
         for src in ("E2", "AE"):
             mm(R("p2", 0, 128, 1, up), R(src, 0, 64), R("NBO"), False, False)
             mm(R("p2", 128, 256), R(src, 64, L), R("NBO"), False, src == "AE")
-        one_hot(0, range(3, 8))
-        act(R("MM", 128, 384), R("p2", 0, 256), Act.Relu, scale=1024.0)
+        for c in (1, 2):
+            act(blk("MM", c), blk("p2", c - 1), Act.Relu, 8192.0, 16384.0)
         for src in ("E2", "AE"):
             mm(R("p6", 0, L), R("NBO"), R(src), False, src == "AE")
-        products(0)
-        act(R("BS"), R("p6", 0, L), Act.Sign, bias=0.5)
-        act(R("BR"), R("BS"), Act.Relu)
         mm(R("p4", 256, 256 + L), R("ID"), R("FN"), True, False)
         mm(R("p4", 256, 256 + L), R("NI"), R("FY"), False, True)
         one_hot(1, range(8))
@@ -492,65 +508,85 @@ def rank_program(g, core, T, topo):
         products(2)
         if not last:
             lists("p3", 32, "SY", "FY", 0, 12, True, False)
-        ts(R("F2"), R("E2"), 0.5, Op.mult, -0.25, Op.add)
-        tt(R("GF"), R("p4", 256, 256 + L), R("BR"), Op.mult)
+        act(R("BS"), R("p6", 0, L), Act.Sign, 0.5)
+        act(R("p6", 256, 256 + L), R("BS"), Act.Relu)
+        act(R("BR"), R("BS"), Act.Relu)
         tt(R("UH"), R("p0", 0, 128), R("DH"), Op.min)
-        ts(R("MK"), R("p0", 0, 128), 0.0, Op.is_gt)
         tt(R("UL"), R("p0", 0, 128), R("DL"), Op.min)
-        for src, w in (("UH", "I16"), ("MK", "IM"), ("UL", "ID")):
+        for src, w in (("UH", "ID"), ("UL", "IM")):
             mm(R("p7", 0, 128), R(src), R(w), False, src == "UL")
-        tt(R("p5", 256, 256 + L), R("F2"), R("BR"), Op.mult)
+        tt(R("p5", 256, 256 + L), R("F2"), R("p6", 256, 256 + L), Op.mult)
+        tt(R("GF"), R("p4", 256, 256 + L), R("BR"), Op.mult)
         if not last:
-            lists("p3", 32, "SY", "GF", 0, 12, False, True)
-            mm(R("p1", 0, 128), R("MK"), R("IVD"), True, False)
+            mm(R("p1", 0, 128), R("UL"), R("IVD"), True, False)
             mm(R("p1", 0, 128), R("ID"), R("VL"), False, True)
         cp(R("ZU"), R("p7", 0, 128))
         tt(R("HS%d" % t), R("p5", 256, 256 + L), R("Q1"), Op.add)
+        if not last:
+            send(t, "H", "ha")
+            lists("p3", 32, "SY", "GF", 0, 12, False, True)
         if last:
             dma("S", T["yh"][:, :], ap(R("HS%d" % t)), [R("HS%d" % t)], [])
             mm(R("p6", 0, L), R("WNR"), R("FY"), True, False)
             mm(R("p6", 0, L), R("WNR"), R("GF"), False, True)
             s1, s2 = LAST
             agather(R("BF1", 16 * s1, P), R("IOT"), R("ZU", s1, 128))
-            vgather(R("BF1", 0, 16 * s1), R("IOT"), R("ZU", 0, s1))
             cp(R("RB"), R("p6", 0, L))
+            vgather(R("BF1", 0, 16 * s1), R("IOT"), R("ZU", 0, s1))
             dma("S", T["yb"][:, :], ap(row("RB", 0, 0, L)), [R("RB")], [])
             agather(R("ROW", 16 * s2, P), R("BF1"), R("ZU", s2, 128))
             vgather(R("ROW", 0, 16 * s2), R("BF1"), R("ZU", 0, s2))
             dma("S", T["yj"][:, :], ap(row("ROW", 0, 0, P)), [R("ROW")], [])
             break
-        send(t, "H", "ha")
         act(R("VL"), R("p1", 0, 128))
         local("S", row("XV", 0, 0, P), R("VL"))
-        s1, s2, s3 = SPLIT
+        s0, s1, s2, s3 = SPLIT
         agather(R("B1", 16 * s1, P), R("BB"), R("ZU", s1, 128))
-        cp(R("YU"), R("p3", 32, 44))
         lists("p4", 0, "SN", "FY", 0, 12, True, False)
         lists("p4", 0, "SN", "GF", 0, 12, False, True)
+        if t == 0:
+            ts(R("N32"), R("N3b"), -1.0, Op.mult)
+            ts(R("WNR"), R("BO"), CN, Op.mult, 1024.0, Op.mult)
         for b in range(6):
             mm(R("p6", 200, 202), R("N32"), R("MV", 2 * b, 2 * b + 2), b == 0, b == 5)
-        if t == 0:
-            ts(R("SF"), R("SU"), WF, Op.mult)
+        vgather(R("B1", 0, 16 * s0), R("BB"), R("ZU", 0, s0))
+        cp(R("YU"), R("p3", 32, 44))
+        vgather(R("B1", 16 * s0, 16 * s1), R("BB"), R("ZU", s0, s1))
         vgather(R("KS%d" % t), R("PL"), R("YU"))
         send(t, "K", "ka")
-        vgather(R("B1", 0, 16 * s1), R("BB"), R("ZU", 0, s1))
         cp(R("BU"), R("p4", 0, 12))
-        vgather(R("TF", 0, 16 * s2), R("B1"), R("ZU", 0, s2))
-        agather(R("TF", 16 * s2, P), R("B1"), R("ZU", s2, 128))
-        lists("p5", 0, "SF", "TF", 0, s3)
-        lists("p3", 0, "SF", "TF", s3, 128)
         h1 = "H%d" % (t + 1)
         for k in range(GK):
             gcopy(R("HX", k, NX * 16, 16), R(h1, 0, NX), NX)
-        for k in range(GK, 16):
-            cp(R("HX", k, NX * 16, 16), R(h1, 0, NX))
-        agather(R("TF", HS, VO), R("TF", 0, P), R("BU"), NOT1)
-        cp(R("JU", 0, s3), R("p5", 0, s3))
-        cp(R("JU", s3, 128), R("p3", 0, 128 - s3))
+        hx = list(range(GK, 16))
+
+        def copies(m):
+            for _ in range(min(m, len(hx))):
+                cp(R("HX", hx.pop(0), NX * 16, 16), R(h1, 0, NX))
+
+        for j, bank in ((0, "p5"), (1, "p3")):
+            q = 64 * j
+            vgather(R("TF", 16 * q, 16 * (q + s2)), R("B1"), R("ZU", q, q + s2))
+            agather(R("TF", 16 * (q + s2), 16 * (q + 64)), R("B1"), R("ZU", q + s2, q + 64))
+            lists(bank, 0, "SF", "TF", q, q + 64)
+        for j, bank in ((0, "p5"), (1, "p3")):
+            q = 64 * j
+            copies(HC[2 * j])
+            cp(R("JU", q, q + 64), R(bank, 0, 64))
+            copies(HC[2 * j + 1])
+            if j == 0:
+                agather(R("TF", HS, VO), R("TF", 0, P), R("BU"), NOT1)
+            vgather(R("TX", 16 * q, 16 * (q + s3[j])), R("XV"), R("JU", q, q + s3[j]))
+            agather(R("TX", 16 * (q + s3[j]), 16 * (q + 64)), R("XV"), R("JU", q + s3[j], q + 64))
         preload(t + 1)
-        vgather(R("TX", 0, 16 * s3), R("XV"), R("JU", 0, s3))
-        agather(R("TX", 16 * s3, P), R("XV"), R("JU", s3, 128))
+        copies(16)
         if t == 1:
             iota(R("IOT"), [[1, P]], 0, 0)
     finish()
     g.wait_ge(T.sem["loc"], 2 * (NV - 1) * len(topo.engines(core, nxt)))
+
+
+N0 = 5
+SPLIT = (16, 54, 32, (32, 24))
+HC = (0, 0, 2, 3)
+GK = 5

@@ -6,23 +6,25 @@ GATE = 8192.0
 L, P, NV = 192, 2048, 5
 HS = P
 VO = P + L
-NX = 128
+NX = 124
 CB = L - NX
 SPLIT = (56, 64, 64)
-LAST = (60, 64)
+LAST = (64, 64)
 GK = 5
 AK0 = 8
-HI, LO, NH, NL, ONE, L2, C1, C2, C3 = range(9)
+HI, LO, NH, NL, L2, ONE, C1, C2, C3 = range(9)
 
 B16, F32, I32, U16 = "bfloat16", "float32", "int32", "uint16"
 SCRATCH = {
-    "TX": ("sbuf", [128, VO], B16), "XV": ("sbuf", [128, P], B16), "TF": ("sbuf", [128, VO], B16),
+    "TXW": ("sbuf", [128, L + P], B16), "XV": ("sbuf", [128, P], B16), "TFW": ("sbuf", [128, L + P], B16),
+    "KP": ("sbuf", [128, L], I32), "IC": ("sbuf", [128, L], B16), "IL": ("sbuf", [128, 12], B16), "DT": ("sbuf", [128, 2 * 128], B16),
+    "THP": ("sbuf", [128, 4], F32), "W1": ("sbuf", [128, 128], B16),
     "BB": ("sbuf", [128, P], B16), "B1": ("sbuf", [128, P], B16), "PL": ("sbuf", [128, P], I32),
     "IOT": ("sbuf", [128, P], F32), "BF1": ("sbuf", [128, P], F32), "ROW": ("sbuf", [128, P], F32), "RB": ("sbuf", [128, L], F32),
     "HX": ("sbuf", [128, NX * 16], B16), "DX": ("sbuf", [128, NX * 16], B16), "AX": ("sbuf", [128, NX * 16], B16),
     "GB": ("sbuf", [128, CB * 16], B16), "AB": ("sbuf", [128, CB * 16], B16),
     "KI": ("sbuf", [128, L], I32), "KA": ("sbuf", [128, 2 * L], I32), "KAB": ("sbuf", [128, 2 * L], F32),
-    "VT": ("sbuf", [128, 2 * L], F32), "MS": ("sbuf", [128, 2 * L], F32), "RST": ("sbuf", [128, L], F32), "RS0": ("sbuf", [128, L], F32),
+    "VT": ("sbuf", [128, 2 * L], F32), "MS": ("sbuf", [128, 2 * L], I32), "RST": ("sbuf", [128, L], F32), "RS0": ("sbuf", [128, L], F32),
     "MI": ("sbuf", [128, 24], I32), "ML": ("sbuf", [128, 24], I32), "LB": ("sbuf", [128, 24], B16), "MV": ("sbuf", [128, 12], B16),
     "L1": ("sbuf", [128, 12], U16), "CV": ("sbuf", [128, 24], F32), "SEL": ("sbuf", [128, 24], F32),
     "IV": ("sbuf", [128, 12], I32), "IX": ("sbuf", [128, 24], I32),
@@ -36,7 +38,7 @@ SCRATCH = {
     "ZU": ("sbuf", [128, 128], U16), "JU": ("sbuf", [128, 128], U16),
     "AI": ("sbuf", [128, 2], I32), "AJ": ("sbuf", [128, 2], I32), "AK": ("sbuf", [128, 2], F32), "THR": ("sbuf", [128, 2], F32),
     "T1K": ("sbuf", [128, 2], F32),
-    "BD": ("sbuf", [128, 128], B16), "ONES": ("sbuf", [128, 512], B16),
+    "BD": ("sbuf", [128, 128], B16), "ONES": ("sbuf", [128, 256], B16),
     "IDP": ("sbuf", [128, 160], B16), "NI": ("sbuf", [128, 128], B16),
     "N32": ("sbuf", [128, 128], B16), "KBM": ("sbuf", [128, 128], B16), "BO": ("sbuf", [128, 128], B16), "NBO": ("sbuf", [128, 128], B16),
     "IDW": ("sbuf", [128, 3 * 128], B16), "WNR": ("sbuf", [128, 128], B16), "IQ": ("sbuf", [128, 128], B16),
@@ -51,7 +53,8 @@ SCRATCH = {
     "TMP": ("sbuf", [128, 5 * 128], B16),
     "HH": ("sbuf", [128, 2 * NV * L], B16), "KK": ("sbuf", [128, 2 * NV * L], U16),
 }
-ALIAS = {"FY": ("FF", 0, L), "FN": ("FF", L, L), "ID": ("IDP", 16, 128), "ON2": ("ONES", 0, L)}
+ALIAS = {"FY": ("FF", 0, L), "FN": ("FF", L, L), "ID": ("IDP", 16, 128), "ON2": ("ONES", 0, L),
+         "TXM": ("TXW", 0, L), "TX": ("TXW", L, P), "TFM": ("TFW", 0, L), "TF": ("TFW", L, P)}
 for _t in range(NV):
     ALIAS["H%d" % _t] = ("HH", L * _t, L)
     ALIAS["HS%d" % _t] = ("HH", L * (NV + _t), L)
@@ -80,7 +83,7 @@ def make_emitter(g, T):
             return False
         if a[3] == b[3] and a[3] > 1 and (a[1] - b[1]) % a[3]:
             return False
-        if a[4] != b[4] and a[4].step is not None and a[4].step == b[4].step and a[4].start != b[4].start:
+        if a[4] != b[4] and not set(range(128)[a[4]]) & set(range(128)[b[4]]):
             return False
         return True
 
@@ -149,7 +152,14 @@ def make_emitter(g, T):
         for k in range(nd[0]):
             await_("G", "d%d" % k, 16)
 
-    return ap, op, dma, arrive, deps, finish
+    tile = {}
+
+    def row_tile(j):
+        if 1 - j in tile:
+            await_("T", "sT", tile[1 - j])
+        tile[j] = count["T"] + 1
+
+    return ap, op, dma, arrive, deps, finish, row_tile
 
 
 def R(name, c0=0, c1=None, st=1, p=slice(None)):
@@ -171,6 +181,11 @@ def blk(name, j, w=128):
     return R(name, w * j, w * j + w)
 
 
+def doubling(h, a, b):
+    steps = [(R("HX", 16 * a + k, 16 * b, 16), R(h, a, b), b - a) for k in (0, 8)]
+    return steps + [(R("HX", 16 * a + s // 2, 16 * b, s), R("HX", 16 * a, 16 * b, s), 16 * (b - a) // s) for s in (8, 4, 2)]
+
+
 def rank_program(g, core, T, topo):
     rank = T.rank_of(core)
     if rank is None:
@@ -179,7 +194,7 @@ def rank_program(g, core, T, topo):
     nxt, prv = T.cores[(rank + 1) % n], T.cores[(rank - 1) % n]
     rid, pid = topo.addr(nxt, core)
     mask = topo.mask(core, nxt)
-    ap, op, dma, arrive, deps, finish = make_emitter(g, T)
+    ap, op, dma, arrive, deps, finish, row_tile = make_emitter(g, T)
 
     def tt(out, a, b, o):
         op("V", lambda e: e.tensor_tensor(ap(out), ap(a), ap(b), o), [a, b], [out])
@@ -210,6 +225,9 @@ def rank_program(g, core, T, topo):
 
     def act_scale(out, a, c):
         op("A", lambda e: e.activation(ap(out), ap(a), Act.Copy, scale=ap(c)), [a, c], [out])
+
+    def act_bias(out, a, sc, b):
+        op("A", lambda e: e.activation(ap(out), ap(a), Act.Identity, bias=ap(b), scale=sc), [a, b], [out])
 
     def vgather(out, win, off):
         op("V", lambda e: e.tensor_copy(ap(out), ap(win).indirect(ap(off))), [win, off], [out])
@@ -249,7 +267,7 @@ def rank_program(g, core, T, topo):
         arrive("%s%d" % (name, t + 1), "%s%d" % (sem, t + 1), len(topo.engines(prv, core)))
 
     e8 = slice(0, 8)
-    dma("S", T["TX"][:, 0:P], T["xp"][:, :], [], [R("TX", 0, P)])
+    dma("S", ap(R("TX")), T["xp"][:, :], [], [R("TX")])
     dma("C", T["KI"][:, :], T["kt"][:, :], [], [R("KI")])
     dma("C", ap(R("H0")), T["hm"][:, :], [], [R("H0")])
     dma("S", T["NXC"][:, :], T["nx"][:, :], [], [R("NXC")])
@@ -266,8 +284,6 @@ def rank_program(g, core, T, topo):
     iota(R("IP"), [[0, 2]], 0, 1)
     iota(R("BD0"), [[0, 8], [1, 16]], 0, 0)
     fill(R("ONES"), 1.0)
-    for j in range(4):
-        act(blk("TF", j, 512), R("ONES"))
     asel(R("BD1"), R("BD0"), [[-16, 8], [0, 16]], Op.is_ge, -1.0, 0, 1)
     iota(R("IH"), [[1, 8], [0, 16]], 0, 0)
     asel(R("BD"), R("BD1"), [[16, 8], [0, 16]], Op.is_ge, -1.0, 15, -1)
@@ -275,124 +291,121 @@ def rank_program(g, core, T, topo):
     ts(R("IW", 0, 1), R("IP", 0, 1), 15, Op.bitwise_and)
     ts(R("IW", 1, 2), R("IP", 1, 2), 31, Op.bitwise_and)
     fill(R("SU", 128, 144), 0.0)
-    fill(R("BMR"), 0.0)
-    tt(blk("CF", 1), R("BD0"), R("BD0"), Op.mult)
+    act(R("BMR"), R("ON2"), Act.Sigmoid, 0.0, -1000.0)
     cp(PM, R("IW", 0, 1))
-    cp(P32, R("IW", 1, 2))
-    local("S", row("TF", LO, 0, P), R("BD0"))
-    local("S", row("TF", L2, 0, P), blk("CF", 1))
+    ts(PM8, R("IW", 0, 1), 8.0, Op.mult)
+    ts(K64, R("IW", 0, 1), 64.0, Op.mult)
+    ts(R("EQ"), R("BD0", 0, 16), PM, Op.is_equal)
     ts(RM1, R("IW", 1, 2), 16.0, Op.is_ge)
     ts(RM0, R("IW", 1, 2), 16.0, Op.is_lt)
-    ts(R("EQ"), R("BD0", 0, 16), PM, Op.is_equal)
-    ts(PM8, PM, 8.0, Op.mult)
-    ts(K64, PM, 64.0, Op.mult)
-    two = ((CY, HI, 16.0 / 1024, LO, 1.0 / 1024), (CN, NH, 16.0 / 1024, NL, 1.0 / 1024), (WF, HI, 1.0 / 1024, LO, 128.0 / 1024), (CG0, ONE, GATE, C1, -GATE))
-    for c, f, w, f2, w2 in two:
-        ts(c, col("EQ", f), w, Op.mult)
-    ts(blk("CF", 0), R("IH"), PM8, Op.add)
-    for c, f, w, f2, w2 in two:
-        ts(c, col("EQ", f2), w2, Op.mult, c, Op.add)
-    local("S", row("TF", HI, 0, P), blk("CF", 0))
-    ts(NOT1, col("EQ", ONE), -1.0, Op.mult, 1.0, Op.add)
+    two = ((CY, HI, 16.0 / 1024, LO, 1.0 / 1024), (CN, NH, 16.0 / 1024, NL, 1.0 / 1024), (CG0, ONE, GATE, C1, -GATE), (WF, HI, 1.0 / 1024, LO, 128.0 / 1024))
+    for j, (c, f, w, f2, w2) in enumerate(two):
+        ts(col("CO", 24 + j), col("EQ", f), w, Op.mult)
+    ha = doubling("H0", RC, NX)
+    for j, (c, f, w, f2, w2) in enumerate(two):
+        for _ in range((2, 0, 1, 1)[j]):
+            act(*ha.pop(0)[:2])
+        act_bias(c, col("EQ", f2), w2, col("CO", 24 + j))
     ts(CMa, col("EQ", LO), 2 * GATE, Op.mult)
     ts(CMb, col("EQ", C1), -GATE, Op.mult)
-    ts(CMc, col("EQ", L2), -GATE, Op.mult, CG0, Op.add)
-    ts(CD, CN, CY, Op.subtract, 1024.0, Op.mult)
-    ts(R("SU", 0, 128), R("BD"), 15.0, Op.is_equal, 1024.0, Op.mult)
-    ts(R("BO"), R("BD"), 0.0, Op.is_ge)
+    ts(NOT1, col("EQ", ONE), -1.0, Op.mult, 1.0, Op.add)
+    tt(blk("CF", 1), R("BD0"), R("BD0"), Op.mult)
+    local("S", row("TF", LO, 0, P), R("BD0"))
+    local("S", row("TF", L2, 0, P), blk("CF", 1))
+    ts(R("THw", 0, 2, 1, e8), R("TH", 0, 2, 1, e8), 4032, Op.bitwise_and)
+    ts(R("THw", 2, 4, 1, e8), R("TH", 0, 2, 1, e8), 63, Op.bitwise_and)
+    ts(blk("CF", 0), R("IH"), PM8, Op.add)
+    cp(R("THf", 0, 4, 1, e8), R("THw", 0, 4, 1, e8))
+    cp(R("K0"), R("KI"))
+    local("S", row("TF", HI, 0, P), blk("CF", 0))
+    hx = doubling("H0", 0, RC)
+    cp(*hx[0][:2])
+    cp(*hx[1][:2])
     ts(R("CW", 0, 128), R("NXC"), 4, Op.logical_shift_right)
     ts(R("CW", 128, 256), R("NXC"), 15, Op.bitwise_and)
+    cp(*hx[2][:2])
     ts(R("BMw", 0, 12), R("BMC"), 4, Op.logical_shift_right)
     ts(R("BMw", 12, 24), R("BMC"), 15, Op.bitwise_and)
+    ts(R("SU", 0, 128), R("BD"), 15.0, Op.is_equal, 1024.0, Op.mult)
+    cp(*hx[3][:2])
     cp(R("CF", 256, 512), R("CW"))
     cp(R("BMf"), R("BMw"))
-    cp(R("K0"), R("KI"))
     local("S", row("TF", NH, 0, P), blk("CF", 2))
     local("S", row("TF", NL, 0, P), blk("CF", 3))
     for f in (HI, LO):
         local("S", row("BMR", f, 0, L), blk("BMf", f, 12))
-    for S, c in (("SY", CY), ("SN", CN), ("SF", WF)):
-        ts(R(S), R("SU"), c, Op.mult)
-    ts(R("WD"), R("BO", 0, 128, 16), CD, Op.mult)
-    ts(R("THw", 0, 2, 1, e8), R("TH", 0, 2, 1, e8), 4032, Op.bitwise_and)
-    ts(R("THw", 2, 4, 1, e8), R("TH", 0, 2, 1, e8), 63, Op.bitwise_and)
-    for k in range(16):
-        if k < AK0:
-            act(R("HX", k, NX * 16, 16), R("H0", 0, NX))
-        else:
-            cp(R("HX", k, NX * 16, 16), R("H0", 0, NX))
-    act_scale(R("KBM"), R("ID"), K64)
+    for gg in range(8):
+        local("S", R("TF", 0, P, 1, slice(16 * gg + ONE, 16 * gg + 16)), R("ONES", p=slice(0, 8 * (16 - ONE))))
+    cp(*hx[4][:2])
     act(R("NI"), R("ID"), scale=-1.0)
+    act(*ha.pop(0)[:2])
+    act_scale(R("KBM"), R("ID"), K64)
     asel(R("TSx", p=e8), R("ONES", 0, 128, p=e8), [[1, 128]], Op.is_ge, 0.0, 0, -16)
-    iota(R("I12"), [[32, 6], [0, 2]], 0, 0)
-    cp(R("THf", 0, 4, 1, e8), R("THw", 0, 4, 1, e8))
-    ts(R("IV"), R("I12"), P32, Op.add)
+    iota(R("IC"), [[-1, L]], L, 0)
     asel(R("TSR", p=e8), R("TSx", p=e8), [[-1, 128]], Op.is_ge, 0.0, 15, 16)
-    asel(R("TS0", p=e8), R("ONES", 0, 128, p=e8), [[-2, 4], [0, 32]], Op.is_equal, 0.0, 0, 1)
-    asel(R("TS1", p=e8), R("ONES", 0, 128, p=e8), [[-2, 4], [0, 32]], Op.is_equal, 0.0, -1, 1)
-    iota(R("RS0"), [[0, L]], 2 ** 24 - 1, 0)
+    iota(R("I12"), [[16, 12]], 0, 0)
+    asel(R("RST"), R("ON2"), [[0, 12], [1, 16]], Op.not_equal, 0.0, 0, 0)
     iota(R("IQ"), [[1, 128]], 0, 0)
-    asel(R("RST"), R("RS0"), [[0, 12], [1, 16]], Op.is_equal, -BIG, 0, 0)
     for r in range(16):
         gcopy(blk("XV", r), R("TX", r, P, 16), 128)
-    asel(R("N3a"), R("ONES", 0, 128), [[-32, 4], [0, 32]], Op.is_ge, 0.0, 0, 1)
-    asel(R("N3b"), R("N3a"), [[32, 4], [0, 32]], Op.is_ge, 0.0, 31, -1)
     dma("S", T["PL"][:, :], T["pl"][:, :], [], [R("PL")])
     local("S", R("BB"), R("TF", 0, P))
     local("S", R("VL"), row("XV", 0, 0, P))
 
     def constant_sums():
-        mm(R("p5", 0, 4), R("TSR", p=e8), R("THf", 0, 4, 1, e8))
-        for s in range(2):
-            for j in range(2):
-                mm(R("p5", 4 + s, 5 + s), R("TS%d" % s, p=e8), R("THf", 2 * j, 2 * j + 1, 1, e8), j == 0, j == 1)
         lists("p6", 0, "SY", "BMR", 0, 12)
         for r in range(16):
-            mm(R("p4", r, 128, 16), R("TF", r, P, 16), R("WD"))
+            mm(R("p4", 128 + r, 256, 16), R("TF", r, P, 16), R("WD"))
 
     def constants_for_keys():
+        ts(CMc, col("EQ", L2), -GATE, Op.mult, CG0, Op.add)
+        ts(R("WD"), R("BO", 0, 128, 16), CD, Op.mult)
+        ts(R("IL"), R("I12"), PM, Op.add)
+        ts(blk("WT", 0), R("BD"), 0.0, Op.max, CMa, Op.mult)
+        ts(blk("WT", 1), blk("CF", 1), CMb, Op.mult, CMc, Op.add)
+        ts(CV1, col("EQ", C2), col("THP", 1), Op.mult, CG0, Op.add)
+        constant_sums()
         for u in range(2):
             act_scale(blk("PP", u, 160), R("IDP"), RM1 if u else RM0)
         act(R("PP", 320, 640), R("PP", 0, 320), scale=64.0)
+        act_scale(R("SN"), R("SU"), CN)
         act(R("NBO"), R("BO"), scale=-1.0)
-        act(R("IM"), R("ID"), scale=-33.0)
-        act(R("IVD"), R("ID"), scale=VOID)
         lists("p7", 0, "SY", "TF", 0, 128, True, False)
-        cp(R("BU"), R("p6", 0, 12))
-        ts(R("DI"), R("p4", 0, 128), -1.0, Op.mult, 4095.0, Op.add)
-        ts(R("IX", 0, 12), R("IV"), 63, Op.bitwise_and)
-        ts(R("IX", 12, 24), R("IV"), 6, Op.logical_shift_right)
-        ts(R("THR"), R("p5", 4, 6), 1024.0, Op.mult)
-        agather(R("TF", HS, VO), R("TF", 0, P), R("BU"), NOT1)
-        ts(R("DN"), R("DI"), 31, Op.bitwise_and)
-        ts(CV1, col("EQ", C2), R("p5", 1, 2), Op.mult, CG0, Op.add)
-        ts(CV2, col("EQ", C3), R("p5", 3, 4), Op.mult)
         later.extend([
-            lambda: ts(R("CV", 0, 12), R("IX", 0, 12), 64.0, Op.add),
-            lambda: ts(R("CV", 12, 24), R("IX", 12, 24), float(HS // 64 - 1), Op.add),
-            lambda: ts(CG, CV1, CV2, Op.add),
-            lambda: ts(R("T1K"), R("p5", 4, 6), 1024.0, Op.mult),
-            lambda: ts(blk("WT", 0), R("BD"), 0.0, Op.max, CMa, Op.mult),
-            lambda: ts(blk("WT", 1), blk("CF", 1), CMb, Op.mult, CMc, Op.add),
+            lambda: act_scale(R("W1"), R("BO"), col("EQ", ONE)),
+            lambda: act(R("IM"), R("ID"), scale=-33.0),
+            lambda: act(R("IVD"), R("ID"), scale=VOID),
+            lambda: act_scale(R("SF"), R("SU"), WF),
+            lambda: (cp(R("BU"), R("p6", 0, 12)), agather(R("TFM"), R("TF"), R("BU"), NOT1)),
+            lambda: ts(CG, col("EQ", C3), col("THP", 3), Op.mult, CV1, Op.add),
             lambda: act_scale(R("WG"), R("BO"), CG),
-            lambda: ts(R("DL"), R("DN"), 65.0, Op.add),
-            lambda: ts(R("DJ"), R("DN"), 33.0, Op.mult, 33.0 * 65, Op.add),
             lambda: tt(blk("WT", 2), blk("WT", 1), R("BO"), Op.mult),
-            lambda: tt(R("DH"), R("p4", 0, 128), R("DJ"), Op.add),
+            lambda: ts(R("DI"), R("p4", 128, 256), -1.0, Op.mult, 4095.0, Op.add),
             lambda: tt(R("WM"), blk("WT", 0), blk("WT", 2), Op.add),
         ])
 
+    def sub(k):
+        j = max(x for x in range(len(KS)) if KS[x] <= k)
+        return blk("p%d" % (1 + j), k - KS[j], CB)
+
+    def thresholds():
+        for j in range(2):
+            mm(R("p0", 0, L), blk("DT", j), R("ON2"), False, False)
+
     def preload(t):
         mm(R("p0", 0, L), R("KBM"), R("ON2"), True, False)
+        if t:
+            mm(R("p4", 256, 256 + L), R("ID"), R("IC"))
+            thresholds()
         for k in range(16):
-            mm(R("p%d" % (1 + k // 8), (k % 8) * CB, (k % 8) * CB + CB), R("NI"), R("H%d" % t, NX, L), k % 8 == 0, False)
+            mm(sub(k), R("NI"), R("H%d" % t, NX, L), k in KS, False)
 
     preload(0)
     for t in range(NV):
         last = t == NV - 1
         H, K = "H%d" % t, "K%d" % t
         agather(R("GB"), R("TX", 0, P), R(K, NX, L))
-        for a, b in ((0, 64), (64, 128)):
+        for a, b in ((0, RC), (RC, NX)):
             ttgather(R("DX", 16 * a, 16 * b), R("TX", 0, P), R(K, a, b), R("HX", 16 * a, 16 * b), Op.subtract)
 
         def sums(i0, i1, src, ks, stop=False):
@@ -400,128 +413,153 @@ def rank_program(g, core, T, topo):
                 mm(R("p0", i0, i1), R("SU", 15 - k, 143 - k), src(k), False, stop and k == ks[-1])
 
         for k in range(16):
-            mm(R("p%d" % (1 + k // 8), (k % 8) * CB, (k % 8) * CB + CB), R("ID"), R("GB", k, 16 * CB, 16), False, k % 8 == 7)
+            mm(sub(k), R("ID"), R("GB", k, 16 * CB, 16), False, k + 1 in KS)
         if t == 0:
-            constant_sums()
-        act(R("AX", 0, 1024), R("DX", 0, 1024), Act.Abs)
-        for j in range(2):
-            act(blk("AB", j, 8 * CB), R("p%d" % (1 + j), 0, 8 * CB), Act.Abs)
-        if t:
-            cp(R("AI"), R("p6", 200, 202))
-        ts(R("AX", 1024, 2048), R("DX", 1024, 2048), -2.0, Op.mult, 0.0, Op.max)
-        sums(0, 64, lambda k: R("AX", k, 1024, 16), range(16))
-        sums(64, 128, lambda k: R("DX", 1024 + k, 2048, 16), range(16))
-        sums(NX, L, lambda k: blk("AB", k, CB), range(8))
-        sums(64, 128, lambda k: R("AX", 1024 + k, 2048, 16), range(16))
-        sums(NX, L, lambda k: blk("AB", k, CB), range(8, 16), True)
-        act(R("TX", HS, VO), R(H))
+            mm(R("p5", 0, 4), R("TSR", p=e8), R("THf", 0, 4, 1, e8))
+            mm(R("p4", 256, 256 + L), R("ID"), R("IC"))
+            act_scale(R("SY"), R("SU"), CY)
+        else:
+            agather(R("TFM"), R("TF"), R("BU"), NOT1)
+        for j in range(len(KS) - 1):
+            act(R("AB", KS[j] * CB, KS[j + 1] * CB), R("p%d" % (1 + j), 0, (KS[j + 1] - KS[j]) * CB), Act.Abs)
+        act(R("AX", 16 * RC, 16 * NX), R("DX", 16 * RC, 16 * NX), Act.Abs)
+        if t == 0:
+            cp(R("THP"), R("p5", 0, 4))
+        ts(R("AX", 0, 16 * RC), R("DX", 0, 16 * RC), -2.0, Op.mult, 0.0, Op.max)
         if t:
             cp(R("KI"), R(K))
-            ts(R("AJ"), R("AI"), 31, Op.bitwise_and)
-        ts(R("KA", 0, L), R("KI"), 63, Op.bitwise_and)
+        sums(0, RC, lambda k: R("DX", k, 16 * RC, 16), range(16))
+        sums(NX, L, lambda k: blk("AB", k, CB), range(16))
+        if t == 0:
+            for j in range(2):
+                ts(blk("DT", j), R("ID"), col("THP", 2 * j), Op.mult, -1024.0, Op.mult)
+        sums(0, RC, lambda k: R("AX", k, 16 * RC, 16), range(16))
+        if t == 0:
+            thresholds()
+        sums(RC, NX, lambda k: R("AX", 16 * RC + k, 16 * NX, 16), range(16), True)
+        act(R("TXM"), R(H))
+        tt(R("KP"), R("KI"), R("p4", 256, 256 + L), Op.add)
+        if t == 0:
+            ts(CD, CN, CY, Op.subtract, 1024.0, Op.mult)
+            ts(R("BO"), R("BD"), 0.0, Op.is_ge)
+        ts(R("KA", 0, L), R("KP"), 63, Op.bitwise_and)
+        ts(R("KA", L, 2 * L), R("KP"), 6, Op.logical_shift_right)
         if t:
-            ts(R("AK"), R("AJ"), 1024.0, Op.mult)
-        ts(R("KA", L, 2 * L), R("KI"), 6, Op.logical_shift_right)
-        if t:
-            tt(R("THR"), R("AK"), R("T1K"), Op.add)
             lists("p7", 0, "SY", "TF", 0, 128, True, False)
         else:
             constants_for_keys()
+        mm(R("p3", 0, 12), R("ID"), R("IL"), True, False)
         for w in range(2):
             tt(blk("KAB", w, L), R("p0", 0, L), blk("KA", w, L), Op.add)
-        gap(3)
         for w in range(2):
             turn(blk("VT", w, L), blk("KAB", w, L))
         gap(4)
         for w in range(2):
-            scan(blk("MS", w, L), R("RST"), blk("VT", w, L), BIG, Op.max, Op.min)
-        cp(blk("MI", 0, 12), R("MS", 15, L, 16))
-        for s in range(2):
-            ts(R("MV", s, 12, 2), R("MS", 15 + 16 * s, L, 32), col("THR", s), Op.is_ge)
-        cp(blk("MI", 1, 12), R("MS", L + 15, 2 * L, 16))
-        ts(blk("ML", 0, 12), blk("MI", 0, 12), 63, Op.bitwise_and)
-        gap(1)
+            scan(blk("MS", w, L), R("RST"), blk("VT", w, L), 0.0, Op.mult, Op.min)
         for w in range(2):
-            tt(blk("SEL", w, 12), R("MV"), blk("CV", w, 12), Op.mult)
-        ts(blk("ML", 1, 12), blk("MI", 1, 12), 63, Op.bitwise_and)
-        gap(1)
+            ts(blk("ML", w, 12), R("MS", L * w + 15, L * w + L, 16), 63, Op.bitwise_and)
+            gap(1)
         for w in range(2):
-            tt(blk("LB", w, 12), blk("ML", w, 12), blk("SEL", w, 12), Op.max)
+            cp(blk("LB", w, 12), blk("ML", w, 12))
             gap(1)
         for w in range(2):
             for u in range(2):
                 for s in range(2):
                     c = 160 * (2 * w + u) + 16 - 16 * (s - u)
-                    mm(R("p3", u, 12, 2), R("PP", c, c + 128), R("LB", 12 * w + s, 12 * w + 12, 2), w + u + s == 0, w + u + s == 3)
-        gap(7)
+                    mm(R("p3", u, 12, 2), R("PP", c, c + 128), R("LB", 12 * w + s, 12 * w + 12, 2), False, w + u + s == 3)
+        gap(1)
         cp(R("L1"), R("p3", 0, 12))
-        gap(3)
+        gap(1)
 
-        ttgather(R("SI"), R("TX"), R("L1"), R(H), Op.add)
-        agather(R("FY"), R("TF"), R("L1"))
+        ttgather(R("SI"), R("TXW"), R("L1"), R(H), Op.add)
+        agather(R("FY"), R("TFW"), R("L1"))
         gap(3)
+        if t == 0:
+            ts(R("DN"), R("DI"), 31, Op.bitwise_and)
         ts(R("Q1"), R("SI"), 1, Op.arith_shift_right)
-        up = slice(64, 128)
-        WQ = R("ID", HI, 128, 16)
 
-        def one_hot(c, gs):
+        def lanes(bank, c0, src, W, c, st, start=False, stop=False, parts=(0, 1, 2)):
+            n = 128 // st
+            for j in parts:
+                if j == 0:
+                    o, a, w = R(bank, c0, c0 + n), R(src, 0, 128), R(W, c, 128, st)
+                else:
+                    o, a, w = R(bank, c0 + n, c0 + n + n // 2, 1, slice(64 * j - 64, 64 * j)), R(src, 128, L), R(W, 64 * j - 64 + c, 64 * j, st)
+                mm(o, a, w, start and (stop or j == 0), stop and (start or j == 0))
+
+        def one_hot(w, js):
+            for j in js:
+                ts(blk("NN", 12 * w + j), R("IQ"), col("p5", j) if w else col("p4", j) if j < 8 else col("p3", 64 + j), Op.is_equal)
+
+        def positive(w, a, b):
+            act(R("MM", L * w + a, L * w + b), R("p%d" % (1 + w), a, b), Act.Relu, 8192.0, 16384.0)
+
+        def products(w, gs, part=0):
             for gg in gs:
-                ts(blk("NN", 8 * c + gg), R("IQ"), col("p4" if c == 0 else "p5", 8 * c + gg), Op.is_equal)
+                j, p = (gg, slice(None)) if part == 0 else (8 + gg % 4, slice(64 * part - 64, 64 * part))
+                if part:
+                    row_tile(part - 1)
+                mm(R("p0", 16 * gg, 16 * gg + 16), R("NN", 128 * (12 * w + j), 128 * (12 * w + j + 1), 1, p), R("MM", L * w + 16 * j, L * w + 16 * j + 16, 1, p),
+                   w + j == 0, w == 1 and j == 7)
 
-        def products(c):
-            for gg in range(8):
-                mm(R("p0", 16 * gg, 16 * gg + 16), blk("NN", 8 * c + gg), R("MM", 128 * c + 16 * gg, 128 * c + 16 * gg + 16), c == 0 and gg == 0, c == 2 and gg == 7)
-
-        mm(R("p4", 0, 8), blk("FF", 0), WQ)
+        lanes("p4", 0, "FY", "ID", HI, 16, True, True, (0,))
         lists("p3", 16, "SN", "FY", 0, 12)
-        mm(R("p1", 0, 128), blk("FF", 0), R("WM"))
-        mm(R("p2", 128, 256), R("FY", 64, L), R("WG"), True, False)
-        mm(R("p2", 0, 128, 1, up), R("FY", 0, 64), R("WG"), False, False)
-        mm(R("p2", 0, 128, 1, slice(0, 64)), R("FY", 128, L), R("WG"), False, False)
+        lanes("p1", 0, "FY", "WM", 0, 1, True, True)
+        lanes("p2", 0, "FY", "WG", 0, 1, True)
         mm(R("p6", 0, L), R("WG"), R("FY"), True, False)
         one_hot(0, range(N0))
         cp(R("M1"), R("p3", 16, 28))
+        lanes("p3", 64, "FY", "ID", HI, 16, True, True, (1, 2))
         one_hot(0, range(N0, 8))
-        act(blk("MM", 0), R("p1", 0, 128), Act.Relu, 8192.0, 16384.0)
+        positive(0, 0, 128)
+        products(0, range(8))
         ttgather(R("E2"), R("TX", 0, P), R("M1"), R("Q1"), Op.subtract)
         agather(R("FN"), R("TF", 0, P), R("M1"))
-        gap(9)
-        products(0)
+        positive(0, 128, L)
+        one_hot(0, range(8, N2))
+        if t == 0:
+            ts(R("DJ"), R("DN"), 33.0, Op.mult, 33.0 * 65, Op.add)
         ts(R("AE"), R("E2"), -2.0, Op.mult, 0.0, Op.max)
+        one_hot(0, range(N2, 12))
         ts(R("F2"), R("E2"), 0.5, Op.mult, -0.25, Op.add)
-        for c in (1, 2):
-            mm(R("p5", 8 * c, 8 * c + 8), blk("FF", c), WQ)
-        for c in (1, 2):
-            mm(blk("p2", c - 1), blk("FF", c), R("WM"), False, False)
-        for src in ("E2", "AE"):
-            mm(R("p2", 0, 128, 1, up), R(src, 0, 64), R("NBO"), False, False)
-            mm(R("p2", 128, 256), R(src, 64, L), R("NBO"), False, src == "AE")
-        for c in (1, 2):
-            act(blk("MM", c), blk("p2", c - 1), Act.Relu, 8192.0, 16384.0)
+        lanes("p5", 0, "FN", "ID", HI, 16, True, True)
+        lanes("p2", 0, "FN", "WM", 0, 1)
+        lanes("p2", 0, "E2", "NBO", 0, 1)
+        lanes("p2", 0, "AE", "NBO", 0, 1, False, True, (1, 2, 0))
+        positive(1, 128, L)
+        positive(1, 0, 128)
         for src in ("E2", "AE"):
             mm(R("p6", 0, L), R("NBO"), R(src), False, src == "AE")
+        products(0, range(4), 1)
         mm(R("p4", 256, 256 + L), R("ID"), R("FN"), True, False)
         mm(R("p4", 256, 256 + L), R("NI"), R("FY"), False, True)
+        products(0, range(4, 8), 2)
+        one_hot(1, range(8, 12))
         one_hot(1, range(8))
-        one_hot(2, range(8))
-        products(1)
-        products(2)
+        if t == 0:
+            tt(R("DH"), R("p4", 128, 256), R("DJ"), Op.add)
+            ts(R("DL"), R("DN"), 65.0, Op.add)
+        products(1, range(4, 8), 2)
+        products(1, range(6))
+        products(1, range(4), 1)
+        products(1, range(6, 8))
         if not last:
+            mm(R("p2", 256, 256 + L), R("W1"), R("FY"))
             lists("p3", 32, "SY", "FY", 0, 12, True, False)
-        act(R("BS"), R("p6", 0, L), Act.Sign, 0.5)
-        act(R("p6", 256, 256 + L), R("BS"), Act.Relu)
-        act(R("BR"), R("BS"), Act.Relu)
+        act(R("BR"), R("p6", 0, L), Act.Sigmoid, 500.0, 1000.0)
+        if not last:
+            op("A", lambda e: e.activation(ap(R("BS")), ap(R("p2", 256, 256 + L)), Act.Copy, accum_out=ap(col("AK", 0))), [R("p2", 256, 256 + L)], [R("BS"), col("AK", 0)])
+        tt(R("p5", 256, 256 + L), R("F2"), R("BR"), Op.mult)
         tt(R("UH"), R("p0", 0, 128), R("DH"), Op.min)
         tt(R("UL"), R("p0", 0, 128), R("DL"), Op.min)
         for src, w in (("UH", "ID"), ("UL", "IM")):
             mm(R("p7", 0, 128), R(src), R(w), False, src == "UL")
-        tt(R("p5", 256, 256 + L), R("F2"), R("p6", 256, 256 + L), Op.mult)
+        tt(R("HS%d" % t), R("p5", 256, 256 + L), R("Q1"), Op.add)
         tt(R("GF"), R("p4", 256, 256 + L), R("BR"), Op.mult)
         if not last:
             mm(R("p1", 0, 128), R("UL"), R("IVD"), True, False)
             mm(R("p1", 0, 128), R("ID"), R("VL"), False, True)
         cp(R("ZU"), R("p7", 0, 128))
-        tt(R("HS%d" % t), R("p5", 256, 256 + L), R("Q1"), Op.add)
         if not last:
             send(t, "H", "ha")
             lists("p3", 32, "SY", "GF", 0, 12, False, True)
@@ -531,8 +569,8 @@ def rank_program(g, core, T, topo):
             mm(R("p6", 0, L), R("WNR"), R("GF"), False, True)
             s1, s2 = LAST
             agather(R("BF1", 16 * s1, P), R("IOT"), R("ZU", s1, 128))
-            cp(R("RB"), R("p6", 0, L))
             vgather(R("BF1", 0, 16 * s1), R("IOT"), R("ZU", 0, s1))
+            cp(R("RB"), R("p6", 0, L))
             dma("S", T["yb"][:, :], ap(row("RB", 0, 0, L)), [R("RB")], [])
             agather(R("ROW", 16 * s2, P), R("BF1"), R("ZU", s2, 128))
             vgather(R("ROW", 0, 16 * s2), R("BF1"), R("ZU", 0, s2))
@@ -545,39 +583,37 @@ def rank_program(g, core, T, topo):
         lists("p4", 0, "SN", "FY", 0, 12, True, False)
         lists("p4", 0, "SN", "GF", 0, 12, False, True)
         if t == 0:
-            ts(R("N32"), R("N3b"), -1.0, Op.mult)
             ts(R("WNR"), R("BO"), CN, Op.mult, 1024.0, Op.mult)
-        for b in range(6):
-            mm(R("p6", 200, 202), R("N32"), R("MV", 2 * b, 2 * b + 2), b == 0, b == 5)
+        cp(col("AI", 0), col("AK", 0))
         vgather(R("B1", 0, 16 * s0), R("BB"), R("ZU", 0, s0))
+        ts(col("AJ", 0), col("AI", 0), 31, Op.bitwise_and)
         cp(R("YU"), R("p3", 32, 44))
         vgather(R("B1", 16 * s0, 16 * s1), R("BB"), R("ZU", s0, s1))
         vgather(R("KS%d" % t), R("PL"), R("YU"))
         send(t, "K", "ka")
+        ts(col("AK", 1), col("AJ", 0), col("THP", 2), Op.add, -1024.0, Op.mult)
         cp(R("BU"), R("p4", 0, 12))
         h1 = "H%d" % (t + 1)
-        for k in range(GK):
-            gcopy(R("HX", k, NX * 16, 16), R(h1, 0, NX), NX)
-        hx = list(range(GK, 16))
+        for dst, src, width in doubling(h1, GK, NX):
+            gcopy(dst, src, width)
+        hx = doubling(h1, 0, GK)
 
         def copies(m):
             for _ in range(min(m, len(hx))):
-                cp(R("HX", hx.pop(0), NX * 16, 16), R(h1, 0, NX))
+                cp(*hx.pop(0)[:2])
 
-        for j, bank in ((0, "p5"), (1, "p3")):
-            q = 64 * j
-            vgather(R("TF", 16 * q, 16 * (q + s2)), R("B1"), R("ZU", q, q + s2))
-            agather(R("TF", 16 * (q + s2), 16 * (q + 64)), R("B1"), R("ZU", q + s2, q + 64))
-            lists(bank, 0, "SF", "TF", q, q + 64)
-        for j, bank in ((0, "p5"), (1, "p3")):
-            q = 64 * j
+        parts = ((0, "p5", 0, HALF), (1, "p3", HALF, 128))
+        for j, bank, q, e in parts:
+            vgather(R("TF", 16 * q, 16 * (q + s2[j])), R("B1"), R("ZU", q, q + s2[j]))
+            agather(R("TF", 16 * (q + s2[j]), 16 * e), R("B1"), R("ZU", q + s2[j], e))
+            lists(bank, 0, "SF", "TF", q, e)
+        act_scale(blk("DT", 1), R("ID"), col("AK", 1))
+        for j, bank, q, e in parts:
             copies(HC[2 * j])
-            cp(R("JU", q, q + 64), R(bank, 0, 64))
+            cp(R("JU", q, e), R(bank, 0, e - q))
             copies(HC[2 * j + 1])
-            if j == 0:
-                agather(R("TF", HS, VO), R("TF", 0, P), R("BU"), NOT1)
             vgather(R("TX", 16 * q, 16 * (q + s3[j])), R("XV"), R("JU", q, q + s3[j]))
-            agather(R("TX", 16 * (q + s3[j]), 16 * (q + 64)), R("XV"), R("JU", q + s3[j], q + 64))
+            agather(R("TX", 16 * (q + s3[j]), 16 * e), R("XV"), R("JU", q + s3[j], e))
         preload(t + 1)
         copies(16)
         if t == 1:
@@ -586,7 +622,10 @@ def rank_program(g, core, T, topo):
     g.wait_ge(T.sem["loc"], 2 * (NV - 1) * len(topo.engines(core, nxt)))
 
 
-N0 = 5
-SPLIT = (16, 54, 32, (32, 24))
-HC = (0, 0, 2, 3)
-GK = 5
+N0, N2 = 6, 11
+RC = 72
+KS = (0, 4, 10, 16)
+HALF = 56
+SPLIT = (20, 56, (26, 36), (26, 36))
+HC = (2, 1, 0, 1)
+GK = 72

@@ -1,33 +1,30 @@
 from concourse.mybir import AluOpType as Op, ActivationFunctionType as Act
 
-BIG = 1.0e9
+BIG = 2.0 ** 40
+KW, KK = 2.0 ** 17, 4096
 VOID = 128.0
 GATE = 8192.0
 L, P, NV = 192, 2048, 5
-HS = P
-VO = P + L
-NX = 124
-CB = L - NX
-SPLIT = (56, 64, 64)
+CH = L // 16
+TURNS = pow(16, NV, L - 1)
 LAST = (64, 64)
-GK = 5
-AK0 = 8
 HI, LO, NH, NL, L2, ONE, C1, C2, C3 = range(9)
 
-B16, F32, I32, U16 = "bfloat16", "float32", "int32", "uint16"
+B16, F16, F32, I32, U16 = "bfloat16", "float16", "float32", "int32", "uint16"
 SCRATCH = {
-    "TXW": ("sbuf", [128, L + P], B16), "XV": ("sbuf", [128, P], B16), "TFW": ("sbuf", [128, L + P], B16),
-    "KP": ("sbuf", [128, L], I32), "IC": ("sbuf", [128, L], B16), "IL": ("sbuf", [128, 12], B16), "DT": ("sbuf", [128, 2 * 128], B16),
+    "TXW": ("sbuf", [128, P + NV * L], B16), "XV": ("sbuf", [128, P], B16), "TFW": ("sbuf", [128, P + NV * L], B16),
+    "KF": ("sbuf", [128, L], F32), "KJ": ("sbuf", [128, L], F16), "FZ": ("sbuf", [128, L], B16),
+    "ZN": ("sbuf", [128, L], B16), "RR": ("sbuf", [128, L], F32), "WO": ("sbuf", [128, 12], F32), "LI": ("sbuf", [128, 12], F32),
+    "OWN": ("sbuf", [128, 12 * NV], F32), "OWU": ("sbuf", [128, 12 * NV], U16), "IO": ("sbuf", [128, 12 * NV], I32), "IK": ("sbuf", [128, 12], I32),
+    "CQ": ("sbuf", [128, 36], F32), "CA": ("sbuf", [128, 36], I32), "CB": ("sbuf", [128, 36], F32), "CC": ("sbuf", [128, 36], F32),
+    "CD": ("sbuf", [128, 36], F32), "LU": ("sbuf", [128, 24], U16), "LK": ("sbuf", [128, 24], U16),
+    "HJ": ("sbuf", [128, L], B16), "HC": ("sbuf", [128, L], B16), "KC": ("sbuf", [128, L], B16), "DT": ("sbuf", [128, 2 * 128], B16),
     "THP": ("sbuf", [128, 4], F32), "W1": ("sbuf", [128, 128], B16),
     "BB": ("sbuf", [128, P], B16), "B1": ("sbuf", [128, P], B16), "PL": ("sbuf", [128, P], I32),
     "IOT": ("sbuf", [128, P], F32), "BF1": ("sbuf", [128, P], F32), "ROW": ("sbuf", [128, P], F32), "RB": ("sbuf", [128, L], F32),
-    "HX": ("sbuf", [128, NX * 16], B16), "DX": ("sbuf", [128, NX * 16], B16), "AX": ("sbuf", [128, NX * 16], B16),
-    "GB": ("sbuf", [128, CB * 16], B16), "AB": ("sbuf", [128, CB * 16], B16),
-    "KI": ("sbuf", [128, L], I32), "KA": ("sbuf", [128, 2 * L], I32), "KAB": ("sbuf", [128, 2 * L], F32),
-    "VT": ("sbuf", [128, 2 * L], F32), "MS": ("sbuf", [128, 2 * L], I32), "RST": ("sbuf", [128, L], F32), "RS0": ("sbuf", [128, L], F32),
-    "MI": ("sbuf", [128, 24], I32), "ML": ("sbuf", [128, 24], I32), "LB": ("sbuf", [128, 24], B16), "MV": ("sbuf", [128, 12], B16),
-    "L1": ("sbuf", [128, 12], U16), "CV": ("sbuf", [128, 24], F32), "SEL": ("sbuf", [128, 24], F32),
-    "IV": ("sbuf", [128, 12], I32), "IX": ("sbuf", [128, 24], I32),
+    "HX": ("sbuf", [128, L * 16], B16), "DX": ("sbuf", [128, L * 16], B16), "AX": ("sbuf", [128, L * 16], B16),
+    "KI": ("sbuf", [128, L], I32), "VT": ("sbuf", [128, 6, 2, 32], F16), "MS": ("sbuf", [128, L], F32), "RST": ("sbuf", [128, L], F32),
+    "L1": ("sbuf", [128, 12], U16),
     "SI": ("sbuf", [128, L], I32), "Q1": ("sbuf", [128, L], I32), "FF": ("sbuf", [128, 2 * L], B16), "GF": ("sbuf", [128, L], B16),
     "M1": ("sbuf", [128, 12], U16), "E2": ("sbuf", [128, L], B16), "AE": ("sbuf", [128, L], B16), "F2": ("sbuf", [128, L], I32),
     "BR": ("sbuf", [128, L], B16), "YU": ("sbuf", [128, 12], U16), "BU": ("sbuf", [128, 12], U16),
@@ -40,7 +37,7 @@ SCRATCH = {
     "T1K": ("sbuf", [128, 2], F32),
     "BD": ("sbuf", [128, 128], B16), "ONES": ("sbuf", [128, 256], B16),
     "IDP": ("sbuf", [128, 160], B16), "NI": ("sbuf", [128, 128], B16),
-    "N32": ("sbuf", [128, 128], B16), "KBM": ("sbuf", [128, 128], B16), "BO": ("sbuf", [128, 128], B16), "NBO": ("sbuf", [128, 128], B16),
+    "BO": ("sbuf", [128, 128], B16), "NBO": ("sbuf", [128, 128], B16),
     "IDW": ("sbuf", [128, 3 * 128], B16), "WNR": ("sbuf", [128, 128], B16), "IQ": ("sbuf", [128, 128], B16),
     "WM": ("sbuf", [128, 128], B16), "WG": ("sbuf", [128, 128], B16), "WD": ("sbuf", [128, 8], B16), "WT": ("sbuf", [128, 3 * 128], B16),
     "SU": ("sbuf", [128, 144], B16), "SY": ("sbuf", [128, 144], B16), "SN": ("sbuf", [128, 144], B16), "SF": ("sbuf", [128, 144], B16),
@@ -51,15 +48,15 @@ SCRATCH = {
     "TH": ("sbuf", [128, 2], I32), "THw": ("sbuf", [128, 4], I32), "THf": ("sbuf", [128, 4], B16),
     "TSR": ("sbuf", [128, 128], B16), "TSx": ("sbuf", [128, 128], B16), "TS0": ("sbuf", [128, 128], B16), "TS1": ("sbuf", [128, 128], B16),
     "TMP": ("sbuf", [128, 5 * 128], B16),
-    "HH": ("sbuf", [128, 2 * NV * L], B16), "KK": ("sbuf", [128, 2 * NV * L], U16),
+    "HH": ("sbuf", [128, NV * L], B16), "KU": ("sbuf", [128, 2 * NV * L], U16),
 }
-ALIAS = {"FY": ("FF", 0, L), "FN": ("FF", L, L), "ID": ("IDP", 16, 128), "ON2": ("ONES", 0, L),
-         "TXM": ("TXW", 0, L), "TX": ("TXW", L, P), "TFM": ("TFW", 0, L), "TF": ("TFW", L, P)}
+ALIAS = {"FY": ("FF", 0, L), "FN": ("FF", L, L), "ID": ("IDP", 16, 128), "ON2": ("ONES", 0, L), "TX": ("TXW", 0, P), "TF": ("TFW", 0, P)}
 for _t in range(NV):
-    ALIAS["H%d" % _t] = ("HH", L * _t, L)
-    ALIAS["HS%d" % _t] = ("HH", L * (NV + _t), L)
-    ALIAS["K%d" % _t] = ("KK", L * _t, L)
-    ALIAS["KS%d" % _t] = ("KK", L * (NV + _t), L)
+    ALIAS["H%d" % _t] = ("TXW", P + L * _t, L)
+    ALIAS["TFM%d" % _t] = ("TFW", P + L * _t, L)
+    ALIAS["HS%d" % _t] = ("HH", L * _t, L)
+    ALIAS["K%d" % _t] = ("KU", L * _t, L)
+    ALIAS["KS%d" % _t] = ("KU", L * (NV + _t), L)
 for _k, _n in enumerate(("BD0", "BD1", "N3a", "N3b", "IH")):
     ALIAS[_n] = ("TMP", 128 * _k, 128)
 for _k, _n in enumerate(("I16", "IM", "IVD")):
@@ -76,6 +73,8 @@ def make_emitter(g, T):
 
     def ap(r):
         name, c0, c1, st, p = r
+        if name == "VT":
+            return T[name][p, :, :, c0:c1] if st == 1 else T[name][p, :, -1 - st, c0:c1]
         return T[name][p, c0:c1:st] if st != 1 else T[name][p, c0:c1]
 
     def clash(a, b):
@@ -267,14 +266,14 @@ def rank_program(g, core, T, topo):
         arrive("%s%d" % (name, t + 1), "%s%d" % (sem, t + 1), len(topo.engines(prv, core)))
 
     e8 = slice(0, 8)
+    dma("C", ap(R("HS0")), T["hm"][:, :], [], [R("HS0")])
+    dma("S", T["KI"][:, :], T["kt"][:, :], [], [R("KI")])
     dma("S", ap(R("TX")), T["xp"][:, :], [], [R("TX")])
-    dma("C", T["KI"][:, :], T["kt"][:, :], [], [R("KI")])
-    dma("C", ap(R("H0")), T["hm"][:, :], [], [R("H0")])
     dma("S", T["NXC"][:, :], T["nx"][:, :], [], [R("NXC")])
     dma("S", T["BMC"][:, :], T["bm"][:, :], [], [R("BMC")])
     dma("C", T["TH"][e8, :], T["th"][:, :], [], [R("TH")])
 
-    PM, RM1, RM0, K64, P32, WF, PM8, NOT1, CY, CN, CMa, CMb, CMc, CG0, CG, CD, CV1, CV2 = (col("CO", j) for j in range(18))
+    PM, RM1, RM0, PMC, NZ, WF, PM8, NOT1, CY, CN, CMa, CMb, CMc, CG0, CG, CD, CV1, CV2 = (col("CO", j) for j in range(18))
     later = []
 
     def gap(k):
@@ -282,92 +281,109 @@ def rank_program(g, core, T, topo):
             later.pop(0)()
 
     iota(R("IP"), [[0, 2]], 0, 1)
+    iota(R("I12"), [[16, 12]], 0, 0)
+    iota(R("IO"), [[L, NV], [1, 12]], P, 0)
+    iota(R("IK"), [[1, 6], [6, 2]], 0, 0)
     iota(R("BD0"), [[0, 8], [1, 16]], 0, 0)
     fill(R("ONES"), 1.0)
     asel(R("BD1"), R("BD0"), [[-16, 8], [0, 16]], Op.is_ge, -1.0, 0, 1)
     iota(R("IH"), [[1, 8], [0, 16]], 0, 0)
     asel(R("BD"), R("BD1"), [[16, 8], [0, 16]], Op.is_ge, -1.0, 15, -1)
     asel(R("IDP"), R("ONES", 0, 160), [[-1, 160]], Op.is_equal, 0.0, 16, 1)
+    ones = [blk("TF", j, 512) for j in range(4)]
     ts(R("IW", 0, 1), R("IP", 0, 1), 15, Op.bitwise_and)
     ts(R("IW", 1, 2), R("IP", 1, 2), 31, Op.bitwise_and)
-    fill(R("SU", 128, 144), 0.0)
-    act(R("BMR"), R("ON2"), Act.Sigmoid, 0.0, -1000.0)
+    act(R("RST"), R("ON2"), Act.Sigmoid, 0.0, -1000.0)
+    fill(ones.pop(), 1.0)
     cp(PM, R("IW", 0, 1))
-    ts(PM8, R("IW", 0, 1), 8.0, Op.mult)
-    ts(K64, R("IW", 0, 1), 64.0, Op.mult)
+    ts(PMC, R("IW", 0, 1), float(CH), Op.mult)
+    fill(ones.pop(), 1.0)
+    ts(R("CQ", 0, 12), R("I12"), PM, Op.add)
+    ts(R("CQ", 12, 24), R("IK"), PMC, Op.add)
+    ts(R("CQ", 24, 36), R("IO", 0, 12), PMC, Op.add, -float(P), Op.add)
+    ts(R("OWN"), R("IO"), PMC, Op.add)
+    fill(ones.pop(), 1.0)
+    times = ((0, 24, TURNS), (24, 36, 16 * TURNS % (L - 1)))
+    for a, b, m in times:
+        ts(R("CA", a, b), R("CQ", a, b), m / (L - 1.0), Op.mult, -0.502, Op.add)
+    for a, b, m in times:
+        ts(R("CC", a, b), R("CQ", a, b), float(m), Op.mult)
+    cp(R("LK"), R("CQ", 12, 36))
+    ts(R("CB"), R("CA"), 0.0, Op.max, 1.0 - L, Op.mult)
+    fill(ones.pop(), 1.0)
+    tt(R("CD"), R("CB"), R("CC"), Op.add)
     ts(R("EQ"), R("BD0", 0, 16), PM, Op.is_equal)
-    ts(RM1, R("IW", 1, 2), 16.0, Op.is_ge)
-    ts(RM0, R("IW", 1, 2), 16.0, Op.is_lt)
-    two = ((CY, HI, 16.0 / 1024, LO, 1.0 / 1024), (CN, NH, 16.0 / 1024, NL, 1.0 / 1024), (CG0, ONE, GATE, C1, -GATE), (WF, HI, 1.0 / 1024, LO, 128.0 / 1024))
+    ts(PM8, R("IW", 0, 1), 8.0, Op.mult)
+    tt(blk("CF", 1), R("BD0"), R("BD0"), Op.mult)
+    cp(R("LU"), R("CD", 0, 24))
+    local("S", row("TF", LO, 0, P), R("BD0"))
+    local("S", row("TF", L2, 0, P), blk("CF", 1))
+    agather(R("HC"), R("HS0"), R("LU", 0, 12))
+    two = ((CY, HI, 16.0 / KW, LO, 1.0 / KW), (CN, NH, 16.0 / KW, NL, 1.0 / KW), (CG0, ONE, GATE, C1, -GATE), (WF, HI, 1.0 / KW, LO, 128.0 / KW))
     for j, (c, f, w, f2, w2) in enumerate(two):
         ts(col("CO", 24 + j), col("EQ", f), w, Op.mult)
-    ha = doubling("H0", RC, NX)
+    ha = doubling("HC", RC, NX)
+    act(R("NI"), R("ID"), scale=-1.0)
     for j, (c, f, w, f2, w2) in enumerate(two):
         for _ in range((2, 0, 1, 1)[j]):
             act(*ha.pop(0)[:2])
         act_bias(c, col("EQ", f2), w2, col("CO", 24 + j))
-    ts(CMa, col("EQ", LO), 2 * GATE, Op.mult)
-    ts(CMb, col("EQ", C1), -GATE, Op.mult)
-    ts(NOT1, col("EQ", ONE), -1.0, Op.mult, 1.0, Op.add)
-    tt(blk("CF", 1), R("BD0"), R("BD0"), Op.mult)
-    local("S", row("TF", LO, 0, P), R("BD0"))
-    local("S", row("TF", L2, 0, P), blk("CF", 1))
-    ts(R("THw", 0, 2, 1, e8), R("TH", 0, 2, 1, e8), 4032, Op.bitwise_and)
-    ts(R("THw", 2, 4, 1, e8), R("TH", 0, 2, 1, e8), 63, Op.bitwise_and)
     ts(blk("CF", 0), R("IH"), PM8, Op.add)
-    cp(R("THf", 0, 4, 1, e8), R("THw", 0, 4, 1, e8))
-    cp(R("K0"), R("KI"))
     local("S", row("TF", HI, 0, P), blk("CF", 0))
-    hx = doubling("H0", 0, RC)
+    vgather(R("K0"), R("KI"), R("LU", 0, 12))
+    hx = doubling("HC", 0, RC)
     cp(*hx[0][:2])
     cp(*hx[1][:2])
-    ts(R("CW", 0, 128), R("NXC"), 4, Op.logical_shift_right)
-    ts(R("CW", 128, 256), R("NXC"), 15, Op.bitwise_and)
+    vgather(R("KJ"), R("KI"), R("LU", 12, 24))
     cp(*hx[2][:2])
-    ts(R("BMw", 0, 12), R("BMC"), 4, Op.logical_shift_right)
-    ts(R("BMw", 12, 24), R("BMC"), 15, Op.bitwise_and)
-    ts(R("SU", 0, 128), R("BD"), 15.0, Op.is_equal, 1024.0, Op.mult)
+    ts(R("OWN", 0, 12), R("CD", 24, 36), float(P), Op.add)
+    ts(R("THw", 0, 2, 1, e8), R("TH", 0, 2, 1, e8), 4032, Op.bitwise_and)
+    ts(R("THw", 2, 4, 1, e8), R("TH", 0, 2, 1, e8), 63, Op.bitwise_and)
+    cp(R("VT", 16, 17), R("RST", 1, 13))
     cp(*hx[3][:2])
-    cp(R("CF", 256, 512), R("CW"))
-    cp(R("BMf"), R("BMw"))
-    local("S", row("TF", NH, 0, P), blk("CF", 2))
-    local("S", row("TF", NL, 0, P), blk("CF", 3))
-    for f in (HI, LO):
-        local("S", row("BMR", f, 0, L), blk("BMf", f, 12))
-    for gg in range(8):
-        local("S", R("TF", 0, P, 1, slice(16 * gg + ONE, 16 * gg + 16)), R("ONES", p=slice(0, 8 * (16 - ONE))))
+    turn(R("VT", 0, 16), R("KJ"))
+    cp(R("THf", 0, 4, 1, e8), R("THw", 0, 4, 1, e8))
+    ts(R("SU", 0, 128), R("BD"), 15.0, Op.is_equal, KW, Op.mult)
+    fill(R("SU", 128, 144), 0.0)
     cp(*hx[4][:2])
-    act(R("NI"), R("ID"), scale=-1.0)
+    cp(R("OWU"), R("OWN"))
+    ts(RM1, R("IW", 1, 2), 16.0, Op.is_ge)
+    ts(RM0, R("IW", 1, 2), 16.0, Op.is_lt)
+    fill(R("RST", 0, L, 16), BIG)
+    agather(R("H0"), R("HS0"), R("LK", 12, 24))
     act(*ha.pop(0)[:2])
-    act_scale(R("KBM"), R("ID"), K64)
+    iota(R("KC"), [[0, 12], [KK, 16]], KK, 0)
     asel(R("TSx", p=e8), R("ONES", 0, 128, p=e8), [[1, 128]], Op.is_ge, 0.0, 0, -16)
-    iota(R("IC"), [[-1, L]], L, 0)
     asel(R("TSR", p=e8), R("TSx", p=e8), [[-1, 128]], Op.is_ge, 0.0, 15, 16)
-    iota(R("I12"), [[16, 12]], 0, 0)
-    asel(R("RST"), R("ON2"), [[0, 12], [1, 16]], Op.not_equal, 0.0, 0, 0)
     iota(R("IQ"), [[1, 128]], 0, 0)
     for r in range(16):
         gcopy(blk("XV", r), R("TX", r, P, 16), 128)
-    dma("S", T["PL"][:, :], T["pl"][:, :], [], [R("PL")])
-    local("S", R("BB"), R("TF", 0, P))
-    local("S", R("VL"), row("XV", 0, 0, P))
+
+    def successors_and_bookmarks():
+        ts(R("CW", 0, 128), R("NXC"), 4, Op.logical_shift_right)
+        ts(R("CW", 128, 256), R("NXC"), 15, Op.bitwise_and)
+        cp(R("BU"), R("BMC"))
+        ts(CMa, col("EQ", LO), 2 * GATE, Op.mult)
+        ts(CMb, col("EQ", C1), -GATE, Op.mult)
+        ts(NOT1, col("EQ", ONE), -1.0, Op.mult, 1.0, Op.add)
+        cp(R("CF", 256, 512), R("CW"))
+        local("S", row("TF", NH, 0, P), blk("CF", 2))
+        local("S", row("TF", NL, 0, P), blk("CF", 3))
+        dma("S", T["PL"][:, :], T["pl"][:, :], [], [R("PL")])
+        local("S", R("BB"), R("TF", 0, P))
+        local("S", R("VL"), row("XV", 0, 0, P))
 
     def constant_sums():
-        lists("p6", 0, "SY", "BMR", 0, 12)
         for r in range(16):
-            mm(R("p4", 128 + r, 256, 16), R("TF", r, P, 16), R("WD"))
+            mm(R("p6", 256 + r, 384, 16), R("TF", r, P, 16), R("WD"))
 
     def constants_for_keys():
         ts(CMc, col("EQ", L2), -GATE, Op.mult, CG0, Op.add)
         ts(R("WD"), R("BO", 0, 128, 16), CD, Op.mult)
-        ts(R("IL"), R("I12"), PM, Op.add)
         ts(blk("WT", 0), R("BD"), 0.0, Op.max, CMa, Op.mult)
         ts(blk("WT", 1), blk("CF", 1), CMb, Op.mult, CMc, Op.add)
         ts(CV1, col("EQ", C2), col("THP", 1), Op.mult, CG0, Op.add)
         constant_sums()
-        for u in range(2):
-            act_scale(blk("PP", u, 160), R("IDP"), RM1 if u else RM0)
-        act(R("PP", 320, 640), R("PP", 0, 320), scale=64.0)
         act_scale(R("SN"), R("SU"), CN)
         act(R("NBO"), R("BO"), scale=-1.0)
         lists("p7", 0, "SY", "TF", 0, 128, True, False)
@@ -376,103 +392,116 @@ def rank_program(g, core, T, topo):
             lambda: act(R("IM"), R("ID"), scale=-33.0),
             lambda: act(R("IVD"), R("ID"), scale=VOID),
             lambda: act_scale(R("SF"), R("SU"), WF),
-            lambda: (cp(R("BU"), R("p6", 0, 12)), agather(R("TFM"), R("TF"), R("BU"), NOT1)),
+            lambda: agather(R("TFM0"), R("TF"), R("BU"), NOT1),
             lambda: ts(CG, col("EQ", C3), col("THP", 3), Op.mult, CV1, Op.add),
             lambda: act_scale(R("WG"), R("BO"), CG),
             lambda: tt(blk("WT", 2), blk("WT", 1), R("BO"), Op.mult),
-            lambda: ts(R("DI"), R("p4", 128, 256), -1.0, Op.mult, 4095.0, Op.add),
+            lambda: ts(R("DI"), R("p6", 256, 384), -1.0, Op.mult, 4095.0, Op.add),
             lambda: tt(R("WM"), blk("WT", 0), blk("WT", 2), Op.add),
         ])
 
-    def sub(k):
-        j = max(x for x in range(len(KS)) if KS[x] <= k)
-        return blk("p%d" % (1 + j), k - KS[j], CB)
+    banks = [("p%d" % (1 + j), AB[j], AB[j + 1]) for j in range(len(AB) - 1)]
 
     def thresholds():
         for j in range(2):
             mm(R("p0", 0, L), blk("DT", j), R("ON2"), False, False)
 
     def preload(t):
-        mm(R("p0", 0, L), R("KBM"), R("ON2"), True, False)
+        mm(R("p0", 0, L), R("ID"), R("KC"), True, False)
         if t:
-            mm(R("p4", 256, 256 + L), R("ID"), R("IC"))
             thresholds()
-        for k in range(16):
-            mm(sub(k), R("NI"), R("H%d" % t, NX, L), k in KS, False)
+
+    def less_h(t, js):
+        for bank, a, b in banks[js]:
+            for k in range(16):
+                mm(R(bank, k, 16 * (b - a), 16), R("NI"), R("H%d" % t if t else "HC", a, b), k == 0, False)
+
+    def sums(src, c0, c1, stop=False):
+        rs = range(c0 // CH, (c1 - 1) // CH + 1)
+        for r in rs:
+            a, b = max(c0, CH * r), min(c1, CH * r + CH)
+            mm(R("p0", 16 * (a - CH * r), 16 * (b - CH * r)), R("SU", 15 - r, 143 - r), R(src, 16 * a, 16 * b), False, stop and r == rs[-1])
+
+    def steps_to_keys():
+        for u in range(2):
+            for s in range(2):
+                for w in range(2):
+                    c = 160 * (2 * w + u) + 16 - 16 * (s - u)
+                    mm(R("p4", 256 + 96 * u, 352 + 96 * u), R("PP", c, c + 128), R("VT", w, w + 16, -1 - s), u + s + w == 0, u + s + w == 3)
 
     preload(0)
+    less_h(0, slice(None))
     for t in range(NV):
         last = t == NV - 1
-        H, K = "H%d" % t, "K%d" % t
-        agather(R("GB"), R("TX", 0, P), R(K, NX, L))
-        for a, b in ((0, RC), (RC, NX)):
-            ttgather(R("DX", 16 * a, 16 * b), R("TX", 0, P), R(K, a, b), R("HX", 16 * a, 16 * b), Op.subtract)
-
-        def sums(i0, i1, src, ks, stop=False):
-            for k in ks:
-                mm(R("p0", i0, i1), R("SU", 15 - k, 143 - k), src(k), False, stop and k == ks[-1])
-
-        for k in range(16):
-            mm(sub(k), R("ID"), R("GB", k, 16 * CB, 16), False, k + 1 in KS)
+        K, WIN = "K%d" % t, P + L * (t + 1)
         if t == 0:
             mm(R("p5", 0, 4), R("TSR", p=e8), R("THf", 0, 4, 1, e8))
-            mm(R("p4", 256, 256 + L), R("ID"), R("IC"))
-            act_scale(R("SY"), R("SU"), CY)
-        else:
-            agather(R("TFM"), R("TF"), R("BU"), NOT1)
-        for j in range(len(KS) - 1):
-            act(R("AB", KS[j] * CB, KS[j + 1] * CB), R("p%d" % (1 + j), 0, (KS[j + 1] - KS[j]) * CB), Act.Abs)
-        act(R("AX", 16 * RC, 16 * NX), R("DX", 16 * RC, 16 * NX), Act.Abs)
+        for j, (what, a, b) in enumerate(STEP1):
+            d, x = R("DX", 16 * a, 16 * b), R("AX", 16 * a, 16 * b)
+            if what == "less h":
+                ttgather(d, R("TX"), R(K, a, b), R("HX", 16 * a, 16 * b), Op.subtract)
+            elif what == "plain":
+                agather(d, R("TX"), R(K, a, b))
+                for bank, c, e in banks:
+                    if a < e <= b:
+                        mm(R(bank, 0, 16 * (e - c)), R("ID"), R("DX", 16 * c, 16 * e), False, True)
+            elif what == "relu":
+                ts(x, d, -2.0, Op.mult, 0.0, Op.max)
+            elif what == "abs":
+                act(x, d if a < NX else R(banks[AB.index(a)][0], 0, 16 * (b - a)), Act.Abs)
+            elif what == "sum d":
+                sums("DX", a, b)
+            elif what == "sum":
+                sums("AX", a, b, "sum" not in [w for w, _, _ in STEP1[j + 1:]])
+            elif what == "misses" and t:
+                agather(R("TFM%d" % t), R("TF"), R("BU"), NOT1)
+            elif what == "misses":
+                act_scale(R("SY"), R("SU"), CY)
+            elif what == "tile" and t:
+                cp(R("KF"), R(K))
+            elif what == "reorder" and t:
+                agather(R("KJ"), R("KF"), R("LK", 0, 12))
+            elif what == "reorder":
+                for u in range(2):
+                    act_scale(blk("PP", u, 160), R("IDP"), RM1 if u else RM0)
+            elif what == "turn" and t == 0:
+                ts(R("PP", 320, 640), R("PP", 0, 320), -1.0, Op.mult)
+            elif what == "turn" and t:
+                turn(R("VT", 0, 16), R("KJ"))
+            elif what == "steps":
+                steps_to_keys()
+            elif what == "thresholds" and t == 0:
+                cp(R("THP"), R("p5", 0, 4))
+                successors_and_bookmarks()
+                for w in range(2):
+                    ts(blk("DT", w), R("ID"), col("THP", 2 * w), Op.mult, -KW, Op.mult)
+                thresholds()
+        agather(R("HJ"), R("TXW", 0, WIN), blk("OWU", t, 12))
         if t == 0:
-            cp(R("THP"), R("p5", 0, 4))
-        ts(R("AX", 0, 16 * RC), R("DX", 0, 16 * RC), -2.0, Op.mult, 0.0, Op.max)
-        if t:
-            cp(R("KI"), R(K))
-        sums(0, RC, lambda k: R("DX", k, 16 * RC, 16), range(16))
-        sums(NX, L, lambda k: blk("AB", k, CB), range(16))
-        if t == 0:
-            for j in range(2):
-                ts(blk("DT", j), R("ID"), col("THP", 2 * j), Op.mult, -1024.0, Op.mult)
-        sums(0, RC, lambda k: R("AX", k, 16 * RC, 16), range(16))
-        if t == 0:
-            thresholds()
-        sums(RC, NX, lambda k: R("AX", 16 * RC + k, 16 * NX, 16), range(16), True)
-        act(R("TXM"), R(H))
-        tt(R("KP"), R("KI"), R("p4", 256, 256 + L), Op.add)
-        if t == 0:
-            ts(CD, CN, CY, Op.subtract, 1024.0, Op.mult)
+            ts(CD, CN, CY, Op.subtract, KW, Op.mult)
             ts(R("BO"), R("BD"), 0.0, Op.is_ge)
-        ts(R("KA", 0, L), R("KP"), 63, Op.bitwise_and)
-        ts(R("KA", L, 2 * L), R("KP"), 6, Op.logical_shift_right)
         if t:
             lists("p7", 0, "SY", "TF", 0, 128, True, False)
         else:
             constants_for_keys()
-        mm(R("p3", 0, 12), R("ID"), R("IL"), True, False)
-        for w in range(2):
-            tt(blk("KAB", w, L), R("p0", 0, L), blk("KA", w, L), Op.add)
-        for w in range(2):
-            turn(blk("VT", w, L), blk("KAB", w, L))
-        gap(4)
-        for w in range(2):
-            scan(blk("MS", w, L), R("RST"), blk("VT", w, L), 0.0, Op.mult, Op.min)
-        for w in range(2):
-            ts(blk("ML", w, 12), R("MS", L * w + 15, L * w + L, 16), 63, Op.bitwise_and)
-            gap(1)
-        for w in range(2):
-            cp(blk("LB", w, 12), blk("ML", w, 12))
-            gap(1)
-        for w in range(2):
-            for u in range(2):
-                for s in range(2):
-                    c = 160 * (2 * w + u) + 16 - 16 * (s - u)
-                    mm(R("p3", u, 12, 2), R("PP", c, c + 128), R("LB", 12 * w + s, 12 * w + 12, 2), False, w + u + s == 3)
+            gap(4)
+        halves = list(zip(KEYS, KEYS[1:]))
+        for a, b in halves:
+            scan(R("MS", a, b), R("RST", a, b), R("p0", a, b), 0.0, Op.add, Op.min)
         gap(1)
-        cp(R("L1"), R("p3", 0, 12))
+        for a, b in halves:
+            tt(R("ZN", a, b), R("p0", a, b), R("MS", a, b), Op.not_equal)
+        tt(R("WO"), R("MS", 15, L, 16), blk("OWN", t, 12), Op.min)
+        for a, b in halves:
+            scan(R("RR", a, b), R("ZN", a, b), R("p4", 256 + a, 256 + b), 0.0, Op.mult, Op.add)
+        gap(1)
+        tt(R("LI"), R("RR", 15, L, 16), R("WO"), Op.max)
+        gap(1)
+        cp(R("L1"), R("LI"))
         gap(1)
 
-        ttgather(R("SI"), R("TXW"), R("L1"), R(H), Op.add)
-        agather(R("FY"), R("TFW"), R("L1"))
+        ttgather(R("SI"), R("TXW", 0, WIN), R("L1"), R("HJ"), Op.add)
+        agather(R("FY"), R("TFW", 0, WIN), R("L1"))
         gap(3)
         if t == 0:
             ts(R("DN"), R("DI"), 31, Op.bitwise_and)
@@ -518,7 +547,7 @@ def rank_program(g, core, T, topo):
         positive(0, 128, L)
         one_hot(0, range(8, N2))
         if t == 0:
-            ts(R("DJ"), R("DN"), 33.0, Op.mult, 33.0 * 65, Op.add)
+            ts(R("DJ"), R("DN"), 33.0, Op.mult, 33.0 * 65 + 4095, Op.add)
         ts(R("AE"), R("E2"), -2.0, Op.mult, 0.0, Op.max)
         one_hot(0, range(N2, 12))
         ts(R("F2"), R("E2"), 0.5, Op.mult, -0.25, Op.add)
@@ -537,7 +566,7 @@ def rank_program(g, core, T, topo):
         one_hot(1, range(8, 12))
         one_hot(1, range(8))
         if t == 0:
-            tt(R("DH"), R("p4", 128, 256), R("DJ"), Op.add)
+            tt(R("DH"), R("DJ"), R("DI"), Op.subtract)
             ts(R("DL"), R("DN"), 65.0, Op.add)
         products(1, range(4, 8), 2)
         products(1, range(6))
@@ -549,20 +578,28 @@ def rank_program(g, core, T, topo):
         act(R("BR"), R("p6", 0, L), Act.Sigmoid, 500.0, 1000.0)
         if not last:
             op("A", lambda e: e.activation(ap(R("BS")), ap(R("p2", 256, 256 + L)), Act.Copy, accum_out=ap(col("AK", 0))), [R("p2", 256, 256 + L)], [R("BS"), col("AK", 0)])
-        tt(R("p5", 256, 256 + L), R("F2"), R("BR"), Op.mult)
-        tt(R("UH"), R("p0", 0, 128), R("DH"), Op.min)
-        tt(R("UL"), R("p0", 0, 128), R("DL"), Op.min)
-        for src, w in (("UH", "ID"), ("UL", "IM")):
-            mm(R("p7", 0, 128), R(src), R(w), False, src == "UL")
-        tt(R("HS%d" % t), R("p5", 256, 256 + L), R("Q1"), Op.add)
-        tt(R("GF"), R("p4", 256, 256 + L), R("BR"), Op.mult)
-        if not last:
-            mm(R("p1", 0, 128), R("UL"), R("IVD"), True, False)
-            mm(R("p1", 0, 128), R("ID"), R("VL"), False, True)
-        cp(R("ZU"), R("p7", 0, 128))
-        if not last:
-            send(t, "H", "ha")
-            lists("p3", 32, "SY", "GF", 0, 12, False, True)
+        for what in (ENDL if last else END):
+            if what == "half":
+                tt(R("p5", 256, 256 + L), R("F2"), R("BR"), Op.mult)
+            elif what == "h":
+                tt(R("HS%d" % t), R("p5", 256, 256 + L), R("Q1"), Op.add)
+                if not last:
+                    send(t, "H", "ha")
+            elif what == "fields":
+                tt(R("GF"), R("p4", 256, 256 + L), R("BR"), Op.mult)
+            elif what == "y":
+                lists("p3", 32, "SY", "GF", 0, 12, False, True)
+            elif what == "marks":
+                tt(R("UH"), R("p0", 0, 128), R("DH"), Op.min)
+                tt(R("UL"), R("p0", 0, 128), R("DL"), Op.min)
+            elif what == "J2":
+                for src, w in (("UH", "ID"), ("UL", "IM")):
+                    mm(R("p7", 0, 128), R(src), R(w), False, src == "UL")
+            elif what == "void":
+                mm(R("p1", 0, 128), R("UL"), R("IVD"), True, False)
+                mm(R("p1", 0, 128), R("ID"), R("VL"), False, True)
+            elif what == "list":
+                cp(R("ZU"), R("p7", 0, 128))
         if last:
             dma("S", T["yh"][:, :], ap(R("HS%d" % t)), [R("HS%d" % t)], [])
             mm(R("p6", 0, L), R("WNR"), R("FY"), True, False)
@@ -583,7 +620,7 @@ def rank_program(g, core, T, topo):
         lists("p4", 0, "SN", "FY", 0, 12, True, False)
         lists("p4", 0, "SN", "GF", 0, 12, False, True)
         if t == 0:
-            ts(R("WNR"), R("BO"), CN, Op.mult, 1024.0, Op.mult)
+            ts(R("WNR"), R("BO"), CN, Op.mult, KW, Op.mult)
         cp(col("AI", 0), col("AK", 0))
         vgather(R("B1", 0, 16 * s0), R("BB"), R("ZU", 0, s0))
         ts(col("AJ", 0), col("AI", 0), 31, Op.bitwise_and)
@@ -591,7 +628,7 @@ def rank_program(g, core, T, topo):
         vgather(R("B1", 16 * s0, 16 * s1), R("BB"), R("ZU", s0, s1))
         vgather(R("KS%d" % t), R("PL"), R("YU"))
         send(t, "K", "ka")
-        ts(col("AK", 1), col("AJ", 0), col("THP", 2), Op.add, -1024.0, Op.mult)
+        ts(col("AK", 1), col("AJ", 0), col("THP", 2), Op.add, -KW, Op.mult)
         cp(R("BU"), R("p4", 0, 12))
         h1 = "H%d" % (t + 1)
         for dst, src, width in doubling(h1, GK, NX):
@@ -615,6 +652,7 @@ def rank_program(g, core, T, topo):
             vgather(R("TX", 16 * q, 16 * (q + s3[j])), R("XV"), R("JU", q, q + s3[j]))
             agather(R("TX", 16 * (q + s3[j]), 16 * e), R("XV"), R("JU", q + s3[j], e))
         preload(t + 1)
+        less_h(t + 1, slice(None))
         copies(16)
         if t == 1:
             iota(R("IOT"), [[1, P]], 0, 0)
@@ -623,8 +661,16 @@ def rank_program(g, core, T, topo):
 
 
 N0, N2 = 6, 11
-RC = 72
-KS = (0, 4, 10, 16)
+RC, NX = 72, 128
+AB = (128, 160, 192)
+STEP1 = (("tile", 0, 0), ("plain", 128, 160), ("less h", 0, 24), ("less h", 24, 48), ("sum d", 0, 24), ("thresholds", 0, 0), ("plain", 160, 192),
+         ("relu", 0, 24), ("sum d", 24, 48), ("less h", 48, 84), ("sum", 0, 24), ("reorder", 0, 0), ("abs", 128, 160), ("relu", 24, 48),
+         ("abs", 160, 192), ("sum", 128, 160), ("less h", 84, 108), ("sum", 24, 48), ("abs", 48, 84), ("sum", 160, 192), ("less h", 108, 128),
+         ("sum d", 84, 108), ("relu", 84, 108), ("sum d", 108, 128), ("misses", 0, 0), ("sum", 48, 84), ("turn", 0, 0), ("sum", 84, 108),
+         ("relu", 108, 128), ("sum", 108, 128), ("steps", 0, 0))
+END = ("half", "marks", "J2", "h", "fields", "void", "list", "y")
+ENDL = ("half", "marks", "J2", "h", "fields", "list")
+KEYS = (0, 64, 128, 192)
 HALF = 56
 SPLIT = (20, 56, (26, 36), (26, 36))
 HC = (2, 1, 0, 1)

@@ -4,62 +4,57 @@ BIG = 2.0 ** 40
 KW, KK = 2.0 ** 17, 4096
 VOID = 128.0
 GATE = 8192.0
+ODD = 2559.5
 L, P, NV = 192, 2048, 5
+PV = P + 16
 CH = L // 16
 TURNS = pow(16, NV, L - 1)
-LAST = (64, 64)
-HI, LO, NH, NL, L2, ONE, C1, C2, C3 = range(9)
+HI, LO, NH, NL, SH, SL, L2, ONE, C1, C2, C3 = range(11)
 
 B16, F16, F32, I32, U16 = "bfloat16", "float16", "float32", "int32", "uint16"
 SCRATCH = {
-    "TXW": ("sbuf", [128, P + NV * L], B16), "XV": ("sbuf", [128, P], B16), "TFW": ("sbuf", [128, P + NV * L], B16),
-    "KF": ("sbuf", [128, L], F32), "KJ": ("sbuf", [128, L], F16), "FZ": ("sbuf", [128, L], B16),
-    "ZN": ("sbuf", [128, L], B16), "RR": ("sbuf", [128, L], F32), "WO": ("sbuf", [128, 12], F32), "LI": ("sbuf", [128, 12], F32),
-    "OWN": ("sbuf", [128, 12 * NV], F32), "OWU": ("sbuf", [128, 12 * NV], U16), "IO": ("sbuf", [128, 12 * NV], I32), "IK": ("sbuf", [128, 12], I32),
-    "CQ": ("sbuf", [128, 36], F32), "CA": ("sbuf", [128, 36], I32), "CB": ("sbuf", [128, 36], F32), "CC": ("sbuf", [128, 36], F32),
-    "CD": ("sbuf", [128, 36], F32), "LU": ("sbuf", [128, 24], U16), "LK": ("sbuf", [128, 24], U16),
-    "HJ": ("sbuf", [128, L], B16), "HC": ("sbuf", [128, L], B16), "KC": ("sbuf", [128, L], B16), "DT": ("sbuf", [128, 2 * 128], B16),
-    "THP": ("sbuf", [128, 4], F32), "W1": ("sbuf", [128, 128], B16),
-    "BB": ("sbuf", [128, P], B16), "B1": ("sbuf", [128, P], B16), "PL": ("sbuf", [128, P], I32),
+    "TXW": ("sbuf", [128, PV + NV * L], B16), "XV": ("sbuf", [128, P], B16), "TFW": ("sbuf", [128, PV + NV * L], B16),
+    "BBW": ("sbuf", [128, PV + L], B16), "B1": ("sbuf", [128, P], B16), "PL": ("sbuf", [128, P], I32),
     "IOT": ("sbuf", [128, P], F32), "BF1": ("sbuf", [128, P], F32), "ROW": ("sbuf", [128, P], F32), "RB": ("sbuf", [128, L], F32),
     "HX": ("sbuf", [128, L * 16], B16), "DX": ("sbuf", [128, L * 16], B16), "AX": ("sbuf", [128, L * 16], B16),
-    "KI": ("sbuf", [128, L], I32), "VT": ("sbuf", [128, 6, 2, 32], F16), "MS": ("sbuf", [128, L], F32), "RST": ("sbuf", [128, L], F32),
-    "L1": ("sbuf", [128, 12], U16),
-    "SI": ("sbuf", [128, L], I32), "Q1": ("sbuf", [128, L], I32), "FF": ("sbuf", [128, 2 * L], B16), "GF": ("sbuf", [128, L], B16),
-    "M1": ("sbuf", [128, 12], U16), "E2": ("sbuf", [128, L], B16), "AE": ("sbuf", [128, L], B16), "F2": ("sbuf", [128, L], I32),
-    "BR": ("sbuf", [128, L], B16), "YU": ("sbuf", [128, 12], U16), "BU": ("sbuf", [128, 12], U16),
-    "MM": ("sbuf", [128, 3 * 128], B16), "NN": ("sbuf", [128, 24 * 128], B16),
-    "MK": ("sbuf", [128, 128], B16), "UH": ("sbuf", [128, 128], B16), "UL": ("sbuf", [128, 128], B16), "VL": ("sbuf", [128, 128], B16),
-    "DI": ("sbuf", [128, 128], I32), "DH": ("sbuf", [128, 128], I32), "DL": ("sbuf", [128, 128], I32),
-    "DN": ("sbuf", [128, 128], I32), "DJ": ("sbuf", [128, 128], F32), "BS": ("sbuf", [128, L], B16),
+    "KI": ("sbuf", [128, L], I32), "KF": ("sbuf", [128, L], F32), "KJ": ("sbuf", [128, L], F16), "VT": ("sbuf", [128, 6, 2, 32], F16),
+    "MS": ("sbuf", [128, L], F32), "RST": ("sbuf", [128, L], F32), "ZN": ("sbuf", [128, L], B16), "RR": ("sbuf", [128, L], F32),
+    "WO": ("sbuf", [128, 12], F32), "LI": ("sbuf", [128, 12], F32), "L1": ("sbuf", [128, 12], U16),
+    "HJ": ("sbuf", [128, L], F32), "Q2": ("sbuf", [128, L], F16), "Q1": ("sbuf", [128, L], B16), "QO": ("sbuf", [128, L], F32),
+    "FF": ("sbuf", [128, 2 * L], B16), "GF": ("sbuf", [128, L], B16), "NR": ("sbuf", [128, L], F32), "M1": ("sbuf", [128, 12], U16),
+    "MX": ("sbuf", [128, L], B16), "HB": ("sbuf", [128, L], F16), "BR": ("sbuf", [128, L], B16), "BY": ("sbuf", [128, 24], U16),
+    "MM": ("sbuf", [128, 4 * 128], B16), "NN": ("sbuf", [128, 24 * 128], B16),
+    "YC": ("sbuf", [128, 12], B16), "NC": ("sbuf", [128, 24], B16), "UH": ("sbuf", [128, 128], B16), "UL": ("sbuf", [128, 128], B16), "VL": ("sbuf", [128, 256], B16),
     "ZU": ("sbuf", [128, 128], U16), "JU": ("sbuf", [128, 128], U16),
-    "AI": ("sbuf", [128, 2], I32), "AJ": ("sbuf", [128, 2], I32), "AK": ("sbuf", [128, 2], F32), "THR": ("sbuf", [128, 2], F32),
-    "T1K": ("sbuf", [128, 2], F32),
-    "BD": ("sbuf", [128, 128], B16), "ONES": ("sbuf", [128, 256], B16),
-    "IDP": ("sbuf", [128, 160], B16), "NI": ("sbuf", [128, 128], B16),
-    "BO": ("sbuf", [128, 128], B16), "NBO": ("sbuf", [128, 128], B16),
-    "IDW": ("sbuf", [128, 3 * 128], B16), "WNR": ("sbuf", [128, 128], B16), "IQ": ("sbuf", [128, 128], B16),
-    "WM": ("sbuf", [128, 128], B16), "WG": ("sbuf", [128, 128], B16), "WD": ("sbuf", [128, 8], B16), "WT": ("sbuf", [128, 3 * 128], B16),
+    "BS": ("sbuf", [128, L], B16), "AK": ("sbuf", [128, 2], F32), "SG": ("sbuf", [128, 12], F32), "LV": ("sbuf", [128, L], B16),
+    "ONES": ("sbuf", [128, 192], B16), "BD0": ("sbuf", [128, 144], B16), "BD1": ("sbuf", [128, 144], B16), "BD": ("sbuf", [128, 144], B16),
+    "IDP": ("sbuf", [128, 160], B16), "NI": ("sbuf", [128, 128], B16), "IDW": ("sbuf", [128, 4 * 128], B16), "IH": ("sbuf", [128, 256], B16),
+    "BO": ("sbuf", [128, 128], B16), "NBO": ("sbuf", [128, 128], B16), "WS": ("sbuf", [128, 128], B16), "WN": ("sbuf", [128, 128], B16),
+    "WNR": ("sbuf", [128, 128], B16), "W1": ("sbuf", [128, 128], B16), "WM": ("sbuf", [128, 128], B16), "SM": ("sbuf", [128, 144], B16),
+    "WH": ("sbuf", [128, 2 * 128], B16), "WC": ("sbuf", [128, 16], B16), "WT": ("sbuf", [128, 3 * 128], B16),
     "SU": ("sbuf", [128, 144], B16), "SY": ("sbuf", [128, 144], B16), "SN": ("sbuf", [128, 144], B16), "SF": ("sbuf", [128, 144], B16),
-    "PP": ("sbuf", [128, 4 * 160], B16), "CO": ("sbuf", [128, 32], F32), "EQ": ("sbuf", [128, 16], F32),
-    "IP": ("sbuf", [128, 2], I32), "IW": ("sbuf", [128, 2], I32), "I12": ("sbuf", [128, 12], I32),
-    "CF": ("sbuf", [128, 4 * 128], B16), "CW": ("sbuf", [128, 2 * 128], I32), "NXC": ("sbuf", [128, 128], I32),
-    "BMC": ("sbuf", [128, 12], I32), "BMw": ("sbuf", [128, 24], I32), "BMf": ("sbuf", [128, 24], B16), "BMR": ("sbuf", [128, L], B16),
-    "TH": ("sbuf", [128, 2], I32), "THw": ("sbuf", [128, 4], I32), "THf": ("sbuf", [128, 4], B16),
-    "TSR": ("sbuf", [128, 128], B16), "TSx": ("sbuf", [128, 128], B16), "TS0": ("sbuf", [128, 128], B16), "TS1": ("sbuf", [128, 128], B16),
-    "TMP": ("sbuf", [128, 5 * 128], B16),
+    "PP": ("sbuf", [128, 4 * 160], B16), "CO": ("sbuf", [128, 16], B16), "EQ": ("sbuf", [128, 24], B16), "IQ": ("sbuf", [128, 128], B16),
+    "KC": ("sbuf", [128, L], B16), "NOT1": ("sbuf", [128, 1], F32), "R2": ("sbuf", [128, 128], B16), "CL": ("sbuf", [128, L], B16), "S12": ("sbuf", [128, 12], F32),
+    "IP": ("sbuf", [128, 2], I32), "IW": ("sbuf", [128, 4], I32), "I12": ("sbuf", [128, 12], I32), "IK": ("sbuf", [128, 12], I32),
+    "IO": ("sbuf", [128, 12 * NV], I32), "OWN": ("sbuf", [128, 12 * NV], F32), "OWU": ("sbuf", [128, 12 * NV], U16), "LK": ("sbuf", [128, 24], U16),
+    "CQ": ("sbuf", [128, 12], F32), "CA": ("sbuf", [128, 12], I32), "CB": ("sbuf", [128, 12], F32), "CC": ("sbuf", [128, 12], F32),
+    "CD": ("sbuf", [128, 12], F32), "LU": ("sbuf", [128, 12], U16),
+    "CF": ("sbuf", [128, 7 * 256], B16), "NXC": ("sbuf", [128, 256], I32), "BMC": ("sbuf", [128, 12], I32),
+    "TH": ("sbuf", [128, 2], I32), "THw": ("sbuf", [128, 4], I32), "THf": ("sbuf", [128, 4], B16), "T1": ("sbuf", [128, 2 * L], B16),
+    "TSR": ("sbuf", [128, 128], B16), "TSx": ("sbuf", [128, 128], B16), "TSQ": ("sbuf", [128, 160], B16),
+    "DI": ("sbuf", [128, 128], I32), "DN": ("sbuf", [128, 128], I32), "DL": ("sbuf", [128, 128], F32), "DJ": ("sbuf", [128, 128], F32),
+    "DH": ("sbuf", [128, 128], F32),
     "HH": ("sbuf", [128, NV * L], B16), "KU": ("sbuf", [128, 2 * NV * L], U16),
 }
-ALIAS = {"FY": ("FF", 0, L), "FN": ("FF", L, L), "ID": ("IDP", 16, 128), "ON2": ("ONES", 0, L), "TX": ("TXW", 0, P), "TF": ("TFW", 0, P)}
+ALIAS = {"FY": ("FF", 0, L), "FN": ("FF", L, L), "ID": ("IDP", 16, 128), "ON2": ("ONES", 0, L), "TX": ("TXW", 0, P), "TF": ("TFW", 0, P),
+         "HC": ("TFW", PV, L), "BB": ("BBW", 0, P), "BU": ("BY", 0, 12), "YU": ("BY", 12, 12)}
 for _t in range(NV):
-    ALIAS["H%d" % _t] = ("TXW", P + L * _t, L)
-    ALIAS["TFM%d" % _t] = ("TFW", P + L * _t, L)
+    ALIAS["H%d" % _t] = ("TXW", PV + L * _t, L)
+    ALIAS["TFM%d" % _t] = ("TFW" if _t else "BBW", PV + L * _t, L)
     ALIAS["HS%d" % _t] = ("HH", L * _t, L)
     ALIAS["K%d" % _t] = ("KU", L * _t, L)
     ALIAS["KS%d" % _t] = ("KU", L * (NV + _t), L)
-for _k, _n in enumerate(("BD0", "BD1", "N3a", "N3b", "IH")):
-    ALIAS[_n] = ("TMP", 128 * _k, 128)
-for _k, _n in enumerate(("I16", "IM", "IVD")):
+for _k, _n in enumerate(("IM", "IVD", "IP2", "IM2")):
     ALIAS[_n] = ("IDW", 128 * _k, 128)
 for _t in range(8):
     SCRATCH["p%d" % _t] = ("psum", [128, 512], F32)
@@ -151,14 +146,7 @@ def make_emitter(g, T):
         for k in range(nd[0]):
             await_("G", "d%d" % k, 16)
 
-    tile = {}
-
-    def row_tile(j):
-        if 1 - j in tile:
-            await_("T", "sT", tile[1 - j])
-        tile[j] = count["T"] + 1
-
-    return ap, op, dma, arrive, deps, finish, row_tile
+    return ap, op, dma, arrive, deps, finish
 
 
 def R(name, c0=0, c1=None, st=1, p=slice(None)):
@@ -193,7 +181,7 @@ def rank_program(g, core, T, topo):
     nxt, prv = T.cores[(rank + 1) % n], T.cores[(rank - 1) % n]
     rid, pid = topo.addr(nxt, core)
     mask = topo.mask(core, nxt)
-    ap, op, dma, arrive, deps, finish, row_tile = make_emitter(g, T)
+    ap, op, dma, arrive, deps, finish = make_emitter(g, T)
 
     def tt(out, a, b, o):
         op("V", lambda e: e.tensor_tensor(ap(out), ap(a), ap(b), o), [a, b], [out])
@@ -219,23 +207,19 @@ def rank_program(g, core, T, topo):
     def scan(out, a, b, init, o0, o1):
         op("V", lambda e: e.tensor_tensor_scan(ap(out), ap(a), ap(b), init, o0, o1), [a, b], [out])
 
-    def act(out, a, f=Act.Copy, bias=0.0, scale=1.0):
-        op("A", lambda e: e.activation(ap(out), ap(a), f, bias=bias, scale=scale), [a], [out])
-
-    def act_scale(out, a, c):
-        op("A", lambda e: e.activation(ap(out), ap(a), Act.Copy, scale=ap(c)), [a, c], [out])
-
-    def act_bias(out, a, sc, b):
-        op("A", lambda e: e.activation(ap(out), ap(a), Act.Identity, bias=ap(b), scale=sc), [a, b], [out])
+    def act(out, a, f=Act.Copy, bias=0.0, scale=1.0, total=None, off=None):
+        rd = [a] + [s for s in (bias, scale, off) if isinstance(s, tuple)]
+        kw = {"bias": ap(bias) if isinstance(bias, tuple) else bias, "scale": ap(scale) if isinstance(scale, tuple) else scale}
+        if total:
+            kw["accum_out"] = ap(total)
+        src = ap(a).indirect(ap(off)) if off else ap(a)
+        op("A", lambda e: e.activation(ap(out), src, f, **kw), rd, [out, total] if total else [out])
 
     def vgather(out, win, off):
         op("V", lambda e: e.tensor_copy(ap(out), ap(win).indirect(ap(off))), [win, off], [out])
 
-    def agather(out, win, off, c=None):
-        if c is None:
-            op("A", lambda e: e.activation(ap(out), ap(win).indirect(ap(off)), Act.Copy), [win, off], [out])
-        else:
-            op("A", lambda e: e.activation(ap(out), ap(win).indirect(ap(off)), Act.Copy, scale=ap(c)), [win, off, c], [out])
+    def agather(out, win, off, c=1.0):
+        act(out, win, scale=c, off=off)
 
     def ttgather(out, win, off, b, o):
         op("V", lambda e: e.tensor_tensor(ap(out), ap(win).indirect(ap(off)), ap(b), o), [win, off, b], [out])
@@ -265,154 +249,152 @@ def rank_program(g, core, T, topo):
         g.remote_dma(ap(R("%s%d" % (name, t + 1))), ap(R("%sS%d" % (name, t))), T.sem["%s%d" % (sem, t + 1)], T.sem["loc"], pid, rid, mask)
         arrive("%s%d" % (name, t + 1), "%s%d" % (sem, t + 1), len(topo.engines(prv, core)))
 
-    e8 = slice(0, 8)
-    dma("C", ap(R("HS0")), T["hm"][:, :], [], [R("HS0")])
+    e8, h64 = slice(0, 8), slice(0, 64)
+    dma("C", ap(R("HC")), T["hm"][:, :], [], [R("HC")])
     dma("S", T["KI"][:, :], T["kt"][:, :], [], [R("KI")])
     dma("S", ap(R("TX")), T["xp"][:, :], [], [R("TX")])
-    dma("S", T["NXC"][:, :], T["nx"][:, :], [], [R("NXC")])
-    dma("S", T["BMC"][:, :], T["bm"][:, :], [], [R("BMC")])
+    dma("S", T["NXC"][h64, :], T["nx"][:, :], [], [R("NXC")])
     dma("C", T["TH"][e8, :], T["th"][:, :], [], [R("TH")])
 
-    PM, RM1, RM0, PMC, NZ, WF, PM8, NOT1, CY, CN, CMa, CMb, CMc, CG0, CG, CD, CV1, CV2 = (col("CO", j) for j in range(18))
-    later = []
+    PM, P12, P256, RM0, RM1, CF_, C2L, CL2, CG1, CS, CG = (col("CO", j) for j in range(11))
+    NOT1 = R("NOT1")
+    EQ = lambda f: col("EQ", f)
+    PAIR = lambda f: col("EQ", 16 + f // 2)
 
-    def gap(k):
-        for _ in range(min(k, len(later))):
-            later.pop(0)()
+    def scaled(q, out, a, c):
+        if q == "A":
+            act(out, a, scale=c)
+        else:
+            ts(out, a, c, Op.mult)
 
-    iota(R("IP"), [[0, 2]], 0, 1)
-    iota(R("I12"), [[16, 12]], 0, 0)
-    iota(R("IO"), [[L, NV], [1, 12]], P, 0)
-    iota(R("IK"), [[1, 6], [6, 2]], 0, 0)
-    iota(R("BD0"), [[0, 8], [1, 16]], 0, 0)
+    def cf(j):
+        return R("CF", 256 * j, 256 * j + 256, 1, h64)
+
+    def field(f, j):
+        local("S", row("BB", f, 0, P), cf(j))
+
     fill(R("ONES"), 1.0)
-    asel(R("BD1"), R("BD0"), [[-16, 8], [0, 16]], Op.is_ge, -1.0, 0, 1)
-    iota(R("IH"), [[1, 8], [0, 16]], 0, 0)
-    asel(R("BD"), R("BD1"), [[16, 8], [0, 16]], Op.is_ge, -1.0, 15, -1)
+    iota(R("IP"), [[0, 2]], 0, 1)
+    iota(R("BD0"), [[0, 9], [1, 16]], 0, 0)
     asel(R("IDP"), R("ONES", 0, 160), [[-1, 160]], Op.is_equal, 0.0, 16, 1)
-    ones = [blk("TF", j, 512) for j in range(4)]
-    ts(R("IW", 0, 1), R("IP", 0, 1), 15, Op.bitwise_and)
-    ts(R("IW", 1, 2), R("IP", 1, 2), 31, Op.bitwise_and)
-    act(R("RST"), R("ON2"), Act.Sigmoid, 0.0, -1000.0)
-    fill(ones.pop(), 1.0)
-    cp(PM, R("IW", 0, 1))
-    ts(PMC, R("IW", 0, 1), float(CH), Op.mult)
-    fill(ones.pop(), 1.0)
-    ts(R("CQ", 0, 12), R("I12"), PM, Op.add)
-    ts(R("CQ", 12, 24), R("IK"), PMC, Op.add)
-    ts(R("CQ", 24, 36), R("IO", 0, 12), PMC, Op.add, -float(P), Op.add)
-    ts(R("OWN"), R("IO"), PMC, Op.add)
-    fill(ones.pop(), 1.0)
-    times = ((0, 24, TURNS), (24, 36, 16 * TURNS % (L - 1)))
-    for a, b, m in times:
-        ts(R("CA", a, b), R("CQ", a, b), m / (L - 1.0), Op.mult, -0.502, Op.add)
-    for a, b, m in times:
-        ts(R("CC", a, b), R("CQ", a, b), float(m), Op.mult)
-    cp(R("LK"), R("CQ", 12, 36))
-    ts(R("CB"), R("CA"), 0.0, Op.max, 1.0 - L, Op.mult)
-    fill(ones.pop(), 1.0)
-    tt(R("CD"), R("CB"), R("CC"), Op.add)
-    ts(R("EQ"), R("BD0", 0, 16), PM, Op.is_equal)
-    ts(PM8, R("IW", 0, 1), 8.0, Op.mult)
-    tt(blk("CF", 1), R("BD0"), R("BD0"), Op.mult)
-    cp(R("LU"), R("CD", 0, 24))
-    local("S", row("TF", LO, 0, P), R("BD0"))
-    local("S", row("TF", L2, 0, P), blk("CF", 1))
-    agather(R("HC"), R("HS0"), R("LU", 0, 12))
-    two = ((CY, HI, 16.0 / KW, LO, 1.0 / KW), (CN, NH, 16.0 / KW, NL, 1.0 / KW), (CG0, ONE, GATE, C1, -GATE), (WF, HI, 1.0 / KW, LO, 128.0 / KW))
-    for j, (c, f, w, f2, w2) in enumerate(two):
-        ts(col("CO", 24 + j), col("EQ", f), w, Op.mult)
-    ha = doubling("HC", RC, NX)
-    act(R("NI"), R("ID"), scale=-1.0)
-    for j, (c, f, w, f2, w2) in enumerate(two):
-        for _ in range((2, 0, 1, 1)[j]):
-            act(*ha.pop(0)[:2])
-        act_bias(c, col("EQ", f2), w2, col("CO", 24 + j))
-    ts(blk("CF", 0), R("IH"), PM8, Op.add)
-    local("S", row("TF", HI, 0, P), blk("CF", 0))
-    vgather(R("K0"), R("KI"), R("LU", 0, 12))
-    hx = doubling("HC", 0, RC)
-    cp(*hx[0][:2])
-    cp(*hx[1][:2])
-    vgather(R("KJ"), R("KI"), R("LU", 12, 24))
-    cp(*hx[2][:2])
-    ts(R("OWN", 0, 12), R("CD", 24, 36), float(P), Op.add)
-    ts(R("THw", 0, 2, 1, e8), R("TH", 0, 2, 1, e8), 4032, Op.bitwise_and)
-    ts(R("THw", 2, 4, 1, e8), R("TH", 0, 2, 1, e8), 63, Op.bitwise_and)
-    cp(R("VT", 16, 17), R("RST", 1, 13))
-    cp(*hx[3][:2])
-    turn(R("VT", 0, 16), R("KJ"))
-    cp(R("THf", 0, 4, 1, e8), R("THw", 0, 4, 1, e8))
-    ts(R("SU", 0, 128), R("BD"), 15.0, Op.is_equal, KW, Op.mult)
-    fill(R("SU", 128, 144), 0.0)
-    cp(*hx[4][:2])
-    cp(R("OWU"), R("OWN"))
-    ts(RM1, R("IW", 1, 2), 16.0, Op.is_ge)
-    ts(RM0, R("IW", 1, 2), 16.0, Op.is_lt)
-    fill(R("RST", 0, L, 16), BIG)
-    agather(R("H0"), R("HS0"), R("LK", 12, 24))
-    act(*ha.pop(0)[:2])
+    iota(R("IK"), [[1, 6], [6, 2]], 0, 0)
+    asel(R("BD1"), R("BD0"), [[-16, 9], [0, 16]], Op.is_ge, -1.0, 0, 1)
     iota(R("KC"), [[0, 12], [KK, 16]], KK, 0)
+    asel(R("BD"), R("BD1"), [[16, 9], [0, 16]], Op.is_ge, -1.0, 15, -1)
+    iota(R("IH", p=h64), [[16, 16], [0, 16]], 0, 0)
+    iota(cf(6), [[0, 16], [1, 16]], 0, 0)
     asel(R("TSx", p=e8), R("ONES", 0, 128, p=e8), [[1, 128]], Op.is_ge, 0.0, 0, -16)
+    iota(R("IO"), [[L, NV], [1, 12]], PV, 0)
     asel(R("TSR", p=e8), R("TSx", p=e8), [[-1, 128]], Op.is_ge, 0.0, 15, 16)
-    iota(R("IQ"), [[1, 128]], 0, 0)
+    iota(R("I12"), [[16, 12]], 0, 0)
+    iota(R("IQ"), [[16, 128]], 0, 0)
+    asel(R("TSQ", p=e8), R("ONES", 0, 160, p=e8), [[-1, 160]], Op.is_equal, 0.0, 16, 16)
     for r in range(16):
         gcopy(blk("XV", r), R("TX", r, P, 16), 128)
+    iota(R("S12"), [[1024, 2], [-64, 6]], 1 - 64, 0)
+    iota(R("CL"), [[0, L]], int(-16 * KW), 0)
 
-    def successors_and_bookmarks():
-        ts(R("CW", 0, 128), R("NXC"), 4, Op.logical_shift_right)
-        ts(R("CW", 128, 256), R("NXC"), 15, Op.bitwise_and)
-        cp(R("BU"), R("BMC"))
-        ts(CMa, col("EQ", LO), 2 * GATE, Op.mult)
-        ts(CMb, col("EQ", C1), -GATE, Op.mult)
-        ts(NOT1, col("EQ", ONE), -1.0, Op.mult, 1.0, Op.add)
-        cp(R("CF", 256, 512), R("CW"))
-        local("S", row("TF", NH, 0, P), blk("CF", 2))
-        local("S", row("TF", NL, 0, P), blk("CF", 3))
-        dma("S", T["PL"][:, :], T["pl"][:, :], [], [R("PL")])
-        local("S", R("BB"), R("TF", 0, P))
-        local("S", R("VL"), row("XV", 0, 0, P))
-
-    def constant_sums():
-        for r in range(16):
-            mm(R("p6", 256 + r, 384, 16), R("TF", r, P, 16), R("WD"))
-
-    def constants_for_keys():
-        ts(CMc, col("EQ", L2), -GATE, Op.mult, CG0, Op.add)
-        ts(R("WD"), R("BO", 0, 128, 16), CD, Op.mult)
-        ts(blk("WT", 0), R("BD"), 0.0, Op.max, CMa, Op.mult)
-        ts(blk("WT", 1), blk("CF", 1), CMb, Op.mult, CMc, Op.add)
-        ts(CV1, col("EQ", C2), col("THP", 1), Op.mult, CG0, Op.add)
-        constant_sums()
-        act_scale(R("SN"), R("SU"), CN)
-        act(R("NBO"), R("BO"), scale=-1.0)
-        lists("p7", 0, "SY", "TF", 0, 128, True, False)
-        later.extend([
-            lambda: act_scale(R("W1"), R("BO"), col("EQ", ONE)),
-            lambda: act(R("IM"), R("ID"), scale=-33.0),
-            lambda: act(R("IVD"), R("ID"), scale=VOID),
-            lambda: act_scale(R("SF"), R("SU"), WF),
-            lambda: agather(R("TFM0"), R("TF"), R("BU"), NOT1),
-            lambda: ts(CG, col("EQ", C3), col("THP", 3), Op.mult, CV1, Op.add),
-            lambda: act_scale(R("WG"), R("BO"), CG),
-            lambda: tt(blk("WT", 2), blk("WT", 1), R("BO"), Op.mult),
-            lambda: ts(R("DI"), R("p6", 256, 384), -1.0, Op.mult, 4095.0, Op.add),
-            lambda: tt(R("WM"), blk("WT", 0), blk("WT", 2), Op.add),
-        ])
+    hv, ha = doubling("HC", 0, RC), doubling("HC", RC, NX)
+    once = {
+        "RST": lambda: act(R("RST"), R("ON2"), Act.Sigmoid, 0.0, -1000.0),
+        "IW": lambda: (ts(R("IW", 0, 1), R("IP", 0, 1), 15, Op.bitwise_and), ts(R("IW", 1, 2), R("IP", 1, 2), 16, Op.bitwise_and),
+                       ts(R("IW", 2, 3), R("IP", 1, 2), 7, Op.bitwise_and)),
+        "PM": lambda: (cp(PM, R("IW", 0, 1)), ts(P12, R("IW", 0, 1), float(CH), Op.mult), ts(P256, R("IW", 2, 3), 256.0, Op.mult)),
+        "RM": lambda: (ts(RM0, R("IW", 1, 2), 0.0, Op.is_equal), ts(RM1, R("IW", 1, 2), 16.0, Op.is_equal)),
+        "EQ": lambda: ts(R("EQ", 0, 16), R("BD0", 0, 16), PM, Op.is_equal),
+        "PAIR": lambda: tt(R("EQ", 16, 24), R("EQ", 0, 16, 2), R("EQ", 1, 16, 2), Op.add),
+        "L2": lambda: (act(cf(1), cf(6), Act.Square), field(LO, 6), field(L2, 1)),
+        "R2": lambda: act(R("R2"), R("BD0", 0, 128), Act.Square),
+        "HI": lambda: (ts(cf(0), R("IH", p=h64), P256[:4] + (h64,), Op.add), field(HI, 0)),
+        "NH": lambda: (ts(cf(2), R("NXC", p=h64), 3.0 * 2 ** 26, Op.add, -3.0 * 2 ** 26, Op.add), field(NH, 2)),
+        "NL": lambda: (tt(cf(3), R("NXC", p=h64), cf(2), Op.subtract), field(NL, 3)),
+        "S": lambda: [mm(R("p3", 0, 256, 1, h64), R("SU", 15 - 2 * m, 143 - 2 * m, 2), blk("TX", m, 256), m == 0, m == 7) for m in range(8)],
+        "SH": lambda: (act(cf(4), R("p3", 0, 256, 1, h64)), field(SH, 4)),
+        "SL": lambda: (tt(cf(5), R("p3", 0, 256, 1, h64), cf(4), Op.subtract), field(SL, 5)),
+        "bm": lambda: dma("S", T["BMC"][:, :], T["bm"][:, :], [], [R("BMC")]),
+        "pl": lambda: dma("S", T["PL"][:, :], T["pl"][:, :], [], [R("PL")]),
+        "VL0": lambda: local("S", R("VL", p=h64), row("XV", 0, 0, P)),
+        "K0": lambda: cp(R("K0"), R("KI")),
+        "LK": lambda: ts(R("LK", 0, 12), R("IK"), P12, Op.add),
+        "LH": lambda: ts(R("LK", 12, 24), R("IO", 0, 12), P12, Op.add, -float(PV), Op.add),
+        "KJ": lambda: vgather(R("KJ"), R("KI"), R("LK", 0, 12)),
+        "VT0": lambda: cp(R("VT", 16, 17), R("RST", 1, 13)),
+        "BIG": lambda: fill(R("RST", 0, L, 16), BIG),
+        "NI": lambda: act(R("NI"), R("ID"), scale=-1.0),
+        "SU": lambda: ts(R("SU"), R("BD"), 15.0, Op.is_equal, KW, Op.mult),
+        "SY": lambda: ts(R("SY"), R("BD"), 15.0, Op.is_equal, PAIR(HI), Op.mult),
+        "SN": lambda: ts(R("SN"), R("BD"), 15.0, Op.is_equal, PAIR(NH), Op.mult),
+        "CF": lambda: ts(CF_, PM, 128.0 - 1.0 / 16, Op.mult, 1.0 / 16, Op.add),
+        "SF": lambda: scaled("V", R("SF"), R("SY"), CF_),
+        "TH": lambda: (ts(R("THw", 0, 2, 1, e8), R("TH", 0, 2, 1, e8), 4032, Op.bitwise_and), ts(R("THw", 2, 4, 1, e8), R("TH", 0, 2, 1, e8), 63, Op.bitwise_and)),
+        "THf": lambda: cp(R("THf", 0, 4, 1, e8), R("THw", 0, 4, 1, e8)),
+        "T1": lambda: [ts(R("T1", L * j, L * j + L, 1, e8), R("ON2", p=e8), R("THf", 2 * j, 2 * j + 1, 1, e8), Op.mult, -KW, Op.mult) for j in range(2)],
+        "t1": lambda: thresholds(),
+        "t2": lambda: [mm(col("p5", 0), R("TSQ", 16 - f, 144 - f, 1, e8), R("THf", j, j + 1, 1, e8), f == C2, f == C3) for f, j in ((C2, 1), (C3, 3))],
+        "PP": lambda: [scaled("V", blk("PP", u, 160), R("IDP"), RM1 if u else RM0) for u in range(2)],
+        "PN": lambda: ts(R("PP", 320, 640), R("PP", 0, 320), -1.0, Op.mult),
+        "OWN": lambda: (ts(R("OWN", 12), R("IO", 12), P12, Op.add), ts(R("OWN", 0, 12), R("I12"), PM, Op.add, float(PV), Op.add)),
+        "OWU": lambda: ts(R("OWU"), R("IO"), P12, Op.add),
+        "void column": lambda: (fill(R("TXW", P, PV), GATE), fill(R("TFW", P, PV), 1.0)),
+        "H0": lambda: act(R("H0"), R("HJ"), Act.Identity, -ODD),
+        "BU0": lambda: cp(R("BU"), R("BMC")),
+        "NOT1": lambda: ts(NOT1, EQ(ONE), -1.0, Op.mult, 1.0, Op.add),
+        "BO": lambda: ts(R("BO"), R("BD", 0, 128), 0.0, Op.is_ge),
+        "CG1": lambda: ts(CG1, EQ(ONE), -GATE / 2, Op.mult, PAIR(NH), Op.add),
+        "SM": lambda: ts(R("SM"), R("BD"), 15.0, Op.is_equal, CG1, Op.mult),
+        "WNR": lambda: scaled("V", R("WNR"), R("BO"), PAIR(NH)),
+        "CM": lambda: (ts(C2L, EQ(LO), 2.0, Op.mult), tt(CL2, EQ(L2), EQ(ONE), Op.subtract)),
+        "WT": lambda: (ts(blk("WT", 0), R("BD", 0, 128), 0.0, Op.max, C2L, Op.mult), ts(blk("WT", 1), R("R2"), EQ(C1), Op.mult, CL2, Op.add)),
+        "WT2": lambda: tt(blk("WT", 2), blk("WT", 1), R("BO"), Op.mult),
+        "WM": lambda: tt(R("WM"), blk("WT", 0), blk("WT", 2), Op.subtract),
+        "WH": lambda: [scaled("V", blk("WH", u), R("WM"), RM1 if u else RM0) for u in range(2)],
+        "CS": lambda: ts(CS, PAIR(SH), -1.0 / KW, Op.mult),
+        "CG": lambda: ts(CG, col("p5", 0), -1.0, Op.mult, CS, Op.add),
+        "WS": lambda: scaled("V", R("WS"), R("BO"), CG),
+        "WC": lambda: (cp(R("WC", 0, 8), R("ID", HI, 128, 16)), ts(R("WC", 8, 16), R("BO", 0, 128, 16), CG, Op.mult)),
+        "WN": lambda: scaled("A", R("WN"), R("BO"), -1.0),
+        "NBO": lambda: scaled("A", R("NBO"), R("BO"), 2.0),
+        "W1": lambda: scaled("V", R("W1"), R("BO"), EQ(ONE)),
+        "IM": lambda: scaled("A", R("IM"), R("ID"), -33.0),
+        "IVD": lambda: scaled("A", R("IVD"), R("ID"), VOID),
+        "IP2": lambda: scaled("A", R("IP2"), R("ID"), 0.5),
+        "IM2": lambda: scaled("A", R("IM2"), R("ID"), -0.5),
+        "nx - p": lambda: (mm(R("p6", 256, 384), R("IQ"), R("NI"), True, False), mm(R("p6", 256, 384), R("NI"), R("BD0", 0, 128), False, False),
+                           [mm(R("p6", 256 + r, 384, 16), R("BB", r, P, 16), R("WNR", 0, 128, 16), False, r == 15) for r in range(16)]),
+        "DI": lambda: ts(R("DI"), R("p6", 256, 384), -1.0, Op.mult, 4095.0, Op.add),
+        "DN": lambda: ts(R("DN"), R("DI"), 31, Op.bitwise_and),
+        "DL": lambda: ts(R("DL"), R("DN"), 65.0, Op.add),
+        "DJ": lambda: act(R("DJ"), R("DL"), Act.Identity, 4095.0, 33.0),
+        "DH": lambda: tt(R("DH"), R("DJ"), R("DI"), Op.subtract),
+    }
+    for j in range(4):
+        once["ones%d" % j] = lambda j=j: fill(blk("BBW", j, PV // 4), 1.0)
+    for j in range(5):
+        once["hv%d" % j] = lambda j=j: cp(*hv[j][:2])
+        once["ha%d" % j] = lambda j=j: act(*ha[j][:2])
+    later = [
+        lambda: ts(R("CQ"), R("I12"), PM, Op.add),
+        lambda: ts(R("CA"), R("CQ"), TURNS / (L - 1.0), Op.mult, -0.502, Op.add),
+        lambda: ts(R("CC"), R("CQ"), float(TURNS), Op.mult),
+        lambda: ts(R("CB"), R("CA"), 0.0, Op.max, 1.0 - L, Op.mult),
+        lambda: tt(R("CD"), R("CB"), R("CC"), Op.add),
+        lambda: cp(R("LU"), R("CD")),
+    ]
 
     banks = [("p%d" % (1 + j), AB[j], AB[j + 1]) for j in range(len(AB) - 1)]
 
     def thresholds():
         for j in range(2):
-            mm(R("p0", 0, L), blk("DT", j), R("ON2"), False, False)
+            mm(R("p0", 0, L), R("TSR", p=e8), R("T1", L * j, L * j + L, 1, e8), False, False)
 
     def preload(t):
         mm(R("p0", 0, L), R("ID"), R("KC"), True, False)
         if t:
+            mm(R("p0", 0, L), R("NI"), R("LV"), False, False)
             thresholds()
 
-    def less_h(t, js):
-        for bank, a, b in banks[js]:
+    def less_h(t):
+        for bank, a, b in banks:
             for k in range(16):
                 mm(R(bank, k, 16 * (b - a), 16), R("NI"), R("H%d" % t if t else "HC", a, b), k == 0, False)
 
@@ -429,249 +411,217 @@ def rank_program(g, core, T, topo):
                     c = 160 * (2 * w + u) + 16 - 16 * (s - u)
                     mm(R("p4", 256 + 96 * u, 352 + 96 * u), R("PP", c, c + 128), R("VT", w, w + 16, -1 - s), u + s + w == 0, u + s + w == 3)
 
-    preload(0)
-    less_h(0, slice(None))
+    def lanes(bank, c0, c1, src, ws, start=False, stop=False, parts=(0, 1, 2)):
+        for j in parts:
+            n = len(range(*ws[j][1:4]))
+            o, a = (R(bank, c1, c1 + n, 1, slice(64 * j - 64, 64 * j)), R(src, 128, L)) if j else (R(bank, c0, c0 + n), R(src, 0, 128))
+            mm(o, a, ws[j], start and (stop or j == 0), stop and (start or j == 0))
+
+    def one(W, c=0):
+        return R(W, c, 128, 16), R(W, c, 128, 32), R(W, 16 + c, 128, 32)
+
+    low = (R("WM"), blk("WH", 0), blk("WH", 1))
+    both = (R("WC"), R("WC", 0, 16, 2), R("WC", 1, 16, 2))
+
+    def one_hot(w, js):
+        for j in js:
+            if w:
+                ts(blk("NN", 12 + j), R("IQ"), col("NC", j + j // 8 * 8), Op.is_equal, col("NC", j + 8 + j // 8 * 4), Op.is_gt)
+            else:
+                ts(blk("NN", j), R("IQ"), col("YC", j), Op.is_equal)
+
+    done = []
+
+    def products(w, js):
+        for j in js:
+            c, m = (16 * j, 16) if j < 8 else (32 * j - 256, 32)
+            done.append(j)
+            a = 256 * w + 128 * (j // 8) + c
+            mm(R("p0", c, c + m), blk("NN", 12 * w + j), R("MM", a, a + m), len(done) % 24 == 1, len(done) % 24 == 0)
+
+    def own_h(t):
+        win, off = (R("TXW", 0, PV + L * (t + 1)), blk("OWU", t, 12)) if t else (R("HC"), R("LK", 12, 24))
+        act(R("HJ"), win, Act.Identity, ODD, off=off)
+
+    once["keys0"], once["less h0"] = lambda: preload(0), lambda: less_h(0)
+    for what in START:
+        once[what]()
+    last_sum = [s for s in STEP1 if s[0] == "sum"][-1]
     for t in range(NV):
         last = t == NV - 1
-        K, WIN = "K%d" % t, P + L * (t + 1)
-        if t == 0:
-            mm(R("p5", 0, 4), R("TSR", p=e8), R("THf", 0, 4, 1, e8))
-        for j, (what, a, b) in enumerate(STEP1):
-            d, x = R("DX", 16 * a, 16 * b), R("AX", 16 * a, 16 * b)
-            if what == "less h":
-                ttgather(d, R("TX"), R(K, a, b), R("HX", 16 * a, 16 * b), Op.subtract)
-            elif what == "plain":
-                agather(d, R("TX"), R(K, a, b))
-                for bank, c, e in banks:
-                    if a < e <= b:
-                        mm(R(bank, 0, 16 * (e - c)), R("ID"), R("DX", 16 * c, 16 * e), False, True)
-            elif what == "relu":
-                ts(x, d, -2.0, Op.mult, 0.0, Op.max)
-            elif what == "abs":
-                act(x, d if a < NX else R(banks[AB.index(a)][0], 0, 16 * (b - a)), Act.Abs)
-            elif what == "sum d":
-                sums("DX", a, b)
-            elif what == "sum":
-                sums("AX", a, b, "sum" not in [w for w, _, _ in STEP1[j + 1:]])
-            elif what == "misses" and t:
-                agather(R("TFM%d" % t), R("TF"), R("BU"), NOT1)
-            elif what == "misses":
-                act_scale(R("SY"), R("SU"), CY)
-            elif what == "tile" and t:
-                cp(R("KF"), R(K))
-            elif what == "reorder" and t:
-                agather(R("KJ"), R("KF"), R("LK", 0, 12))
-            elif what == "reorder":
-                for u in range(2):
-                    act_scale(blk("PP", u, 160), R("IDP"), RM1 if u else RM0)
-            elif what == "turn" and t == 0:
-                ts(R("PP", 320, 640), R("PP", 0, 320), -1.0, Op.mult)
-            elif what == "turn" and t:
-                turn(R("VT", 0, 16), R("KJ"))
-            elif what == "steps":
-                steps_to_keys()
-            elif what == "thresholds" and t == 0:
-                cp(R("THP"), R("p5", 0, 4))
-                successors_and_bookmarks()
-                for w in range(2):
-                    ts(blk("DT", w), R("ID"), col("THP", 2 * w), Op.mult, -KW, Op.mult)
-                thresholds()
-        agather(R("HJ"), R("TXW", 0, WIN), blk("OWU", t, 12))
-        if t == 0:
-            ts(CD, CN, CY, Op.subtract, KW, Op.mult)
-            ts(R("BO"), R("BD"), 0.0, Op.is_ge)
-        if t:
-            lists("p7", 0, "SY", "TF", 0, 128, True, False)
-        else:
-            constants_for_keys()
-            gap(4)
-        halves = list(zip(KEYS, KEYS[1:]))
-        for a, b in halves:
-            scan(R("MS", a, b), R("RST", a, b), R("p0", a, b), 0.0, Op.add, Op.min)
-        gap(1)
-        for a, b in halves:
-            tt(R("ZN", a, b), R("p0", a, b), R("MS", a, b), Op.not_equal)
-        tt(R("WO"), R("MS", 15, L, 16), blk("OWN", t, 12), Op.min)
-        for a, b in halves:
-            scan(R("RR", a, b), R("ZN", a, b), R("p4", 256 + a, 256 + b), 0.0, Op.mult, Op.add)
-        gap(1)
-        tt(R("LI"), R("RR", 15, L, 16), R("WO"), Op.max)
-        gap(1)
-        cp(R("L1"), R("LI"))
-        gap(1)
-
-        ttgather(R("SI"), R("TXW", 0, WIN), R("L1"), R("HJ"), Op.add)
-        agather(R("FY"), R("TFW", 0, WIN), R("L1"))
-        gap(3)
-        if t == 0:
-            ts(R("DN"), R("DI"), 31, Op.bitwise_and)
-        ts(R("Q1"), R("SI"), 1, Op.arith_shift_right)
-
-        def lanes(bank, c0, src, W, c, st, start=False, stop=False, parts=(0, 1, 2)):
-            n = 128 // st
-            for j in parts:
-                if j == 0:
-                    o, a, w = R(bank, c0, c0 + n), R(src, 0, 128), R(W, c, 128, st)
-                else:
-                    o, a, w = R(bank, c0 + n, c0 + n + n // 2, 1, slice(64 * j - 64, 64 * j)), R(src, 128, L), R(W, 64 * j - 64 + c, 64 * j, st)
-                mm(o, a, w, start and (stop or j == 0), stop and (start or j == 0))
-
-        def one_hot(w, js):
-            for j in js:
-                ts(blk("NN", 12 * w + j), R("IQ"), col("p5", j) if w else col("p4", j) if j < 8 else col("p3", 64 + j), Op.is_equal)
-
-        def positive(w, a, b):
-            act(R("MM", L * w + a, L * w + b), R("p%d" % (1 + w), a, b), Act.Relu, 8192.0, 16384.0)
-
-        def products(w, gs, part=0):
-            for gg in gs:
-                j, p = (gg, slice(None)) if part == 0 else (8 + gg % 4, slice(64 * part - 64, 64 * part))
-                if part:
-                    row_tile(part - 1)
-                mm(R("p0", 16 * gg, 16 * gg + 16), R("NN", 128 * (12 * w + j), 128 * (12 * w + j + 1), 1, p), R("MM", L * w + 16 * j, L * w + 16 * j + 16, 1, p),
-                   w + j == 0, w == 1 and j == 7)
-
-        lanes("p4", 0, "FY", "ID", HI, 16, True, True, (0,))
-        lists("p3", 16, "SN", "FY", 0, 12)
-        lanes("p1", 0, "FY", "WM", 0, 1, True, True)
-        lanes("p2", 0, "FY", "WG", 0, 1, True)
-        mm(R("p6", 0, L), R("WG"), R("FY"), True, False)
-        one_hot(0, range(N0))
-        cp(R("M1"), R("p3", 16, 28))
-        lanes("p3", 64, "FY", "ID", HI, 16, True, True, (1, 2))
-        one_hot(0, range(N0, 8))
-        positive(0, 0, 128)
-        products(0, range(8))
-        ttgather(R("E2"), R("TX", 0, P), R("M1"), R("Q1"), Op.subtract)
-        agather(R("FN"), R("TF", 0, P), R("M1"))
-        positive(0, 128, L)
-        one_hot(0, range(8, N2))
-        if t == 0:
-            ts(R("DJ"), R("DN"), 33.0, Op.mult, 33.0 * 65 + 4095, Op.add)
-        ts(R("AE"), R("E2"), -2.0, Op.mult, 0.0, Op.max)
-        one_hot(0, range(N2, 12))
-        ts(R("F2"), R("E2"), 0.5, Op.mult, -0.25, Op.add)
-        lanes("p5", 0, "FN", "ID", HI, 16, True, True)
-        lanes("p2", 0, "FN", "WM", 0, 1)
-        lanes("p2", 0, "E2", "NBO", 0, 1)
-        lanes("p2", 0, "AE", "NBO", 0, 1, False, True, (1, 2, 0))
-        positive(1, 128, L)
-        positive(1, 0, 128)
-        for src in ("E2", "AE"):
-            mm(R("p6", 0, L), R("NBO"), R(src), False, src == "AE")
-        products(0, range(4), 1)
-        mm(R("p4", 256, 256 + L), R("ID"), R("FN"), True, False)
-        mm(R("p4", 256, 256 + L), R("NI"), R("FY"), False, True)
-        products(0, range(4, 8), 2)
-        one_hot(1, range(8, 12))
-        one_hot(1, range(8))
-        if t == 0:
-            tt(R("DH"), R("DJ"), R("DI"), Op.subtract)
-            ts(R("DL"), R("DN"), 65.0, Op.add)
-        products(1, range(4, 8), 2)
-        products(1, range(6))
-        products(1, range(4), 1)
-        products(1, range(6, 8))
-        if not last:
-            mm(R("p2", 256, 256 + L), R("W1"), R("FY"))
-            lists("p3", 32, "SY", "FY", 0, 12, True, False)
-        act(R("BR"), R("p6", 0, L), Act.Sigmoid, 500.0, 1000.0)
-        if not last:
-            op("A", lambda e: e.activation(ap(R("BS")), ap(R("p2", 256, 256 + L)), Act.Copy, accum_out=ap(col("AK", 0))), [R("p2", 256, 256 + L)], [R("BS"), col("AK", 0)])
-        for what in (ENDL if last else END):
-            if what == "half":
-                tt(R("p5", 256, 256 + L), R("F2"), R("BR"), Op.mult)
-            elif what == "h":
-                tt(R("HS%d" % t), R("p5", 256, 256 + L), R("Q1"), Op.add)
-                if not last:
-                    send(t, "H", "ha")
-            elif what == "fields":
-                tt(R("GF"), R("p4", 256, 256 + L), R("BR"), Op.mult)
-            elif what == "y":
-                lists("p3", 32, "SY", "GF", 0, 12, False, True)
-            elif what == "marks":
-                tt(R("UH"), R("p0", 0, 128), R("DH"), Op.min)
-                tt(R("UL"), R("p0", 0, 128), R("DL"), Op.min)
-            elif what == "J2":
-                for src, w in (("UH", "ID"), ("UL", "IM")):
-                    mm(R("p7", 0, 128), R(src), R(w), False, src == "UL")
-            elif what == "void":
-                mm(R("p1", 0, 128), R("UL"), R("IVD"), True, False)
-                mm(R("p1", 0, 128), R("ID"), R("VL"), False, True)
-            elif what == "list":
-                cp(R("ZU"), R("p7", 0, 128))
-        if last:
-            dma("S", T["yh"][:, :], ap(R("HS%d" % t)), [R("HS%d" % t)], [])
-            mm(R("p6", 0, L), R("WNR"), R("FY"), True, False)
-            mm(R("p6", 0, L), R("WNR"), R("GF"), False, True)
-            s1, s2 = LAST
-            agather(R("BF1", 16 * s1, P), R("IOT"), R("ZU", s1, 128))
-            vgather(R("BF1", 0, 16 * s1), R("IOT"), R("ZU", 0, s1))
-            cp(R("RB"), R("p6", 0, L))
-            dma("S", T["yb"][:, :], ap(row("RB", 0, 0, L)), [R("RB")], [])
-            agather(R("ROW", 16 * s2, P), R("BF1"), R("ZU", s2, 128))
-            vgather(R("ROW", 0, 16 * s2), R("BF1"), R("ZU", 0, s2))
-            dma("S", T["yj"][:, :], ap(row("ROW", 0, 0, P)), [R("ROW")], [])
-            break
-        act(R("VL"), R("p1", 0, 128))
-        local("S", row("XV", 0, 0, P), R("VL"))
-        s0, s1, s2, s3 = SPLIT
-        agather(R("B1", 16 * s1, P), R("BB"), R("ZU", s1, 128))
-        lists("p4", 0, "SN", "FY", 0, 12, True, False)
-        lists("p4", 0, "SN", "GF", 0, 12, False, True)
-        if t == 0:
-            ts(R("WNR"), R("BO"), CN, Op.mult, KW, Op.mult)
-        cp(col("AI", 0), col("AK", 0))
-        vgather(R("B1", 0, 16 * s0), R("BB"), R("ZU", 0, s0))
-        ts(col("AJ", 0), col("AI", 0), 31, Op.bitwise_and)
-        cp(R("YU"), R("p3", 32, 44))
-        vgather(R("B1", 16 * s0, 16 * s1), R("BB"), R("ZU", s0, s1))
-        vgather(R("KS%d" % t), R("PL"), R("YU"))
-        send(t, "K", "ka")
-        ts(col("AK", 1), col("AJ", 0), col("THP", 2), Op.add, -KW, Op.mult)
-        cp(R("BU"), R("p4", 0, 12))
-        h1 = "H%d" % (t + 1)
-        for dst, src, width in doubling(h1, GK, NX):
-            gcopy(dst, src, width)
+        K, WIN, HS, h1 = "K%d" % t, PV + L * (t + 1), R("HS%d" % t), "H%d" % min(t + 1, NV - 1)
+        TFW = "TFW" if t else "BBW"
         hx = doubling(h1, 0, GK)
-
-        def copies(m):
-            for _ in range(min(m, len(hx))):
-                cp(*hx.pop(0)[:2])
-
-        parts = ((0, "p5", 0, HALF), (1, "p3", HALF, 128))
-        for j, bank, q, e in parts:
-            vgather(R("TF", 16 * q, 16 * (q + s2[j])), R("B1"), R("ZU", q, q + s2[j]))
-            agather(R("TF", 16 * (q + s2[j]), 16 * e), R("B1"), R("ZU", q + s2[j], e))
-            lists(bank, 0, "SF", "TF", q, e)
-        act_scale(blk("DT", 1), R("ID"), col("AK", 1))
-        for j, bank, q, e in parts:
-            copies(HC[2 * j])
-            cp(R("JU", q, e), R(bank, 0, e - q))
-            copies(HC[2 * j + 1])
-            vgather(R("TX", 16 * q, 16 * (q + s3[j])), R("XV"), R("JU", q, q + s3[j]))
-            agather(R("TX", 16 * (q + s3[j]), 16 * e), R("XV"), R("JU", q + s3[j], e))
-        preload(t + 1)
-        less_h(t + 1, slice(None))
-        copies(16)
-        if t == 1:
-            iota(R("IOT"), [[1, P]], 0, 0)
+        part = lambda a: ("p5", "p4", "p3")[PARTS.index(a)]
+        steps = {
+            "tile": lambda: t and (gcopy(R("KF"), R(K), L), t == 1 and iota(R("IOT"), [[1, P]], 0, 0)),
+            "reorder": lambda: t and agather(R("KJ"), R("KF"), R("LK", 0, 12)),
+            "turn": lambda: turn(R("VT", 0, 16), R("KJ")),
+            "steps": steps_to_keys,
+            "own h": lambda: own_h(t),
+            "misses": lambda: agather(R("TFM%d" % t), R("TF" if t else "BB"), R("BU"), NOT1),
+            "J": lambda: lists("p7", 0, "SY", "TF", 0, 128, True, False) if t else
+            (mm(R("p7", 0, 128), R("ID"), R("IQ"), True, False), mm(R("p7", 0, 128), R("BD0", 0, 128), R("ID"), False, False)),
+            "own": lambda: tt(R("WO"), R("MS", 15, L, 16), blk("OWN", t, 12), Op.min),
+            "LI": lambda: tt(R("LI"), R("RR", 15, L, 16), R("WO"), Op.max),
+            "L1": lambda: cp(R("L1"), R("LI")),
+            "late": lambda: t and later and later.pop(0)(),
+            "Q2": lambda: ttgather(R("Q2"), R("TXW", 0, WIN), R("L1"), R("HJ"), Op.add),
+            "y": lambda: agather(R("FY"), R(TFW, 0, WIN), R("L1")),
+            "Q1": lambda: act(R("Q1"), R("Q2"), Act.Identity, -1280.0, 0.5),
+            "QO": lambda: act(R("QO"), R("Q2"), Act.Identity, ODD - 1280.0, 0.5),
+            "next": lambda: lists("p3", 16, "SM", "FY", 0, 12),
+            "M1": lambda: ts(R("M1"), R("p3", 16, 28), GATE / 2, Op.add, float(P), Op.min),
+            "y high": lambda: lanes("p2", 256, 0, "FY", one("ID", HI), True, True, (0,)),
+            "y high 2": lambda: lanes("p2", 0, 264, "FY", one("ID", HI), True, True, (1, 2)),
+            "y cols": lambda: cp(R("YC"), R("p2", 256, 268)),
+            "n cols": lambda: ts(R("NC"), R("p5", 0, 24), 0.0, Op.max),
+            "y low": lambda: lanes("p1", 0, 128, "FY", low, True, True),
+            "gate": lambda: mm(R("p5", 0, 24), R("FY", 0, 128), R("SU", 0, 96, 4), True, False),
+            "h sum": lambda: lanes("p5", 8, 20, "Q1", one("WN")),
+            "flag y": lambda: mm(R("p6", 0, L), R("WN"), R("Q1"), True, False),
+            "max": lambda: ttgather(R("MX"), R("TXW", 0, PV), R("M1"), R("Q1"), Op.max),
+            "n": lambda: agather(R("FN"), R(TFW, 0, PV), R("M1")),
+            "blend": lambda: ttgather(R("HB"), R("TXW", 0, PV), R("M1"), R("QO"), Op.add),
+            "n max": lambda: lanes("p5", 8, 20, "MX", one("NBO")),
+            "n high": lambda: lanes("p5", 0, 16, "FN", both, False, True, (1, 2, 0)),
+            "n low": lambda: lanes("p2", 0, 128, "FN", low, True, True),
+            "flag n": lambda: (mm(R("p6", 0, L), R("NBO"), R("MX"), False, False), mm(R("p6", 0, L), R("WS"), R("FN"), False, True)),
+            "less y": lambda: (mm(R("p4", 256, 256 + L), R("NI"), R("FY"), True, False), mm(R("p4", 64, 64 + L), R("IM2"), R("Q2"), False, False)),
+            "plus n": lambda: (mm(R("p4", 256, 256 + L), R("ID"), R("FN"), False, False), mm(R("p4", 64, 64 + L), R("IP2"), R("HB"), False, True)),
+            "BR": lambda: act(R("BR"), R("p6", 0, L), Act.Sigmoid, 500.0, -1000.0),
+            "half": lambda: tt(R("p4", 64, 64 + L), R("p4", 64, 64 + L), R("BR"), Op.mult),
+            "h": lambda: (tt(HS, R("p4", 64, 64 + L), R("Q1"), Op.add), last or send(t, "H", "ha")),
+            "fields": lambda: tt(R("GF"), R("p4", 256, 256 + L), R("BR"), Op.mult),
+            "marks": lambda: (tt(R("UH"), R("p0", 0, 128), R("DH"), Op.min), tt(R("UL"), R("p0", 0, 128), R("DL"), Op.min)),
+            "J2": lambda: (mm(R("p7", 0, 128), R("UH"), R("ID"), False, False), mm(R("p7", 0, 128), R("UL"), R("IM"), False, True)),
+            "list": lambda: cp(R("ZU"), R("p7", 0, 128)),
+        }
+        onward = {
+            "flags": lambda: mm(R("p1", 256, 256 + L), R("W1"), R("FY")),
+            "count": lambda: act(R("BS"), R("p1", 256, 256 + L), scale=KW, total=col("AK", 0)),
+            "32s": lambda: act(R("SG"), R("S12"), Act.Sign, col("AK", 0), KW / 2, total=col("AK", 1)),
+            "level": lambda: act(R("LV"), R("CL"), Act.Identity, col("AK", 0), col("AK", 1)),
+            "void 0": lambda: mm(R("p1", 0, 256, 1, h64), R("ID", 0, 64, 1, h64), R("VL", p=h64), True, False),
+            "void": lambda: [mm(R("p1", 128 * j, 128 * j + 128, 1, h64), R("UL", j, 128, 2), R("IVD"), False, j == 1) for j in range(2)],
+            "VL": lambda: (act(R("VL", p=h64), R("p1", 0, 256, 1, h64)), local("S", row("XV", 0, 0, P), R("VL", p=h64))),
+            "y list": lambda: lists("p3", 28, "SY", "FY", 0, 12, True, False),
+            "y list 2": lambda: lists("p3", 28, "SY", "GF", 0, 12, False, True),
+            "b list": lambda: lists("p2", 0, "SN", "FY", 0, 12, True, False),
+            "b list 2": lambda: lists("p2", 0, "SN", "GF", 0, 12, False, True),
+            "YU": lambda: cp(R("YU"), R("p3", 28, 40)),
+            "K": lambda: (vgather(R("KS%d" % t), R("PL"), R("YU")), send(t, "K", "ka")),
+            "BU": lambda: cp(R("BU"), R("p2", 0, 12)),
+            "G": lambda: [gcopy(*c) for c in doubling(h1, GK, NX)],
+            "keys": lambda: preload(t + 1),
+            "less h": lambda: less_h(t + 1),
+        }
+        s1, s2 = LAST
+        final = {
+            "b rows": lambda: (mm(R("p6", 0, L), R("WNR"), R("FY"), True, False), mm(R("p6", 0, L), R("WNR"), R("GF"), False, True)),
+            "RB": lambda: act(R("RB"), R("p6", 0, L)),
+            "yb": lambda: (agather(R("NR"), R("RB"), R("LU")), dma("S", T["yb"][:, :], ap(row("NR", 0, 0, L)), [R("NR")], [])),
+            "yh": lambda: (vgather(R("MX"), HS, R("LU")), dma("S", T["yh"][:, :], ap(R("MX")), [R("MX")], [])),
+            "J2 a": lambda: agather(R("BF1", 16 * s1, P), R("IOT"), R("ZU", s1, 128)),
+            "J2 v": lambda: vgather(R("BF1", 0, 16 * s1), R("IOT"), R("ZU", 0, s1)),
+            "yj a": lambda: (agather(R("ROW", 16 * s2, P), R("BF1"), R("ZU", s2, 128)),
+                             dma("C", T["yj"][:, 16 * s2:P], ap(row("ROW", 0, 16 * s2, P)), [R("ROW", 16 * s2, P)], [])),
+            "yj v": lambda: (vgather(R("ROW", 0, 16 * s2), R("BF1"), R("ZU", 0, s2)),
+                             dma("S", T["yj"][:, 0:16 * s2], ap(row("ROW", 0, 0, 16 * s2)), [R("ROW", 0, 16 * s2)], [])),
+        }
+        for w in ("fields", "half", "h"):
+            onward[w] = final[w + " last"] = steps.pop(w)
+        for j in range(5):
+            onward["h%d" % j] = lambda j=j: cp(*hx[j][:2])
+        if t == 0:
+            for w in ("h0", "h1", "h2", "h3", "h4", "G", "less h"):
+                once[w + " first"] = onward.pop(w)
+        for what in STEP1 + MATCH + TABLES:
+            if isinstance(what, str):
+                for kind, now in ((steps, True), (onward, not last), (final, last), (once, t == 0)):
+                    if what in kind and now:
+                        kind[what]()
+                continue
+            w, a, b = what
+            d, x = R("DX", 16 * a, 16 * b), R("AX", 16 * a, 16 * b)
+            if w == "less h":
+                ttgather(d, R("TX"), R(K, a, b), R("HX", 16 * a, 16 * b), Op.subtract)
+            elif w == "plain":
+                agather(d, R("TX"), R(K, a, b))
+            elif w == "plus x":
+                mm(R(banks[AB.index(a)][0], 0, 16 * (b - a)), R("ID"), d, False, True)
+            elif w == "relu":
+                ts(x, d, -2.0, Op.mult, 0.0, Op.max)
+            elif w == "abs":
+                act(x, d if a < NX else R(banks[AB.index(a)][0], 0, 16 * (b - a)), Act.Abs)
+            elif w == "sum d":
+                sums("DX", a, b)
+            elif w == "sum":
+                sums("AX", a, b, what == last_sum)
+            elif w == "least":
+                scan(R("MS", a, b), R("RST", a, b), R("p0", a, b), 0.0, Op.add, Op.min)
+            elif w == "stays":
+                tt(R("ZN", a, b), R("p0", a, b), R("MS", a, b), Op.not_equal)
+            elif w == "column":
+                scan(R("RR", a, b), R("ZN", a, b), R("p4", 256 + a, 256 + b), 0.0, Op.mult, Op.add)
+            elif w in ("hot y", "hot n"):
+                one_hot(w == "hot n", range(a, b))
+            elif w in ("low y", "low n"):
+                j = w == "low n"
+                act(R("MM", 256 * j + a, 256 * j + b), R("p%d" % (1 + j), a, b), Act.Relu, 0.0, GATE)
+            elif w in ("prod y", "prod n"):
+                products(w == "prod n", range(a, b))
+            elif last:
+                continue
+            elif w == "SF":
+                lists(part(a), 0, "SF", "TF", a, b)
+            elif w == "JU":
+                cp(R("JU", a, b), R(part(a), 0, b - a))
+            else:
+                src, off = {"B1": ("BB", "ZU"), "TF": ("B1", "ZU"), "TX": ("XV", "JU")}[w[1:]]
+                (vgather if w[0] == "v" else agather)(R(w[1:], 16 * a, 16 * b), R(src), R(off, a, b))
     finish()
     g.wait_ge(T.sem["loc"], 2 * (NV - 1) * len(topo.engines(core, nxt)))
 
 
-N0, N2 = 6, 11
 RC, NX = 72, 128
 AB = (128, 160, 192)
-STEP1 = (("tile", 0, 0), ("plain", 128, 160), ("less h", 0, 24), ("less h", 24, 48), ("sum d", 0, 24), ("thresholds", 0, 0), ("plain", 160, 192),
-         ("relu", 0, 24), ("sum d", 24, 48), ("less h", 48, 84), ("sum", 0, 24), ("reorder", 0, 0), ("abs", 128, 160), ("relu", 24, 48),
-         ("abs", 160, 192), ("sum", 128, 160), ("less h", 84, 108), ("sum", 24, 48), ("abs", 48, 84), ("sum", 160, 192), ("less h", 108, 128),
-         ("sum d", 84, 108), ("relu", 84, 108), ("sum d", 108, 128), ("misses", 0, 0), ("sum", 48, 84), ("turn", 0, 0), ("sum", 84, 108),
-         ("relu", 108, 128), ("sum", 108, 128), ("steps", 0, 0))
-END = ("half", "marks", "J2", "h", "fields", "void", "list", "y")
-ENDL = ("half", "marks", "J2", "h", "fields", "list")
-KEYS = (0, 64, 128, 192)
-HALF = 56
-SPLIT = (20, 56, (26, 36), (26, 36))
-HC = (2, 1, 0, 1)
+LAST = (64, 64)
+PARTS = (0, 32, 80)
 GK = 72
+START = ("ones3", "ones1", "RST", "NI", "IW", "ones0", "RM", "PM", "EQ", "CK", "void column", "CM", "TH", "ha0", "PAIR", "hv1", "less h0", "hv0", "LK",
+         "ones2", "VT0", "keys0", "hv2", "MK", "BIG", "ha1", "SU", "hv3", "PP", "KJ", "PN", "NH", "K0", "ha2", "HI", "ha3")
+STEP1 = ("L2", "ha4", ("plain", 128, 160), "hv4", "S", ("plus x", 128, 160), "OWN", "NL", "CG1", "THf", ("less h", 36, 60), ("less h", 60, 84), "T1",
+         ("plain", 160, 192), ("sum d", 36, 84), ("plus x", 160, 192), ("less h", 0, 36), "t1", ("relu", 36, 60), ("abs", 128, 160), "SH",
+         ("sum", 128, 160), ("sum", 36, 60), ("less h", 84, 108), ("relu", 60, 84), "tile", ("abs", 160, 192), ("sum", 160, 192), "SL",
+         ("less h", 108, 128), ("sum d", 84, 108), ("relu", 84, 108), "BO", ("abs", 0, 36), ("relu", 108, 128), "reorder", "LH", "late", "turn", "WG",
+         "BU0", "SY", ("sum", 60, 84), "IM2", "own h", "NOT1", ("sum", 0, 36), ("sum d", 108, 128), ("sum", 84, 108), ("sum", 108, 128), "WT", "steps")
+MATCH = (("least", 0, 64), ("least", 64, 128), "IVD", ("least", 128, 192), "NBO", ("stays", 0, 64), "H0", ("stays", 64, 128), ("stays", 128, 192), "own",
+         ("column", 0, 64), ("column", 64, 128), ("column", 128, 192), "t2", "WT2", "LI", "CF", "TFM0", "nx - p", "CS", "mask", "L1", "WM", "late", "CG",
+         "Q2", "WH", "y", "J", "next", "y high", "WN", "y high 2", "DI", "WC", "pick", ("hot y", 0, 2), "Q1", ("hot y", 2, 4), "M1", ("hot y", 4, 6),
+         "y low", ("hot y", 6, 8), "QO", ("low y", 0, 256), "gate", "DN", "max", "h sum", "flag y", ("hot y", 8, 10), "less y", "W1", ("hot y", 10, 12),
+         "flags", "WS", ("prod y", 0, 8), "n", "n max", "n high", "IP2", "n low", "DL", "DJ", "blend", ("hot n", 0, 12), "flag n", "plus n",
+         ("prod y", 8, 12), ("low n", 0, 256), "DH", "BR", "IM", "count", ("prod n", 0, 12), "half", "late", "y list", "32s", "SF", "marks", "level",
+         "J2", "void", "h", "fields", "VL", "SN", "y list 2", "list", "b list", ("aB1", 58, 128), ("vB1", 0, 20), "keys")
+TABLES = ("YU", ("vB1", 20, 58), "b list 2", "K", ("aTF", 30, 64), ("vTF", 0, 30), ("vTF", 64, 96), ("SF", 0, 64), "BU", ("aTF", 96, 128), "h1", "G", "h0",
+          ("JU", 0, 64), "h2", ("vTX", 0, 30), ("SF", 64, 128), ("JU", 64, 128), "h3", ("vTX", 64, 94), "TFM", ("aTX", 30, 64), "h4", ("aTX", 94, 128),
+          "OWU", "less h")
+START = ("IW", "PM", "EQ", "ones0", "CF", "PAIR", "ones2", "LK", "CM", "RM", "RST", "ones1", "ones3", "void column", "CG1", "BO", "VT0", "PP", "hv1", "ha0", "SN", "HI", "ha1", "hv0", "NI", "BIG", "hv2", "keys0", "less h0", "PN", "CK", "ha2", "SU", "K0", "L2", "hv3", "MK", "OWN", "S", "KJ", "LH", "hv4", "NOT1", "ha3", "TH", "CS")
+STEP1 = ("WN", "THf", "T1", "NH", "tile", "ha4", ("plain", 128, 160), ("plain", 160, 192), ("less h", 36, 60), "NL", ("less h", 60, 84), ("relu", 36, 60), "SH", ("plus x", 128, 160), "SL", ("less h", 0, 36), ("less h", 84, 108), ("relu", 60, 84), "W1", "WG", ("abs", 128, 160), ("plus x", 160, 192), "t2", ("abs", 160, 192), ("abs", 0, 36), ("less h", 108, 128), ("sum d", 36, 84), "CG", ("relu", 84, 108), ("sum", 128, 160), ("sum", 36, 60), "reorder", ("relu", 108, 128), "t1", "IM2", "WC", "late", "NBO", "own h", "turn", ("sum", 160, 192), "IVD", ("sum d", 84, 108), ("sum", 60, 84), ("sum", 0, 36), "WT", ("sum d", 108, 128), "BU0", ("sum", 84, 108), ("sum", 108, 128), "IM", "steps", "H0")
+MATCH = (("least", 0, 64), ("least", 64, 128), ("least", 128, 192), "IP2", ("stays", 0, 64), "TFM0", ("stays", 64, 128), "J", ("stays", 128, 192), "own", ("column", 0, 64), ("column", 64, 128), ("column", 128, 192), "WT2", "LI", "nx - p", "SY", "mask", "L1", "y", "WM", "late", "y high", "WS", "y high 2", "next", "Q2", "QO", "DI", "WH", "Q1", "gate", "DN", "y low", "y cols", "pick", "h sum", ("hot y", 0, 2), "DL", ("low y", 0, 256), "M1", ("hot y", 4, 6), ("hot y", 6, 8), "less y", "n", "max", "flags", "n max", ("hot y", 2, 4), "count", "n high", "n low", "DJ", "flag y", ("low n", 0, 256), "blend", "flag n", ("hot y", 8, 10), "n cols", ("hot y", 10, 12), "plus n", ("prod y", 0, 8), ("hot n", 0, 12), ("prod y", 8, 12), ("prod n", 0, 12), "DH", "BR", "half", "marks", "h", "y list", "J2", "fields", "list", "32s", "void", "y list 2", "level", "b list", ("vB1", 0, 20), "SF", "YU", "VL", ("aB1", 58, 128), ("vB1", 20, 58), ("aTF", 30, 64), "K", ("aTF", 96, 128), "late", "b list 2")
+TABLES = ("BU", ("vTF", 0, 30), ("vTF", 64, 96), ("SF", 0, 64), "G", ("SF", 64, 128), "h0", "h1", ("JU", 0, 64), "TFM", "h2", "OWU", ("aTX", 30, 64), ("vTX", 0, 30), ("JU", 64, 128), "keys", "h3", ("aTX", 94, 128), ("vTX", 64, 94), "h4", "less h")
+START = ("IW", "ones0", "RST", "NI", "PM", "ones2", "ones3", "EQ", "RM", "ha0", "ha1", "CM", "ones1", "NOT1", "PP", "VT0", "R2", "PAIR", "BO", "hv1", "hv0", "ha2", "WN", "PN", "LK", "hv2")
+STEP1 = ("BIG", "less h0", "CG1", "tile", "SU", "KJ", "hv3", "bm", "S", "K0", "HI", "WNR", "CS", "W1", "SM", "hv4", "ha3", "OWU", "ha4", "keys0", "WT", "L2", "SN", ("plain", 128, 160), "SY", ("plus x", 128, 160), "LH", ("less h", 0, 36), "NH", "TH", ("plain", 160, 192), ("less h", 36, 60), "THf", ("less h", 60, 84), "SH", ("abs", 128, 160), ("relu", 36, 60), ("plus x", 160, 192), ("abs", 160, 192), ("sum d", 36, 84), "NL", "t2", "SL", ("sum", 128, 160), ("abs", 0, 36), "reorder", "T1", ("sum", 36, 60), "IM2", ("less h", 84, 108), ("relu", 60, 84), ("less h", 108, 128), ("relu", 84, 108), ("relu", 108, 128), "OWN", ("sum", 160, 192), "t1", ("sum d", 84, 108), "late", "own h", ("sum", 60, 84), ("sum", 0, 36), "BU0", "turn", "WT2", ("sum d", 108, 128), ("sum", 84, 108), "H0", ("sum", 108, 128), "pl", "CG")
+MATCH = ("steps", ("least", 0, 64), ("least", 64, 128), "J", ("least", 128, 192), ("stays", 0, 64), ("stays", 64, 128), ("stays", 128, 192), "own", ("column", 0, 64), ("column", 64, 128), ("column", 128, 192), "TFM0", "void column", "LI", "WC", "L1", "y", "nx - p", "y high", "NBO", "WM", "y high 2", "Q2", "Q1", "next", "DI", "y cols", "DN", "WH", "IP2", "flag y", "WS", "y low", "gate", ("hot y", 2, 4), "less y", "QO", "h sum", "M1", ("hot y", 8, 10), "max", ("hot y", 0, 2), "n max", "n", "blend", "n high", "VL0", ("hot y", 10, 12), "n low", ("low y", 0, 256), "flags", "IM", "flag n", "plus n", ("low n", 0, 256), "DL", "n cols", ("hot y", 4, 6), ("hot y", 6, 8), "BR", "DJ", ("hot n", 0, 12), ("prod y", 0, 8), ("prod y", 8, 12), "IVD", "half", "fields last", "count", ("prod n", 0, 12), "y list", "DH", "h", "b rows", "RB", "32s", "void 0", "marks", "fields", "J2", "late", "void", "y list 2", "b list", "level", "half last", "CF", "b list 2", "list", "VL", ("vB1", 0, 20), "h last", "YU", "SF", "late", "K", "keys", ("vB1", 20, 56), ("aB1", 56, 128))
+TABLES = ("yb", "BU", ("vTF", 0, 32), ("vTF", 64, 96), "h1", "J2 v", "yh", "h0", "J2 a", "G", ("aTF", 32, 64), ("SF", 0, 64), ("aTF", 96, 128), ("JU", 0, 64), "h1 first", "h2", "TFM", ("SF", 64, 128), "less h", "less h first", "h0 first", "yj v", ("vTX", 0, 30), "h2 first", ("JU", 64, 128), "yj a", "h3 first", "h3", ("aTX", 30, 64), ("vTX", 64, 94), "G first", "h4 first", ("aTX", 94, 128), "h4")
+START = ("IW", "ones0", "RST", "NI", "keys0", "PM", "ones2", "ones3", "EQ", "RM", "ha0", "ha1", "CM", "bm", "ones1", "NOT1", "PP", "VT0", "R2", "PAIR", "BO", "HI", "hv1", "SN", "less h0", "L2", "WT", "SU", "hv0", "ha2", "WNR", "WN", "CG1", "PN", "LK", "BIG", "hv2", "ha3")
+STEP1 = ("hv3", "SY", "OWU", "hv4", "LH", "KJ", "ha4", "K0", "S", "tile", ("plain", 128, 160), ("plain", 160, 192), "SM", ("plus x", 128, 160), "W1", "CS", ("less h", 36, 72), "NH", ("plus x", 160, 192), ("less h", 0, 36), ("less h", 72, 96), ("sum d", 36, 72), ("abs", 128, 160), "SH", "NL", "TH", ("relu", 36, 72), ("sum", 128, 160), ("abs", 160, 192), ("sum d", 72, 96), "SL", "pl", ("sum", 36, 72), ("abs", 0, 36), "THf", ("sum", 160, 192), ("less h", 96, 116), "t2", ("relu", 72, 96), ("sum d", 96, 116), ("sum", 72, 96), ("less h", 116, 128), "T1", ("relu", 96, 116), "reorder", ("sum", 0, 36), ("relu", 116, 128), ("sum d", 116, 128), "t1", "WT2", "late", ("sum", 96, 116), "turn", "own h", "OWN", ("sum", 116, 128))
+MATCH = ("BU0", ("least", 0, 64), "steps", ("least", 64, 128), ("least", 128, 192), "J", "CG", ("stays", 0, 64), ("stays", 64, 128), "H0", ("stays", 128, 192), "own", ("column", 0, 64), ("column", 64, 128), "IM2", "misses", ("column", 128, 192), "void column", "LI", "WC", "L1", "nx - p", "NBO", "y", "y high", "WM", "y high 2", "DI", "Q2", "y cols", "DN", "WH", "IP2", "next", "WS", ("hot y", 2, 4), "M1", "Q1", "gate", "flag y", ("hot y", 8, 10), "y low", "h sum", "VL0", "max", ("hot y", 0, 2), "QO", "less y", "n", "n max", "n high", "n low", "blend", "flag n", ("low y", 0, 256), ("hot y", 10, 12), "IM", "flags", "n cols", ("hot y", 4, 6), ("low n", 0, 256), "plus n", "BR", ("hot y", 6, 8), ("prod y", 0, 8), "DL", ("hot n", 0, 12), "DJ", "count", "fields last", ("prod y", 8, 12), ("prod n", 0, 12), "half", "32s", "y list", "IVD", "DH", "b rows", "h", "RB", "void 0", "marks", "half last", "yb", "J2", "fields", "late", "CF", "SF", "list", "void", "h last", "level", "y list 2", "VL", "late", "b list", "YU", ("vB1", 0, 20))
+TABLES = ("b list 2", "K", ("vB1", 20, 52), ("aB1", 52, 128), ("aTF", 32, 64), "BU", ("vTF", 0, 32), "J2 v", "G", ("SF", 0, 64), ("vTF", 64, 94), "h1", "h0", ("aTF", 94, 128), ("SF", 64, 128), "h1 first", ("JU", 0, 64), "less h first", ("aTX", 26, 64), "less h", "h0 first", "h2", "h2 first", ("vTX", 0, 26), ("JU", 64, 128), "J2 a", "h3 first", "G first", "yh", "h3", "keys", ("aTX", 92, 128), ("vTX", 64, 92), "yj v", "h4", "h4 first", "yj a")
+STEP1 = ("hv3", "SY", "OWU", "hv4", "LH", "KJ", "ha4", "K0", "tile", "S", "WG", "CK", "W1", "MK", "CS", ("plain", 128, 160), ("less h", 36, 72), ("plus x", 128, 160), ("less h", 72, 96), ("plain", 160, 192), "NH", ("relu", 36, 72), "SH", ("sum d", 36, 72), ("plus x", 160, 192), "NL", "TH", ("sum d", 72, 96), "SL", ("less h", 0, 36), "pl", ("sum", 36, 72), ("abs", 128, 160), ("abs", 160, 192), ("sum", 128, 160), "THf", ("less h", 96, 116), ("relu", 72, 96), ("less h", 116, 128), ("abs", 0, 36), "t2", "T1", ("sum", 160, 192), ("sum d", 96, 116), ("sum", 72, 96), "reorder", ("relu", 96, 116), ("relu", 116, 128), ("sum", 0, 36), "t1", ("sum d", 116, 128), "turn", "WT2", ("sum", 96, 116), "OWN", ("sum", 116, 128), "own h")
+MATCH = ("steps", "BU0", ("least", 0, 64), ("least", 64, 128), ("least", 128, 192), "CG", "H0", ("stays", 0, 64), ("stays", 64, 128), "misses", ("stays", 128, 192), "own", ("column", 0, 64), ("column", 64, 128), ("column", 128, 192), "IM2", "void column", "LI", "WC", "late", "nx - p", "L1", "NBO", "J", "y", "WM", "Q2", "mask", "y high", "DI", "y high 2", "DN", "WH", "next", "y cols", "Q1", "IP2", "pick", ("hot y", 2, 4), "gate", "M1", ("hot y", 8, 10), "max", "WS", "VL0", "QO", "flag y", "n", "IM", "y low", "h sum", ("low y", 0, 256), "less y", "n max", ("hot y", 6, 8), "n high", ("hot y", 10, 12), "n low", "flag n", ("low n", 0, 256), "BR", "blend", "n cols", ("hot y", 0, 2), "flags", "DL", "DJ", ("hot y", 4, 6), ("hot n", 0, 12), "IVD", "plus n", "fields last", ("prod y", 0, 8), "half", ("prod y", 8, 12), ("prod n", 0, 12), "half last", "count", "h", "DH", "void 0", "b rows", "marks", "h last", "32s", "late", "CF", "J2", "level", "fields", "list", "void", "yh", "VL", "y list", "SF", "y list 2")
+TABLES = ("b list", ("vB1", 20, 52), ("vB1", 0, 20), "YU", "late", ("aB1", 52, 128), "K", ("aTF", 32, 64), "RB", ("vTF", 0, 32), ("aTF", 94, 128), ("vTF", 64, 94), "J2 v", "h0", "b list 2", "h1", "J2 a", "BU", ("SF", 0, 64), "yb", ("SF", 64, 128), "h1 first", "less h first", "G", "h0 first", ("JU", 0, 64), "h2", "h2 first", ("vTX", 0, 26), "yj v", "keys", ("JU", 64, 128), "h3 first", "h3", ("vTX", 64, 92), "G first", "less h", ("aTX", 26, 64), "yj a", ("aTX", 92, 128), "h4", "h4 first")
+START = ("ones1", "RST", "IW", "PM", "ones3", "ha0", "NI", "ones2", "LK", "EQ", "RM", "NOT1", "less h0", "PAIR", "hv1", "PP", "ha1", "SU", "S", "hv0", "BO", "VT0", "CG1", "hv2", "ha2", "SY", "CM")
+STEP1 = ("ones0", "K0", "BIG", "keys0", "hv3", "KJ", "W1", "R2", "ha3", "bm", "ha4", "OWU", "PN", "SM", "LH", "tile", ("plain", 128, 160), ("plain", 160, 192), ("plus x", 128, 160), "HI", "hv4", "L2", "CS", "WN", "SN", ("plus x", 160, 192), "WNR", "WT", ("less h", 0, 24), "TH", ("less h", 24, 60), "NH", ("abs", 128, 160), ("less h", 60, 88), "SH", ("abs", 0, 24), ("relu", 24, 60), ("sum d", 24, 60), ("sum", 128, 160), ("abs", 160, 192), "NL", ("sum", 0, 24), ("sum", 24, 60), "SL", "pl", ("abs", 60, 88), ("less h", 88, 114), "THf", ("less h", 114, 128), "T1", ("sum", 160, 192), "reorder", ("sum d", 88, 114), "own h", ("sum", 60, 88), ("relu", 88, 114), ("sum d", 114, 128), "t1", "late", ("relu", 114, 128), ("sum", 88, 114), "OWN", "WT2", "NBO", "turn", ("sum", 114, 128), "void column", "steps", "IP2", "t2")
+MATCH = ("BU0", ("least", 0, 64), "H0", ("least", 64, 128), ("least", 128, 192), "nx - p", ("stays", 0, 64), ("stays", 64, 128), ("stays", 128, 192), "own", "J", "IM", ("column", 0, 64), ("column", 64, 128), "misses", "IM2", ("column", 128, 192), "CG", "LI", "L1", "WM", "Q2", "WH", "DI", "y", "y high", "DN", "y high 2", "y cols", "WS", "Q1", "WC", "next", ("hot y", 2, 4), "M1", "less y", ("hot y", 8, 10), ("hot y", 0, 2), "max", "gate", ("hot y", 10, 12), "flag y", ("hot y", 4, 6), "QO", "IVD", "h sum", "y low", "n max", "n", "n high", "n low", "DL", ("low y", 0, 256), "flag n", "blend", "plus n", "DJ", "n cols", ("low n", 0, 256), "VL0", "BR", ("hot y", 6, 8), "flags", ("hot n", 0, 12), "fields last", "half", ("prod y", 0, 8), ("prod y", 8, 12), ("prod n", 0, 12), "count", "DH", "h", "y list", "b rows", "marks", "late", "RB", "yb", "fields", "32s", "CF", "void 0", "J2", "level", "half last", "void", "y list 2", "list", "late", ("vB1", 0, 20), "b list", "YU", "SF", ("vB1", 20, 52), "VL", "K", "h last")
+TABLES = ("b list 2", "keys", ("aB1", 52, 128), ("aTF", 16, 32), "BU", ("vTF", 0, 16), ("aTF", 54, 80), "J2 v", ("vTF", 32, 54), "yh", "G first", "J2 a", "yj v", ("vTF", 80, 102), ("SF", 0, 32), "G", "h1", "h0", "yj a", ("aTF", 102, 128), ("JU", 0, 32), ("aTX", 12, 32), ("SF", 32, 80), "h2", ("JU", 32, 80), ("SF", 80, 128), "h0 first", "h3", "h1 first", ("vTX", 0, 12), "h4", "less h first", ("aTX", 52, 80), "h2 first", "less h", ("JU", 80, 128), ("vTX", 32, 52), "h3 first", ("vTX", 80, 100), "h4 first", ("aTX", 100, 128))

from concourse.mybir import AluOpType as Op, ActivationFunctionType as Act

BIG = 2.0 ** 40
KW, KK = 2.0 ** 17, 4096
VOID = 128.0
GATE = 8192.0
ODD = 2559.5
L, P, NV = 192, 2048, 5
PV = P + 16
CH = L // 16
TURNS = pow(16, NV, L - 1)
HI, LO, NH, NL, SH, SL, L2, ONE, C1, C2, C3 = range(11)

B16, F16, F32, I32, U16 = "bfloat16", "float16", "float32", "int32", "uint16"
SCRATCH = {
    "TXW": ("sbuf", [128, PV + NV * L], B16), "XV": ("sbuf", [128, P], B16), "TFW": ("sbuf", [128, PV + NV * L], B16),
    "BBW": ("sbuf", [128, PV + L], B16), "B1": ("sbuf", [128, P], B16), "PL": ("sbuf", [128, P], I32),
    "IOT": ("sbuf", [128, P], F32), "BF1": ("sbuf", [128, P], F32), "ROW": ("sbuf", [128, P], F32), "RB": ("sbuf", [128, L], F32),
    "HX": ("sbuf", [128, L * 16], B16), "DX": ("sbuf", [128, L * 16], B16), "AX": ("sbuf", [128, L * 16], B16),
    "KI": ("sbuf", [128, L], I32), "KF": ("sbuf", [128, L], F32), "KJ": ("sbuf", [128, L], F16), "VT": ("sbuf", [128, 6, 2, 32], F16),
    "MS": ("sbuf", [128, L], F32), "RST": ("sbuf", [128, L], F32), "ZN": ("sbuf", [128, L], B16), "RR": ("sbuf", [128, L], F32),
    "WO": ("sbuf", [128, 12], F32), "LI": ("sbuf", [128, 12], F32), "L1": ("sbuf", [128, 12], U16),
    "HJ": ("sbuf", [128, L], F32), "Q2": ("sbuf", [128, L], F16), "Q1": ("sbuf", [128, L], B16), "QO": ("sbuf", [128, L], F32),
    "FF": ("sbuf", [128, 2 * L], B16), "GF": ("sbuf", [128, L], B16), "NR": ("sbuf", [128, L], F32), "M1": ("sbuf", [128, 12], U16),
    "MX": ("sbuf", [128, L], B16), "HB": ("sbuf", [128, L], F16), "BR": ("sbuf", [128, L], B16), "BY": ("sbuf", [128, 24], U16),
    "MM": ("sbuf", [128, 4 * 128], B16), "NN": ("sbuf", [128, 24 * 128], B16),
    "YC": ("sbuf", [128, 12], B16), "NC": ("sbuf", [128, 24], B16), "UH": ("sbuf", [128, 128], B16), "UL": ("sbuf", [128, 128], B16), "VL": ("sbuf", [128, 256], B16),
    "ZU": ("sbuf", [128, 128], U16), "JU": ("sbuf", [128, 128], U16),
    "BS": ("sbuf", [128, L], B16), "AK": ("sbuf", [128, 2], F32), "SG": ("sbuf", [128, 12], F32), "LV": ("sbuf", [128, L], B16),
    "ONES": ("sbuf", [128, 192], B16), "BD0": ("sbuf", [128, 144], B16), "BD1": ("sbuf", [128, 144], B16), "BD": ("sbuf", [128, 144], B16),
    "IDP": ("sbuf", [128, 160], B16), "NI": ("sbuf", [128, 128], B16), "IDW": ("sbuf", [128, 4 * 128], B16), "IH": ("sbuf", [128, 256], B16),
    "BO": ("sbuf", [128, 128], B16), "NBO": ("sbuf", [128, 128], B16), "WS": ("sbuf", [128, 128], B16), "WN": ("sbuf", [128, 128], B16),
    "WNR": ("sbuf", [128, 128], B16), "W1": ("sbuf", [128, 128], B16), "WM": ("sbuf", [128, 128], B16), "SM": ("sbuf", [128, 144], B16),
    "WH": ("sbuf", [128, 2 * 128], B16), "WC": ("sbuf", [128, 16], B16), "WT": ("sbuf", [128, 3 * 128], B16),
    "SU": ("sbuf", [128, 144], B16), "SY": ("sbuf", [128, 144], B16), "SN": ("sbuf", [128, 144], B16), "SF": ("sbuf", [128, 144], B16),
    "PP": ("sbuf", [128, 4 * 160], B16), "CO": ("sbuf", [128, 16], B16), "EQ": ("sbuf", [128, 24], B16), "IQ": ("sbuf", [128, 128], B16),
    "KC": ("sbuf", [128, L], B16), "NOT1": ("sbuf", [128, 1], F32), "R2": ("sbuf", [128, 128], B16), "CL": ("sbuf", [128, L], B16), "S12": ("sbuf", [128, 12], F32),
    "IP": ("sbuf", [128, 2], I32), "IW": ("sbuf", [128, 4], I32), "I12": ("sbuf", [128, 12], I32), "IK": ("sbuf", [128, 12], I32),
    "IO": ("sbuf", [128, 12 * NV], I32), "OWN": ("sbuf", [128, 12 * NV], F32), "OWU": ("sbuf", [128, 12 * NV], U16), "LK": ("sbuf", [128, 24], U16),
    "CQ": ("sbuf", [128, 12], F32), "CA": ("sbuf", [128, 12], I32), "CB": ("sbuf", [128, 12], F32), "CC": ("sbuf", [128, 12], F32),
    "CD": ("sbuf", [128, 12], F32), "LU": ("sbuf", [128, 12], U16),
    "CF": ("sbuf", [128, 7 * 256], B16), "NXC": ("sbuf", [128, 256], I32), "BMC": ("sbuf", [128, 12], I32),
    "TH": ("sbuf", [128, 2], I32), "THw": ("sbuf", [128, 4], I32), "THf": ("sbuf", [128, 4], B16), "T1": ("sbuf", [128, 2 * L], B16),
    "TSR": ("sbuf", [128, 128], B16), "TSx": ("sbuf", [128, 128], B16), "TSQ": ("sbuf", [128, 160], B16),
    "DI": ("sbuf", [128, 128], I32), "DN": ("sbuf", [128, 128], I32), "DL": ("sbuf", [128, 128], F32), "DJ": ("sbuf", [128, 128], F32),
    "DH": ("sbuf", [128, 128], F32),
    "HH": ("sbuf", [128, NV * L], B16), "KU": ("sbuf", [128, 2 * NV * L], U16),
}
ALIAS = {"FY": ("FF", 0, L), "FN": ("FF", L, L), "ID": ("IDP", 16, 128), "ON2": ("ONES", 0, L), "TX": ("TXW", 0, P), "TF": ("TFW", 0, P),
         "HC": ("TFW", PV, L), "BB": ("BBW", 0, P), "BU": ("BY", 0, 12), "YU": ("BY", 12, 12)}
for _t in range(NV):
    ALIAS["H%d" % _t] = ("TXW", PV + L * _t, L)
    ALIAS["TFM%d" % _t] = ("TFW" if _t else "BBW", PV + L * _t, L)
    ALIAS["HS%d" % _t] = ("HH", L * _t, L)
    ALIAS["K%d" % _t] = ("KU", L * _t, L)
    ALIAS["KS%d" % _t] = ("KU", L * (NV + _t), L)
for _k, _n in enumerate(("IM", "IVD", "IP2", "IM2")):
    ALIAS[_n] = ("IDW", 128 * _k, 128)
for _t in range(8):
    SCRATCH["p%d" % _t] = ("psum", [128, 512], F32)
NDMA = 32
SEMAPHORES = ["sV", "sA", "sT", "sG", "loc"] + ["d%d" % k for k in range(NDMA)] + ["ha%d" % t for t in range(1, NV)] + ["ka%d" % t for t in range(1, NV)]


def make_emitter(g, T):
    queues = {"V": g.vector, "A": g.scalar, "T": g.tensor, "G": g, "S": g.sync, "C": g.scalar}
    hist, know, snap, count, nd = {}, {}, {}, {}, [0]

    def ap(r):
        name, c0, c1, st, p = r
        if name == "VT":
            return T[name][p, :, :, c0:c1] if st == 1 else T[name][p, :, -1 - st, c0:c1]
        return T[name][p, c0:c1:st] if st != 1 else T[name][p, c0:c1]

    def clash(a, b):
        if a[1] >= b[2] or b[1] >= a[2]:
            return False
        if a[3] == b[3] and a[3] > 1 and (a[1] - b[1]) % a[3]:
            return False
        if a[4] != b[4] and not set(range(128)[a[4]]) & set(range(128)[b[4]]):
            return False
        return True

    def await_(q, sem, val):
        k = know.setdefault(q, {})
        if k.get(sem, 0) >= val:
            return
        queues[q].wait_ge(T.sem[sem], val)
        for s, v in snap.get((sem, val), {}).items():
            if v > k.get(s, 0):
                k[s] = v
        k[sem] = val

    def deps(q, reads, writes):
        need = {}
        for w, rs in ((False, reads), (True, writes)):
            for r in rs:
                psum = SCRATCH.get(r[0], ("",))[0] == "psum"
                for (h, hw, hq, sem, val) in hist.get(r[0], []):
                    if psum and hq != q:
                        hit = True
                    else:
                        hit = (w or hw) and clash(r, h)
                        if hit and psum and q == "T":
                            hit = False
                    if hit and val > need.get(sem, 0):
                        need[sem] = val
        for sem in sorted(need):
            await_(q, sem, need[sem])

    def note(q, reads, writes, sem, val):
        for w, rs in ((False, reads), (True, writes)):
            for r in rs:
                h = hist.setdefault(r[0], [])
                if w and r[0][0] != "p":
                    h[:] = [e for e in h if not (r[1] <= e[0][1] and r[2] >= e[0][2] and r[3] == 1 and r[4] == slice(None) and (e[2] != q or e[1]))]
                h[:] = [e for e in h if not (e[2] == q and e[1] == w and e[0] == r)]
                h.append((r, w, q, sem, val))

    def op(q, fn, reads, writes):
        deps(q, reads, writes)
        sem = "s" + q
        count[q] = count.get(q, 0) + 1
        fn(queues[q]).then_inc(T.sem[sem], 1)
        k = dict(know.setdefault(q, {}))
        k[sem] = count[q]
        snap[(sem, count[q])] = k
        note(q, reads, writes, sem, count[q])

    def dma(q, out, in_, reads, writes):
        kq = "A" if q == "C" else q
        deps(kq, reads, writes)
        sem = "d%d" % nd[0]
        nd[0] += 1
        queues[q].dma_start(out, in_).then_inc(T.sem[sem], 16)
        snap[(sem, 16)] = dict(know.setdefault(kq, {}))
        note("D" + sem, reads, writes, sem, 16)

    def arrive(name, sem, val):
        note("R" + sem, [], [R(name)], sem, val)

    def finish():
        for q in ("V", "A", "T", "G"):
            if count.get(q):
                await_("G", "s" + q, count[q])
        for k in range(nd[0]):
            await_("G", "d%d" % k, 16)

    return ap, op, dma, arrive, deps, finish


def R(name, c0=0, c1=None, st=1, p=slice(None)):
    if name in ALIAS:
        base, off, w = ALIAS[name]
        return (base, off + c0, off + (w if c1 is None else c1), st, p)
    return (name, c0, SCRATCH[name][1][1] if c1 is None else c1, st, p)


def col(name, j):
    return R(name, j, j + 1)


def row(name, f, c0, c1):
    return R(name, c0, c1, 1, slice(f, 128, 16))


def blk(name, j, w=128):
    return R(name, w * j, w * j + w)


def doubling(h, a, b):
    steps = [(R("HX", 16 * a + k, 16 * b, 16), R(h, a, b), b - a) for k in (0, 8)]
    return steps + [(R("HX", 16 * a + s // 2, 16 * b, s), R("HX", 16 * a, 16 * b, s), 16 * (b - a) // s) for s in (8, 4, 2)]


def rank_program(g, core, T, topo):
    rank = T.rank_of(core)
    if rank is None:
        return
    n = len(T.cores)
    nxt, prv = T.cores[(rank + 1) % n], T.cores[(rank - 1) % n]
    rid, pid = topo.addr(nxt, core)
    mask = topo.mask(core, nxt)
    ap, op, dma, arrive, deps, finish = make_emitter(g, T)

    def tt(out, a, b, o):
        op("V", lambda e: e.tensor_tensor(ap(out), ap(a), ap(b), o), [a, b], [out])

    def ts(out, a, s1, o0, s2=None, o1=None):
        rd = [a] + [s for s in (s1, s2) if isinstance(s, tuple)]
        v1 = ap(s1) if isinstance(s1, tuple) else s1
        v2 = ap(s2) if isinstance(s2, tuple) else s2
        if o1 is None:
            op("V", lambda e: e.tensor_scalar(ap(out), ap(a), v1, None, o0), rd, [out])
        else:
            op("V", lambda e: e.tensor_scalar(ap(out), ap(a), v1, v2, o0, o1), rd, [out])

    def cp(out, a):
        op("V", lambda e: e.tensor_copy(ap(out), ap(a)), [a], [out])

    def fill(out, c):
        op("V", lambda e: e.memset(ap(out), c), [], [out])

    def turn(out, a):
        op("V", lambda e: e.transpose(ap(out), ap(a)), [a], [out])

    def scan(out, a, b, init, o0, o1):
        op("V", lambda e: e.tensor_tensor_scan(ap(out), ap(a), ap(b), init, o0, o1), [a, b], [out])

    def act(out, a, f=Act.Copy, bias=0.0, scale=1.0, total=None, off=None):
        rd = [a] + [s for s in (bias, scale, off) if isinstance(s, tuple)]
        kw = {"bias": ap(bias) if isinstance(bias, tuple) else bias, "scale": ap(scale) if isinstance(scale, tuple) else scale}
        if total:
            kw["accum_out"] = ap(total)
        src = ap(a).indirect(ap(off)) if off else ap(a)
        op("A", lambda e: e.activation(ap(out), src, f, **kw), rd, [out, total] if total else [out])

    def vgather(out, win, off):
        op("V", lambda e: e.tensor_copy(ap(out), ap(win).indirect(ap(off))), [win, off], [out])

    def agather(out, win, off, c=1.0):
        act(out, win, scale=c, off=off)

    def ttgather(out, win, off, b, o):
        op("V", lambda e: e.tensor_tensor(ap(out), ap(win).indirect(ap(off)), ap(b), o), [win, off, b], [out])

    def mm(out, lhs, rhs, start=True, stop=True):
        op("T", lambda e: e.matmul(ap(out), ap(lhs), ap(rhs), start, stop), [lhs, rhs], [out])

    def iota(out, pat, base, cm):
        small = SCRATCH[out[0]][2] != I32
        op("G", lambda e: e.iota(ap(out), pat, base, cm, allow_small_or_imprecise_dtypes=True) if small else e.iota(ap(out), pat, base, cm), [], [out])

    def asel(out, a, pat, o, fv, base, cm):
        op("G", lambda e: e.affine_select(ap(out), ap(a), pat, o, fv, base, cm), [a], [out])

    def gcopy(out, a, width):
        asel(out, a, [[0, width]], Op.is_ge, 0.0, 1, 0)

    def local(q, dst, src):
        dma(q, ap(dst), ap(src), [src], [dst])

    def lists(bank, c, S, src, q0, q1, start=True, stop=True):
        for r in range(16):
            mm(R(bank, c, c + q1 - q0), R(S, 15 - r, 143 - r), R(src, 16 * q0 + r, 16 * q1, 16), start and r == 0, stop and r == 15)

    def send(t, name, sem):
        deps("G", [R("%sS%d" % (name, t))], [])
        g.remote_dma(ap(R("%s%d" % (name, t + 1))), ap(R("%sS%d" % (name, t))), T.sem["%s%d" % (sem, t + 1)], T.sem["loc"], pid, rid, mask)
        arrive("%s%d" % (name, t + 1), "%s%d" % (sem, t + 1), len(topo.engines(prv, core)))

    e8, h64 = slice(0, 8), slice(0, 64)
    dma("C", ap(R("HC")), T["hm"][:, :], [], [R("HC")])
    dma("S", T["KI"][:, :], T["kt"][:, :], [], [R("KI")])
    dma("S", ap(R("TX")), T["xp"][:, :], [], [R("TX")])
    dma("S", T["NXC"][h64, :], T["nx"][:, :], [], [R("NXC")])
    dma("C", T["TH"][e8, :], T["th"][:, :], [], [R("TH")])

    PM, P12, P256, RM0, RM1, CF_, C2L, CL2, CG1, CS, CG = (col("CO", j) for j in range(11))
    NOT1 = R("NOT1")
    EQ = lambda f: col("EQ", f)
    PAIR = lambda f: col("EQ", 16 + f // 2)

    def scaled(q, out, a, c):
        if q == "A":
            act(out, a, scale=c)
        else:
            ts(out, a, c, Op.mult)

    def cf(j):
        return R("CF", 256 * j, 256 * j + 256, 1, h64)

    def field(f, j):
        local("S", row("BB", f, 0, P), cf(j))

    fill(R("ONES"), 1.0)
    iota(R("IP"), [[0, 2]], 0, 1)
    iota(R("BD0"), [[0, 9], [1, 16]], 0, 0)
    asel(R("IDP"), R("ONES", 0, 160), [[-1, 160]], Op.is_equal, 0.0, 16, 1)
    iota(R("IK"), [[1, 6], [6, 2]], 0, 0)
    asel(R("BD1"), R("BD0"), [[-16, 9], [0, 16]], Op.is_ge, -1.0, 0, 1)
    iota(R("KC"), [[0, 12], [KK, 16]], KK, 0)
    asel(R("BD"), R("BD1"), [[16, 9], [0, 16]], Op.is_ge, -1.0, 15, -1)
    iota(R("IH", p=h64), [[16, 16], [0, 16]], 0, 0)
    iota(cf(6), [[0, 16], [1, 16]], 0, 0)
    asel(R("TSx", p=e8), R("ONES", 0, 128, p=e8), [[1, 128]], Op.is_ge, 0.0, 0, -16)
    iota(R("IO"), [[L, NV], [1, 12]], PV, 0)
    asel(R("TSR", p=e8), R("TSx", p=e8), [[-1, 128]], Op.is_ge, 0.0, 15, 16)
    iota(R("I12"), [[16, 12]], 0, 0)
    iota(R("IQ"), [[16, 128]], 0, 0)
    asel(R("TSQ", p=e8), R("ONES", 0, 160, p=e8), [[-1, 160]], Op.is_equal, 0.0, 16, 16)
    for r in range(16):
        gcopy(blk("XV", r), R("TX", r, P, 16), 128)
    iota(R("S12"), [[1024, 2], [-64, 6]], 1 - 64, 0)
    iota(R("CL"), [[0, L]], int(-16 * KW), 0)

    hv, ha = doubling("HC", 0, RC), doubling("HC", RC, NX)
    once = {
        "RST": lambda: act(R("RST"), R("ON2"), Act.Sigmoid, 0.0, -1000.0),
        "IW": lambda: (ts(R("IW", 0, 1), R("IP", 0, 1), 15, Op.bitwise_and), ts(R("IW", 1, 2), R("IP", 1, 2), 16, Op.bitwise_and),
                       ts(R("IW", 2, 3), R("IP", 1, 2), 7, Op.bitwise_and)),
        "PM": lambda: (cp(PM, R("IW", 0, 1)), ts(P12, R("IW", 0, 1), float(CH), Op.mult), ts(P256, R("IW", 2, 3), 256.0, Op.mult)),
        "RM": lambda: (ts(RM0, R("IW", 1, 2), 0.0, Op.is_equal), ts(RM1, R("IW", 1, 2), 16.0, Op.is_equal)),
        "EQ": lambda: ts(R("EQ", 0, 16), R("BD0", 0, 16), PM, Op.is_equal),
        "PAIR": lambda: tt(R("EQ", 16, 24), R("EQ", 0, 16, 2), R("EQ", 1, 16, 2), Op.add),
        "L2": lambda: (act(cf(1), cf(6), Act.Square), field(LO, 6), field(L2, 1)),
        "R2": lambda: act(R("R2"), R("BD0", 0, 128), Act.Square),
        "HI": lambda: (ts(cf(0), R("IH", p=h64), P256[:4] + (h64,), Op.add), field(HI, 0)),
        "NH": lambda: (ts(cf(2), R("NXC", p=h64), 3.0 * 2 ** 26, Op.add, -3.0 * 2 ** 26, Op.add), field(NH, 2)),
        "NL": lambda: (tt(cf(3), R("NXC", p=h64), cf(2), Op.subtract), field(NL, 3)),
        "S": lambda: [mm(R("p3", 0, 256, 1, h64), R("SU", 15 - 2 * m, 143 - 2 * m, 2), blk("TX", m, 256), m == 0, m == 7) for m in range(8)],
        "SH": lambda: (act(cf(4), R("p3", 0, 256, 1, h64)), field(SH, 4)),
        "SL": lambda: (tt(cf(5), R("p3", 0, 256, 1, h64), cf(4), Op.subtract), field(SL, 5)),
        "bm": lambda: dma("S", T["BMC"][:, :], T["bm"][:, :], [], [R("BMC")]),
        "pl": lambda: dma("S", T["PL"][:, :], T["pl"][:, :], [], [R("PL")]),
        "VL0": lambda: local("S", R("VL", p=h64), row("XV", 0, 0, P)),
        "K0": lambda: cp(R("K0"), R("KI")),
        "LK": lambda: ts(R("LK", 0, 12), R("IK"), P12, Op.add),
        "LH": lambda: ts(R("LK", 12, 24), R("IO", 0, 12), P12, Op.add, -float(PV), Op.add),
        "KJ": lambda: vgather(R("KJ"), R("KI"), R("LK", 0, 12)),
        "VT0": lambda: cp(R("VT", 16, 17), R("RST", 1, 13)),
        "BIG": lambda: fill(R("RST", 0, L, 16), BIG),
        "NI": lambda: act(R("NI"), R("ID"), scale=-1.0),
        "SU": lambda: ts(R("SU"), R("BD"), 15.0, Op.is_equal, KW, Op.mult),
        "SY": lambda: ts(R("SY"), R("BD"), 15.0, Op.is_equal, PAIR(HI), Op.mult),
        "SN": lambda: ts(R("SN"), R("BD"), 15.0, Op.is_equal, PAIR(NH), Op.mult),
        "CF": lambda: ts(CF_, PM, 128.0 - 1.0 / 16, Op.mult, 1.0 / 16, Op.add),
        "SF": lambda: scaled("V", R("SF"), R("SY"), CF_),
        "TH": lambda: (ts(R("THw", 0, 2, 1, e8), R("TH", 0, 2, 1, e8), 4032, Op.bitwise_and), ts(R("THw", 2, 4, 1, e8), R("TH", 0, 2, 1, e8), 63, Op.bitwise_and)),
        "THf": lambda: cp(R("THf", 0, 4, 1, e8), R("THw", 0, 4, 1, e8)),
        "T1": lambda: [ts(R("T1", L * j, L * j + L, 1, e8), R("ON2", p=e8), R("THf", 2 * j, 2 * j + 1, 1, e8), Op.mult, -KW, Op.mult) for j in range(2)],
        "t1": lambda: thresholds(),
        "t2": lambda: [mm(col("p5", 0), R("TSQ", 16 - f, 144 - f, 1, e8), R("THf", j, j + 1, 1, e8), f == C2, f == C3) for f, j in ((C2, 1), (C3, 3))],
        "PP": lambda: [scaled("V", blk("PP", u, 160), R("IDP"), RM1 if u else RM0) for u in range(2)],
        "PN": lambda: ts(R("PP", 320, 640), R("PP", 0, 320), -1.0, Op.mult),
        "OWN": lambda: (ts(R("OWN", 12), R("IO", 12), P12, Op.add), ts(R("OWN", 0, 12), R("I12"), PM, Op.add, float(PV), Op.add)),
        "OWU": lambda: ts(R("OWU"), R("IO"), P12, Op.add),
        "void column": lambda: (fill(R("TXW", P, PV), GATE), fill(R("TFW", P, PV), 1.0)),
        "H0": lambda: act(R("H0"), R("HJ"), Act.Identity, -ODD),
        "BU0": lambda: cp(R("BU"), R("BMC")),
        "NOT1": lambda: ts(NOT1, EQ(ONE), -1.0, Op.mult, 1.0, Op.add),
        "BO": lambda: ts(R("BO"), R("BD", 0, 128), 0.0, Op.is_ge),
        "CG1": lambda: ts(CG1, EQ(ONE), -GATE / 2, Op.mult, PAIR(NH), Op.add),
        "SM": lambda: ts(R("SM"), R("BD"), 15.0, Op.is_equal, CG1, Op.mult),
        "WNR": lambda: scaled("V", R("WNR"), R("BO"), PAIR(NH)),
        "CM": lambda: (ts(C2L, EQ(LO), 2.0, Op.mult), tt(CL2, EQ(L2), EQ(ONE), Op.subtract)),
        "WT": lambda: (ts(blk("WT", 0), R("BD", 0, 128), 0.0, Op.max, C2L, Op.mult), ts(blk("WT", 1), R("R2"), EQ(C1), Op.mult, CL2, Op.add)),
        "WT2": lambda: tt(blk("WT", 2), blk("WT", 1), R("BO"), Op.mult),
        "WM": lambda: tt(R("WM"), blk("WT", 0), blk("WT", 2), Op.subtract),
        "WH": lambda: [scaled("V", blk("WH", u), R("WM"), RM1 if u else RM0) for u in range(2)],
        "CS": lambda: ts(CS, PAIR(SH), -1.0 / KW, Op.mult),
        "CG": lambda: ts(CG, col("p5", 0), -1.0, Op.mult, CS, Op.add),
        "WS": lambda: scaled("V", R("WS"), R("BO"), CG),
        "WC": lambda: (cp(R("WC", 0, 8), R("ID", HI, 128, 16)), ts(R("WC", 8, 16), R("BO", 0, 128, 16), CG, Op.mult)),
        "WN": lambda: scaled("A", R("WN"), R("BO"), -1.0),
        "NBO": lambda: scaled("A", R("NBO"), R("BO"), 2.0),
        "W1": lambda: scaled("V", R("W1"), R("BO"), EQ(ONE)),
        "IM": lambda: scaled("A", R("IM"), R("ID"), -33.0),
        "IVD": lambda: scaled("A", R("IVD"), R("ID"), VOID),
        "IP2": lambda: scaled("A", R("IP2"), R("ID"), 0.5),
        "IM2": lambda: scaled("A", R("IM2"), R("ID"), -0.5),
        "nx - p": lambda: (mm(R("p6", 256, 384), R("IQ"), R("NI"), True, False), mm(R("p6", 256, 384), R("NI"), R("BD0", 0, 128), False, False),
                           [mm(R("p6", 256 + r, 384, 16), R("BB", r, P, 16), R("WNR", 0, 128, 16), False, r == 15) for r in range(16)]),
        "DI": lambda: ts(R("DI"), R("p6", 256, 384), -1.0, Op.mult, 4095.0, Op.add),
        "DN": lambda: ts(R("DN"), R("DI"), 31, Op.bitwise_and),
        "DL": lambda: ts(R("DL"), R("DN"), 65.0, Op.add),
        "DJ": lambda: act(R("DJ"), R("DL"), Act.Identity, 4095.0, 33.0),
        "DH": lambda: tt(R("DH"), R("DJ"), R("DI"), Op.subtract),
    }
    for j in range(4):
        once["ones%d" % j] = lambda j=j: fill(blk("BBW", j, PV // 4), 1.0)
    for j in range(5):
        once["hv%d" % j] = lambda j=j: cp(*hv[j][:2])
        once["ha%d" % j] = lambda j=j: act(*ha[j][:2])
    later = [
        lambda: ts(R("CQ"), R("I12"), PM, Op.add),
        lambda: ts(R("CA"), R("CQ"), TURNS / (L - 1.0), Op.mult, -0.502, Op.add),
        lambda: ts(R("CC"), R("CQ"), float(TURNS), Op.mult),
        lambda: ts(R("CB"), R("CA"), 0.0, Op.max, 1.0 - L, Op.mult),
        lambda: tt(R("CD"), R("CB"), R("CC"), Op.add),
        lambda: cp(R("LU"), R("CD")),
    ]

    banks = [("p%d" % (1 + j), AB[j], AB[j + 1]) for j in range(len(AB) - 1)]

    def thresholds():
        for j in range(2):
            mm(R("p0", 0, L), R("TSR", p=e8), R("T1", L * j, L * j + L, 1, e8), False, False)

    def preload(t):
        mm(R("p0", 0, L), R("ID"), R("KC"), True, False)
        if t:
            mm(R("p0", 0, L), R("NI"), R("LV"), False, False)
            thresholds()

    def less_h(t):
        for bank, a, b in banks:
            for k in range(16):
                mm(R(bank, k, 16 * (b - a), 16), R("NI"), R("H%d" % t if t else "HC", a, b), k == 0, False)

    def sums(src, c0, c1, stop=False):
        rs = range(c0 // CH, (c1 - 1) // CH + 1)
        for r in rs:
            a, b = max(c0, CH * r), min(c1, CH * r + CH)
            mm(R("p0", 16 * (a - CH * r), 16 * (b - CH * r)), R("SU", 15 - r, 143 - r), R(src, 16 * a, 16 * b), False, stop and r == rs[-1])

    def steps_to_keys():
        for u in range(2):
            for s in range(2):
                for w in range(2):
                    c = 160 * (2 * w + u) + 16 - 16 * (s - u)
                    mm(R("p4", 256 + 96 * u, 352 + 96 * u), R("PP", c, c + 128), R("VT", w, w + 16, -1 - s), u + s + w == 0, u + s + w == 3)

    def lanes(bank, c0, c1, src, ws, start=False, stop=False, parts=(0, 1, 2)):
        for j in parts:
            n = len(range(*ws[j][1:4]))
            o, a = (R(bank, c1, c1 + n, 1, slice(64 * j - 64, 64 * j)), R(src, 128, L)) if j else (R(bank, c0, c0 + n), R(src, 0, 128))
            mm(o, a, ws[j], start and (stop or j == 0), stop and (start or j == 0))

    def one(W, c=0):
        return R(W, c, 128, 16), R(W, c, 128, 32), R(W, 16 + c, 128, 32)

    low = (R("WM"), blk("WH", 0), blk("WH", 1))
    both = (R("WC"), R("WC", 0, 16, 2), R("WC", 1, 16, 2))

    def one_hot(w, js):
        for j in js:
            if w:
                ts(blk("NN", 12 + j), R("IQ"), col("NC", j + j // 8 * 8), Op.is_equal, col("NC", j + 8 + j // 8 * 4), Op.is_gt)
            else:
                ts(blk("NN", j), R("IQ"), col("YC", j), Op.is_equal)

    done = []

    def products(w, js):
        for j in js:
            c, m = (16 * j, 16) if j < 8 else (32 * j - 256, 32)
            done.append(j)
            a = 256 * w + 128 * (j // 8) + c
            mm(R("p0", c, c + m), blk("NN", 12 * w + j), R("MM", a, a + m), len(done) % 24 == 1, len(done) % 24 == 0)

    def own_h(t):
        win, off = (R("TXW", 0, PV + L * (t + 1)), blk("OWU", t, 12)) if t else (R("HC"), R("LK", 12, 24))
        act(R("HJ"), win, Act.Identity, ODD, off=off)

    once["keys0"], once["less h0"] = lambda: preload(0), lambda: less_h(0)
    for what in START:
        once[what]()
    last_sum = [s for s in STEP1 if s[0] == "sum"][-1]
    for t in range(NV):
        last = t == NV - 1
        K, WIN, HS, h1 = "K%d" % t, PV + L * (t + 1), R("HS%d" % t), "H%d" % min(t + 1, NV - 1)
        TFW = "TFW" if t else "BBW"
        hx = doubling(h1, 0, GK)
        part = lambda a: ("p5", "p4", "p3")[PARTS.index(a)]
        steps = {
            "tile": lambda: t and (gcopy(R("KF"), R(K), L), t == 1 and iota(R("IOT"), [[1, P]], 0, 0)),
            "reorder": lambda: t and agather(R("KJ"), R("KF"), R("LK", 0, 12)),
            "turn": lambda: turn(R("VT", 0, 16), R("KJ")),
            "steps": steps_to_keys,
            "own h": lambda: own_h(t),
            "misses": lambda: agather(R("TFM%d" % t), R("TF" if t else "BB"), R("BU"), NOT1),
            "J": lambda: lists("p7", 0, "SY", "TF", 0, 128, True, False) if t else
            (mm(R("p7", 0, 128), R("ID"), R("IQ"), True, False), mm(R("p7", 0, 128), R("BD0", 0, 128), R("ID"), False, False)),
            "own": lambda: tt(R("WO"), R("MS", 15, L, 16), blk("OWN", t, 12), Op.min),
            "LI": lambda: tt(R("LI"), R("RR", 15, L, 16), R("WO"), Op.max),
            "L1": lambda: cp(R("L1"), R("LI")),
            "late": lambda: t and later and later.pop(0)(),
            "Q2": lambda: ttgather(R("Q2"), R("TXW", 0, WIN), R("L1"), R("HJ"), Op.add),
            "y": lambda: agather(R("FY"), R(TFW, 0, WIN), R("L1")),
            "Q1": lambda: act(R("Q1"), R("Q2"), Act.Identity, -1280.0, 0.5),
            "QO": lambda: act(R("QO"), R("Q2"), Act.Identity, ODD - 1280.0, 0.5),
            "next": lambda: lists("p3", 16, "SM", "FY", 0, 12),
            "M1": lambda: ts(R("M1"), R("p3", 16, 28), GATE / 2, Op.add, float(P), Op.min),
            "y high": lambda: lanes("p2", 256, 0, "FY", one("ID", HI), True, True, (0,)),
            "y high 2": lambda: lanes("p2", 0, 264, "FY", one("ID", HI), True, True, (1, 2)),
            "y cols": lambda: cp(R("YC"), R("p2", 256, 268)),
            "n cols": lambda: ts(R("NC"), R("p5", 0, 24), 0.0, Op.max),
            "y low": lambda: lanes("p1", 0, 128, "FY", low, True, True),
            "gate": lambda: mm(R("p5", 0, 24), R("FY", 0, 128), R("SU", 0, 96, 4), True, False),
            "h sum": lambda: lanes("p5", 8, 20, "Q1", one("WN")),
            "flag y": lambda: mm(R("p6", 0, L), R("WN"), R("Q1"), True, False),
            "max": lambda: ttgather(R("MX"), R("TXW", 0, PV), R("M1"), R("Q1"), Op.max),
            "n": lambda: agather(R("FN"), R(TFW, 0, PV), R("M1")),
            "blend": lambda: ttgather(R("HB"), R("TXW", 0, PV), R("M1"), R("QO"), Op.add),
            "n max": lambda: lanes("p5", 8, 20, "MX", one("NBO")),
            "n high": lambda: lanes("p5", 0, 16, "FN", both, False, True, (1, 2, 0)),
            "n low": lambda: lanes("p2", 0, 128, "FN", low, True, True),
            "flag n": lambda: (mm(R("p6", 0, L), R("NBO"), R("MX"), False, False), mm(R("p6", 0, L), R("WS"), R("FN"), False, True)),
            "less y": lambda: (mm(R("p4", 256, 256 + L), R("NI"), R("FY"), True, False), mm(R("p4", 64, 64 + L), R("IM2"), R("Q2"), False, False)),
            "plus n": lambda: (mm(R("p4", 256, 256 + L), R("ID"), R("FN"), False, False), mm(R("p4", 64, 64 + L), R("IP2"), R("HB"), False, True)),
            "BR": lambda: act(R("BR"), R("p6", 0, L), Act.Sigmoid, 500.0, -1000.0),
            "half": lambda: tt(R("p4", 64, 64 + L), R("p4", 64, 64 + L), R("BR"), Op.mult),
            "h": lambda: (tt(HS, R("p4", 64, 64 + L), R("Q1"), Op.add), last or send(t, "H", "ha")),
            "fields": lambda: tt(R("GF"), R("p4", 256, 256 + L), R("BR"), Op.mult),
            "marks": lambda: (tt(R("UH"), R("p0", 0, 128), R("DH"), Op.min), tt(R("UL"), R("p0", 0, 128), R("DL"), Op.min)),
            "J2": lambda: (mm(R("p7", 0, 128), R("UH"), R("ID"), False, False), mm(R("p7", 0, 128), R("UL"), R("IM"), False, True)),
            "list": lambda: cp(R("ZU"), R("p7", 0, 128)),
        }
        onward = {
            "flags": lambda: mm(R("p1", 256, 256 + L), R("W1"), R("FY")),
            "count": lambda: act(R("BS"), R("p1", 256, 256 + L), scale=KW, total=col("AK", 0)),
            "32s": lambda: act(R("SG"), R("S12"), Act.Sign, col("AK", 0), KW / 2, total=col("AK", 1)),
            "level": lambda: act(R("LV"), R("CL"), Act.Identity, col("AK", 0), col("AK", 1)),
            "void 0": lambda: mm(R("p1", 0, 256, 1, h64), R("ID", 0, 64, 1, h64), R("VL", p=h64), True, False),
            "void": lambda: [mm(R("p1", 128 * j, 128 * j + 128, 1, h64), R("UL", j, 128, 2), R("IVD"), False, j == 1) for j in range(2)],
            "VL": lambda: (act(R("VL", p=h64), R("p1", 0, 256, 1, h64)), local("S", row("XV", 0, 0, P), R("VL", p=h64))),
            "y list": lambda: lists("p3", 28, "SY", "FY", 0, 12, True, False),
            "y list 2": lambda: lists("p3", 28, "SY", "GF", 0, 12, False, True),
            "b list": lambda: lists("p2", 0, "SN", "FY", 0, 12, True, False),
            "b list 2": lambda: lists("p2", 0, "SN", "GF", 0, 12, False, True),
            "YU": lambda: cp(R("YU"), R("p3", 28, 40)),
            "K": lambda: (vgather(R("KS%d" % t), R("PL"), R("YU")), send(t, "K", "ka")),
            "BU": lambda: cp(R("BU"), R("p2", 0, 12)),
            "G": lambda: [gcopy(*c) for c in doubling(h1, GK, NX)],
            "keys": lambda: preload(t + 1),
            "less h": lambda: less_h(t + 1),
        }
        s1, s2 = LAST
        final = {
            "b rows": lambda: (mm(R("p6", 0, L), R("WNR"), R("FY"), True, False), mm(R("p6", 0, L), R("WNR"), R("GF"), False, True)),
            "RB": lambda: act(R("RB"), R("p6", 0, L)),
            "yb": lambda: (agather(R("NR"), R("RB"), R("LU")), dma("S", T["yb"][:, :], ap(row("NR", 0, 0, L)), [R("NR")], [])),
            "yh": lambda: (vgather(R("MX"), HS, R("LU")), dma("S", T["yh"][:, :], ap(R("MX")), [R("MX")], [])),
            "J2 a": lambda: agather(R("BF1", 16 * s1, P), R("IOT"), R("ZU", s1, 128)),
            "J2 v": lambda: vgather(R("BF1", 0, 16 * s1), R("IOT"), R("ZU", 0, s1)),
            "yj a": lambda: (agather(R("ROW", 16 * s2, P), R("BF1"), R("ZU", s2, 128)),
                             dma("C", T["yj"][:, 16 * s2:P], ap(row("ROW", 0, 16 * s2, P)), [R("ROW", 16 * s2, P)], [])),
            "yj v": lambda: (vgather(R("ROW", 0, 16 * s2), R("BF1"), R("ZU", 0, s2)),
                             dma("S", T["yj"][:, 0:16 * s2], ap(row("ROW", 0, 0, 16 * s2)), [R("ROW", 0, 16 * s2)], [])),
        }
        for w in ("fields", "half", "h"):
            onward[w] = final[w + " last"] = steps.pop(w)
        for j in range(5):
            onward["h%d" % j] = lambda j=j: cp(*hx[j][:2])
        if t == 0:
            for w in ("h0", "h1", "h2", "h3", "h4", "G", "less h"):
                once[w + " first"] = onward.pop(w)
        for what in STEP1 + MATCH + TABLES:
            if isinstance(what, str):
                for kind, now in ((steps, True), (onward, not last), (final, last), (once, t == 0)):
                    if what in kind and now:
                        kind[what]()
                continue
            w, a, b = what
            d, x = R("DX", 16 * a, 16 * b), R("AX", 16 * a, 16 * b)
            if w == "less h":
                ttgather(d, R("TX"), R(K, a, b), R("HX", 16 * a, 16 * b), Op.subtract)
            elif w == "plain":
                agather(d, R("TX"), R(K, a, b))
            elif w == "plus x":
                mm(R(banks[AB.index(a)][0], 0, 16 * (b - a)), R("ID"), d, False, True)
            elif w == "relu":
                ts(x, d, -2.0, Op.mult, 0.0, Op.max)
            elif w == "abs":
                act(x, d if a < NX else R(banks[AB.index(a)][0], 0, 16 * (b - a)), Act.Abs)
            elif w == "sum d":
                sums("DX", a, b)
            elif w == "sum":
                sums("AX", a, b, what == last_sum)
            elif w == "least":
                scan(R("MS", a, b), R("RST", a, b), R("p0", a, b), 0.0, Op.add, Op.min)
            elif w == "stays":
                tt(R("ZN", a, b), R("p0", a, b), R("MS", a, b), Op.not_equal)
            elif w == "column":
                scan(R("RR", a, b), R("ZN", a, b), R("p4", 256 + a, 256 + b), 0.0, Op.mult, Op.add)
            elif w in ("hot y", "hot n"):
                one_hot(w == "hot n", range(a, b))
            elif w in ("low y", "low n"):
                j = w == "low n"
                act(R("MM", 256 * j + a, 256 * j + b), R("p%d" % (1 + j), a, b), Act.Relu, 0.0, GATE)
            elif w in ("prod y", "prod n"):
                products(w == "prod n", range(a, b))
            elif last:
                continue
            elif w == "SF":
                lists(part(a), 0, "SF", "TF", a, b)
            elif w == "JU":
                cp(R("JU", a, b), R(part(a), 0, b - a))
            else:
                src, off = {"B1": ("BB", "ZU"), "TF": ("B1", "ZU"), "TX": ("XV", "JU")}[w[1:]]
                (vgather if w[0] == "v" else agather)(R(w[1:], 16 * a, 16 * b), R(src), R(off, a, b))
    finish()
    g.wait_ge(T.sem["loc"], 2 * (NV - 1) * len(topo.engines(core, nxt)))


RC, NX = 72, 128
AB = (128, 160, 192)
LAST = (64, 64)
PARTS = (0, 32, 80)
GK = 72
START = ("ones3", "ones1", "RST", "NI", "IW", "ones0", "RM", "PM", "EQ", "CK", "void column", "CM", "TH", "ha0", "PAIR", "hv1", "less h0", "hv0", "LK",
         "ones2", "VT0", "keys0", "hv2", "MK", "BIG", "ha1", "SU", "hv3", "PP", "KJ", "PN", "NH", "K0", "ha2", "HI", "ha3")
STEP1 = ("L2", "ha4", ("plain", 128, 160), "hv4", "S", ("plus x", 128, 160), "OWN", "NL", "CG1", "THf", ("less h", 36, 60), ("less h", 60, 84), "T1",
         ("plain", 160, 192), ("sum d", 36, 84), ("plus x", 160, 192), ("less h", 0, 36), "t1", ("relu", 36, 60), ("abs", 128, 160), "SH",
         ("sum", 128, 160), ("sum", 36, 60), ("less h", 84, 108), ("relu", 60, 84), "tile", ("abs", 160, 192), ("sum", 160, 192), "SL",
         ("less h", 108, 128), ("sum d", 84, 108), ("relu", 84, 108), "BO", ("abs", 0, 36), ("relu", 108, 128), "reorder", "LH", "late", "turn", "WG",
         "BU0", "SY", ("sum", 60, 84), "IM2", "own h", "NOT1", ("sum", 0, 36), ("sum d", 108, 128), ("sum", 84, 108), ("sum", 108, 128), "WT", "steps")
MATCH = (("least", 0, 64), ("least", 64, 128), "IVD", ("least", 128, 192), "NBO", ("stays", 0, 64), "H0", ("stays", 64, 128), ("stays", 128, 192), "own",
         ("column", 0, 64), ("column", 64, 128), ("column", 128, 192), "t2", "WT2", "LI", "CF", "TFM0", "nx - p", "CS", "mask", "L1", "WM", "late", "CG",
         "Q2", "WH", "y", "J", "next", "y high", "WN", "y high 2", "DI", "WC", "pick", ("hot y", 0, 2), "Q1", ("hot y", 2, 4), "M1", ("hot y", 4, 6),
         "y low", ("hot y", 6, 8), "QO", ("low y", 0, 256), "gate", "DN", "max", "h sum", "flag y", ("hot y", 8, 10), "less y", "W1", ("hot y", 10, 12),
         "flags", "WS", ("prod y", 0, 8), "n", "n max", "n high", "IP2", "n low", "DL", "DJ", "blend", ("hot n", 0, 12), "flag n", "plus n",
         ("prod y", 8, 12), ("low n", 0, 256), "DH", "BR", "IM", "count", ("prod n", 0, 12), "half", "late", "y list", "32s", "SF", "marks", "level",
         "J2", "void", "h", "fields", "VL", "SN", "y list 2", "list", "b list", ("aB1", 58, 128), ("vB1", 0, 20), "keys")
TABLES = ("YU", ("vB1", 20, 58), "b list 2", "K", ("aTF", 30, 64), ("vTF", 0, 30), ("vTF", 64, 96), ("SF", 0, 64), "BU", ("aTF", 96, 128), "h1", "G", "h0",
          ("JU", 0, 64), "h2", ("vTX", 0, 30), ("SF", 64, 128), ("JU", 64, 128), "h3", ("vTX", 64, 94), "TFM", ("aTX", 30, 64), "h4", ("aTX", 94, 128),
          "OWU", "less h")
START = ("IW", "PM", "EQ", "ones0", "CF", "PAIR", "ones2", "LK", "CM", "RM", "RST", "ones1", "ones3", "void column", "CG1", "BO", "VT0", "PP", "hv1", "ha0", "SN", "HI", "ha1", "hv0", "NI", "BIG", "hv2", "keys0", "less h0", "PN", "CK", "ha2", "SU", "K0", "L2", "hv3", "MK", "OWN", "S", "KJ", "LH", "hv4", "NOT1", "ha3", "TH", "CS")
STEP1 = ("WN", "THf", "T1", "NH", "tile", "ha4", ("plain", 128, 160), ("plain", 160, 192), ("less h", 36, 60), "NL", ("less h", 60, 84), ("relu", 36, 60), "SH", ("plus x", 128, 160), "SL", ("less h", 0, 36), ("less h", 84, 108), ("relu", 60, 84), "W1", "WG", ("abs", 128, 160), ("plus x", 160, 192), "t2", ("abs", 160, 192), ("abs", 0, 36), ("less h", 108, 128), ("sum d", 36, 84), "CG", ("relu", 84, 108), ("sum", 128, 160), ("sum", 36, 60), "reorder", ("relu", 108, 128), "t1", "IM2", "WC", "late", "NBO", "own h", "turn", ("sum", 160, 192), "IVD", ("sum d", 84, 108), ("sum", 60, 84), ("sum", 0, 36), "WT", ("sum d", 108, 128), "BU0", ("sum", 84, 108), ("sum", 108, 128), "IM", "steps", "H0")
MATCH = (("least", 0, 64), ("least", 64, 128), ("least", 128, 192), "IP2", ("stays", 0, 64), "TFM0", ("stays", 64, 128), "J", ("stays", 128, 192), "own", ("column", 0, 64), ("column", 64, 128), ("column", 128, 192), "WT2", "LI", "nx - p", "SY", "mask", "L1", "y", "WM", "late", "y high", "WS", "y high 2", "next", "Q2", "QO", "DI", "WH", "Q1", "gate", "DN", "y low", "y cols", "pick", "h sum", ("hot y", 0, 2), "DL", ("low y", 0, 256), "M1", ("hot y", 4, 6), ("hot y", 6, 8), "less y", "n", "max", "flags", "n max", ("hot y", 2, 4), "count", "n high", "n low", "DJ", "flag y", ("low n", 0, 256), "blend", "flag n", ("hot y", 8, 10), "n cols", ("hot y", 10, 12), "plus n", ("prod y", 0, 8), ("hot n", 0, 12), ("prod y", 8, 12), ("prod n", 0, 12), "DH", "BR", "half", "marks", "h", "y list", "J2", "fields", "list", "32s", "void", "y list 2", "level", "b list", ("vB1", 0, 20), "SF", "YU", "VL", ("aB1", 58, 128), ("vB1", 20, 58), ("aTF", 30, 64), "K", ("aTF", 96, 128), "late", "b list 2")
TABLES = ("BU", ("vTF", 0, 30), ("vTF", 64, 96), ("SF", 0, 64), "G", ("SF", 64, 128), "h0", "h1", ("JU", 0, 64), "TFM", "h2", "OWU", ("aTX", 30, 64), ("vTX", 0, 30), ("JU", 64, 128), "keys", "h3", ("aTX", 94, 128), ("vTX", 64, 94), "h4", "less h")
START = ("IW", "ones0", "RST", "NI", "PM", "ones2", "ones3", "EQ", "RM", "ha0", "ha1", "CM", "ones1", "NOT1", "PP", "VT0", "R2", "PAIR", "BO", "hv1", "hv0", "ha2", "WN", "PN", "LK", "hv2")
STEP1 = ("BIG", "less h0", "CG1", "tile", "SU", "KJ", "hv3", "bm", "S", "K0", "HI", "WNR", "CS", "W1", "SM", "hv4", "ha3", "OWU", "ha4", "keys0", "WT", "L2", "SN", ("plain", 128, 160), "SY", ("plus x", 128, 160), "LH", ("less h", 0, 36), "NH", "TH", ("plain", 160, 192), ("less h", 36, 60), "THf", ("less h", 60, 84), "SH", ("abs", 128, 160), ("relu", 36, 60), ("plus x", 160, 192), ("abs", 160, 192), ("sum d", 36, 84), "NL", "t2", "SL", ("sum", 128, 160), ("abs", 0, 36), "reorder", "T1", ("sum", 36, 60), "IM2", ("less h", 84, 108), ("relu", 60, 84), ("less h", 108, 128), ("relu", 84, 108), ("relu", 108, 128), "OWN", ("sum", 160, 192), "t1", ("sum d", 84, 108), "late", "own h", ("sum", 60, 84), ("sum", 0, 36), "BU0", "turn", "WT2", ("sum d", 108, 128), ("sum", 84, 108), "H0", ("sum", 108, 128), "pl", "CG")
MATCH = ("steps", ("least", 0, 64), ("least", 64, 128), "J", ("least", 128, 192), ("stays", 0, 64), ("stays", 64, 128), ("stays", 128, 192), "own", ("column", 0, 64), ("column", 64, 128), ("column", 128, 192), "TFM0", "void column", "LI", "WC", "L1", "y", "nx - p", "y high", "NBO", "WM", "y high 2", "Q2", "Q1", "next", "DI", "y cols", "DN", "WH", "IP2", "flag y", "WS", "y low", "gate", ("hot y", 2, 4), "less y", "QO", "h sum", "M1", ("hot y", 8, 10), "max", ("hot y", 0, 2), "n max", "n", "blend", "n high", "VL0", ("hot y", 10, 12), "n low", ("low y", 0, 256), "flags", "IM", "flag n", "plus n", ("low n", 0, 256), "DL", "n cols", ("hot y", 4, 6), ("hot y", 6, 8), "BR", "DJ", ("hot n", 0, 12), ("prod y", 0, 8), ("prod y", 8, 12), "IVD", "half", "fields last", "count", ("prod n", 0, 12), "y list", "DH", "h", "b rows", "RB", "32s", "void 0", "marks", "fields", "J2", "late", "void", "y list 2", "b list", "level", "half last", "CF", "b list 2", "list", "VL", ("vB1", 0, 20), "h last", "YU", "SF", "late", "K", "keys", ("vB1", 20, 56), ("aB1", 56, 128))
TABLES = ("yb", "BU", ("vTF", 0, 32), ("vTF", 64, 96), "h1", "J2 v", "yh", "h0", "J2 a", "G", ("aTF", 32, 64), ("SF", 0, 64), ("aTF", 96, 128), ("JU", 0, 64), "h1 first", "h2", "TFM", ("SF", 64, 128), "less h", "less h first", "h0 first", "yj v", ("vTX", 0, 30), "h2 first", ("JU", 64, 128), "yj a", "h3 first", "h3", ("aTX", 30, 64), ("vTX", 64, 94), "G first", "h4 first", ("aTX", 94, 128), "h4")
START = ("IW", "ones0", "RST", "NI", "keys0", "PM", "ones2", "ones3", "EQ", "RM", "ha0", "ha1", "CM", "bm", "ones1", "NOT1", "PP", "VT0", "R2", "PAIR", "BO", "HI", "hv1", "SN", "less h0", "L2", "WT", "SU", "hv0", "ha2", "WNR", "WN", "CG1", "PN", "LK", "BIG", "hv2", "ha3")
STEP1 = ("hv3", "SY", "OWU", "hv4", "LH", "KJ", "ha4", "K0", "S", "tile", ("plain", 128, 160), ("plain", 160, 192), "SM", ("plus x", 128, 160), "W1", "CS", ("less h", 36, 72), "NH", ("plus x", 160, 192), ("less h", 0, 36), ("less h", 72, 96), ("sum d", 36, 72), ("abs", 128, 160), "SH", "NL", "TH", ("relu", 36, 72), ("sum", 128, 160), ("abs", 160, 192), ("sum d", 72, 96), "SL", "pl", ("sum", 36, 72), ("abs", 0, 36), "THf", ("sum", 160, 192), ("less h", 96, 116), "t2", ("relu", 72, 96), ("sum d", 96, 116), ("sum", 72, 96), ("less h", 116, 128), "T1", ("relu", 96, 116), "reorder", ("sum", 0, 36), ("relu", 116, 128), ("sum d", 116, 128), "t1", "WT2", "late", ("sum", 96, 116), "turn", "own h", "OWN", ("sum", 116, 128))
MATCH = ("BU0", ("least", 0, 64), "steps", ("least", 64, 128), ("least", 128, 192), "J", "CG", ("stays", 0, 64), ("stays", 64, 128), "H0", ("stays", 128, 192), "own", ("column", 0, 64), ("column", 64, 128), "IM2", "misses", ("column", 128, 192), "void column", "LI", "WC", "L1", "nx - p", "NBO", "y", "y high", "WM", "y high 2", "DI", "Q2", "y cols", "DN", "WH", "IP2", "next", "WS", ("hot y", 2, 4), "M1", "Q1", "gate", "flag y", ("hot y", 8, 10), "y low", "h sum", "VL0", "max", ("hot y", 0, 2), "QO", "less y", "n", "n max", "n high", "n low", "blend", "flag n", ("low y", 0, 256), ("hot y", 10, 12), "IM", "flags", "n cols", ("hot y", 4, 6), ("low n", 0, 256), "plus n", "BR", ("hot y", 6, 8), ("prod y", 0, 8), "DL", ("hot n", 0, 12), "DJ", "count", "fields last", ("prod y", 8, 12), ("prod n", 0, 12), "half", "32s", "y list", "IVD", "DH", "b rows", "h", "RB", "void 0", "marks", "half last", "yb", "J2", "fields", "late", "CF", "SF", "list", "void", "h last", "level", "y list 2", "VL", "late", "b list", "YU", ("vB1", 0, 20))
TABLES = ("b list 2", "K", ("vB1", 20, 52), ("aB1", 52, 128), ("aTF", 32, 64), "BU", ("vTF", 0, 32), "J2 v", "G", ("SF", 0, 64), ("vTF", 64, 94), "h1", "h0", ("aTF", 94, 128), ("SF", 64, 128), "h1 first", ("JU", 0, 64), "less h first", ("aTX", 26, 64), "less h", "h0 first", "h2", "h2 first", ("vTX", 0, 26), ("JU", 64, 128), "J2 a", "h3 first", "G first", "yh", "h3", "keys", ("aTX", 92, 128), ("vTX", 64, 92), "yj v", "h4", "h4 first", "yj a")
STEP1 = ("hv3", "SY", "OWU", "hv4", "LH", "KJ", "ha4", "K0", "tile", "S", "WG", "CK", "W1", "MK", "CS", ("plain", 128, 160), ("less h", 36, 72), ("plus x", 128, 160), ("less h", 72, 96), ("plain", 160, 192), "NH", ("relu", 36, 72), "SH", ("sum d", 36, 72), ("plus x", 160, 192), "NL", "TH", ("sum d", 72, 96), "SL", ("less h", 0, 36), "pl", ("sum", 36, 72), ("abs", 128, 160), ("abs", 160, 192), ("sum", 128, 160), "THf", ("less h", 96, 116), ("relu", 72, 96), ("less h", 116, 128), ("abs", 0, 36), "t2", "T1", ("sum", 160, 192), ("sum d", 96, 116), ("sum", 72, 96), "reorder", ("relu", 96, 116), ("relu", 116, 128), ("sum", 0, 36), "t1", ("sum d", 116, 128), "turn", "WT2", ("sum", 96, 116), "OWN", ("sum", 116, 128), "own h")
MATCH = ("steps", "BU0", ("least", 0, 64), ("least", 64, 128), ("least", 128, 192), "CG", "H0", ("stays", 0, 64), ("stays", 64, 128), "misses", ("stays", 128, 192), "own", ("column", 0, 64), ("column", 64, 128), ("column", 128, 192), "IM2", "void column", "LI", "WC", "late", "nx - p", "L1", "NBO", "J", "y", "WM", "Q2", "mask", "y high", "DI", "y high 2", "DN", "WH", "next", "y cols", "Q1", "IP2", "pick", ("hot y", 2, 4), "gate", "M1", ("hot y", 8, 10), "max", "WS", "VL0", "QO", "flag y", "n", "IM", "y low", "h sum", ("low y", 0, 256), "less y", "n max", ("hot y", 6, 8), "n high", ("hot y", 10, 12), "n low", "flag n", ("low n", 0, 256), "BR", "blend", "n cols", ("hot y", 0, 2), "flags", "DL", "DJ", ("hot y", 4, 6), ("hot n", 0, 12), "IVD", "plus n", "fields last", ("prod y", 0, 8), "half", ("prod y", 8, 12), ("prod n", 0, 12), "half last", "count", "h", "DH", "void 0", "b rows", "marks", "h last", "32s", "late", "CF", "J2", "level", "fields", "list", "void", "yh", "VL", "y list", "SF", "y list 2")
TABLES = ("b list", ("vB1", 20, 52), ("vB1", 0, 20), "YU", "late", ("aB1", 52, 128), "K", ("aTF", 32, 64), "RB", ("vTF", 0, 32), ("aTF", 94, 128), ("vTF", 64, 94), "J2 v", "h0", "b list 2", "h1", "J2 a", "BU", ("SF", 0, 64), "yb", ("SF", 64, 128), "h1 first", "less h first", "G", "h0 first", ("JU", 0, 64), "h2", "h2 first", ("vTX", 0, 26), "yj v", "keys", ("JU", 64, 128), "h3 first", "h3", ("vTX", 64, 92), "G first", "less h", ("aTX", 26, 64), "yj a", ("aTX", 92, 128), "h4", "h4 first")
START = ("ones1", "RST", "IW", "PM", "ones3", "ha0", "NI", "ones2", "LK", "EQ", "RM", "NOT1", "less h0", "PAIR", "hv1", "PP", "ha1", "SU", "S", "hv0", "BO", "VT0", "CG1", "hv2", "ha2", "SY", "CM")
STEP1 = ("ones0", "K0", "BIG", "keys0", "hv3", "KJ", "W1", "R2", "ha3", "bm", "ha4", "OWU", "PN", "SM", "LH", "tile", ("plain", 128, 160), ("plain", 160, 192), ("plus x", 128, 160), "HI", "hv4", "L2", "CS", "WN", "SN", ("plus x", 160, 192), "WNR", "WT", ("less h", 0, 24), "TH", ("less h", 24, 60), "NH", ("abs", 128, 160), ("less h", 60, 88), "SH", ("abs", 0, 24), ("relu", 24, 60), ("sum d", 24, 60), ("sum", 128, 160), ("abs", 160, 192), "NL", ("sum", 0, 24), ("sum", 24, 60), "SL", "pl", ("abs", 60, 88), ("less h", 88, 114), "THf", ("less h", 114, 128), "T1", ("sum", 160, 192), "reorder", ("sum d", 88, 114), "own h", ("sum", 60, 88), ("relu", 88, 114), ("sum d", 114, 128), "t1", "late", ("relu", 114, 128), ("sum", 88, 114), "OWN", "WT2", "NBO", "turn", ("sum", 114, 128), "void column", "steps", "IP2", "t2")
MATCH = ("BU0", ("least", 0, 64), "H0", ("least", 64, 128), ("least", 128, 192), "nx - p", ("stays", 0, 64), ("stays", 64, 128), ("stays", 128, 192), "own", "J", "IM", ("column", 0, 64), ("column", 64, 128), "misses", "IM2", ("column", 128, 192), "CG", "LI", "L1", "WM", "Q2", "WH", "DI", "y", "y high", "DN", "y high 2", "y cols", "WS", "Q1", "WC", "next", ("hot y", 2, 4), "M1", "less y", ("hot y", 8, 10), ("hot y", 0, 2), "max", "gate", ("hot y", 10, 12), "flag y", ("hot y", 4, 6), "QO", "IVD", "h sum", "y low", "n max", "n", "n high", "n low", "DL", ("low y", 0, 256), "flag n", "blend", "plus n", "DJ", "n cols", ("low n", 0, 256), "VL0", "BR", ("hot y", 6, 8), "flags", ("hot n", 0, 12), "fields last", "half", ("prod y", 0, 8), ("prod y", 8, 12), ("prod n", 0, 12), "count", "DH", "h", "y list", "b rows", "marks", "late", "RB", "yb", "fields", "32s", "CF", "void 0", "J2", "level", "half last", "void", "y list 2", "list", "late", ("vB1", 0, 20), "b list", "YU", "SF", ("vB1", 20, 52), "VL", "K", "h last")
TABLES = ("b list 2", "keys", ("aB1", 52, 128), ("aTF", 16, 32), "BU", ("vTF", 0, 16), ("aTF", 54, 80), "J2 v", ("vTF", 32, 54), "yh", "G first", "J2 a", "yj v", ("vTF", 80, 102), ("SF", 0, 32), "G", "h1", "h0", "yj a", ("aTF", 102, 128), ("JU", 0, 32), ("aTX", 12, 32), ("SF", 32, 80), "h2", ("JU", 32, 80), ("SF", 80, 128), "h0 first", "h3", "h1 first", ("vTX", 0, 12), "h4", "less h first", ("aTX", 52, 80), "h2 first", "less h", ("JU", 80, 128), ("vTX", 32, 52), "h3 first", ("vTX", 80, 100), "h4 first", ("aTX", 100, 128))
